import numpy as np, ml_dtypes
CORES = [35,38,43,46]
N = 4
BF = ml_dtypes.bfloat16
P, V, C, PH, S, Z, CAP, RO = 3072, 1024, 512, 4, 12, 8, 64, 5
I = V // PH
def tail(rng, b, top):
    return np.where(np.arange(16)[:, None] >= rng.integers(0, 17, (N, 8, 1, V)), rng.integers(0, top, b.shape), b)
def parts(rng):
    e = rng.choice(np.array([10.0, 14.0, 18.0, 24.0]), (N, 8, 1, 1))
    x = np.minimum((256 * rng.random((N, 8, 16, P)) ** e).astype(np.int64), 255)
    m = rng.integers(0, 256, (N, 8, 16, V)); b = rng.integers(0, P, (N, 8, 16, V))
    return x, m, b, tail(rng, b, P), rng.integers(0, V, (N, 8, 16, C))
def tops(x, l):
    y = np.take_along_axis(x, l[:, :, 0][:, :, None, :], 3)
    for k in range(1, 16): y = np.maximum(y, np.take_along_axis(x, l[:, :, k][:, :, None, :], 3))
    return y
def late(rng, shape):
    return PH * rng.integers(0, I, shape) + 1 + rng.integers(0, PH - 1, shape)
def pack(x, m, b, d, u):
    r = {"mor": x.reshape(N, 128, P).astype(np.float32).astype(BF), "mea": m.reshape(N, 128, V).astype(np.float32).astype(BF)}
    r["bas"] = b.reshape(N, 128, V).astype(np.int32); r["der"] = d.reshape(N, 128, V).astype(np.int32); r["use"] = u.reshape(N, 128, C).astype(np.int32)
    return r
def setup_inputs(rng):
    x, m, b, d, u = parts(rng); h = rng.integers(0, 8, N)
    for q in range(N):
        g = int(h[q]); x[q, g, :, P - 1] = 255; m[q, g] = rng.integers(0, 151, (16, V)); u[q, g] = late(rng, (16, C))
        d[q, g, rng.integers(0, 16, I), PH * np.arange(I)] = P - 1
    near = rng.random((N, 8, 1, V)) < rng.choice(np.array([0.0, 0.2, 0.5, 0.8]), (N, 8, 1, 1)); near[np.arange(N), h] = False
    m = np.where(near, np.clip(tops(x, d) + rng.integers(-24, 25, m.shape), 0, 255), m)
    for q in range(N):
        for g in range(8):
            v = PH * rng.permutation(I)[:3]; u[q, g][:, b[q, g, 15, v] & (C - 1)] = v
    return pack(x, m, b, d, u)
def setup_inputs_corners(rng):
    x, m, b, d, u = parts(rng); x = np.minimum(x, 100); x[..., P - 1] = 255; m = rng.integers(0, 101, m.shape)
    b = rng.integers(0, P - 1, b.shape); d = tail(rng, b, P - 1); u = late(rng, u.shape)
    u = np.where(rng.random((N, 8, 1, C)) < 0.1, np.where(rng.random((N, 8, 1, C)) < 0.5, V - 1, 1), u); top = tops(x, d)
    for q in range(N):
        for g in range(8):
            if q == 3 and g % 2 == 1:
                n = (0, 1, CAP // 2, CAP - 1)[g // 2]; o = PH * np.arange(I); w = PH * rng.permutation(I) + 1
                m[q, g][:, o] = top[q, g][:, o]; m[q, g][:, w[:n]] = top[q, g][:, w[:n]]
                d[q, g, rng.integers(0, 16, I - n), w[n:]] = P - 1; u[q, g] = PH * rng.integers(0, I, (16, C))
                continue
            n = int(rng.choice(np.array([0, 1, CAP - 1, CAP, CAP + 1, I])))
            if q == 0: n = (CAP, CAP + 1, I, CAP - 1, 1, 0, CAP, CAP + 1)[g]
            if q == 1 or q == 2: n = (CAP, 1, CAP - 1, 0)[g % 4]
            if q == 2 and g == 7: n = CAP + 1
            o = PH * rng.permutation(I); nl = min(n, C // 2); lone, fit, ad = o[:nl], o[nl:n], o[n:]
            cols = 2 * rng.permutation(C // 2)[:nl] + q % 2
            b[q, g, 15, lone] = cols + C * rng.integers(0, P // C - 1, nl); u[q, g][:, cols] = lone
            b[q, g, 15, ad] = 2 * rng.integers(0, C // 2, I - n) + 1 - q % 2 + C * rng.integers(0, P // C - 1, I - n)
            bad = np.concatenate([lone, ad]); d[q, g, rng.integers(0, 16, len(bad)), bad] = P - 1
            m[q, g][:, fit] = top[q, g][:, fit]
            if q == 2:
                o = PH * np.arange(I); z = np.add.reduce(np.arange(1, 17)[:, None] * m[q, g][:, o], axis=0) & (Z - 1)
                left = np.ones(P, dtype=bool); left[P - 1] = False; left[S * np.arange(I) + z] = False
                l = d[q, g][:, o + 1]; l = np.where(left[l], l, rng.choice(np.flatnonzero(left), l.shape))
                d[q, g][:, o + 1] = l; m[q, g][:, o + 1] = np.maximum.reduce(x[q, g][:, l], axis=1)
    return pack(x, m, b, d, u)
def setup_inputs_ties(rng):
    x, m, b, d, u = parts(rng); x[:, 1::2] = x[:, 1::2] >> 6
    k = rng.integers(0, 8, (N, 8, 1, V)); m = np.take_along_axis(m[..., :8], k, 3); m[:, 1::2] = m[:, 1::2] >> 6
    b[:, :2] = np.take_along_axis(b[:, :2, :, :8], k[:, :2], 3); d[:, :2] = np.take_along_axis(d[:, :2, :, :8], k[:, :2], 3)
    lane = np.arange(V); a = rng.integers(40, 81, (N, 16, 1)); high = (np.arange(16)[:, None] == 15) & (lane >= V // 2)
    m[:, 6] = np.where(lane % PH == 0, rng.integers(215, 256, (N, 16, V)), a + high); u[:, 6] = late(rng, (N, 16, C))
    u[..., ::2] = u[:, :, np.arange(16) & 3, ::2]
    return pack(x, m, b, d, u)
def setup_inputs_alike(rng):
    x, m, b, d, u = parts(rng)
    d[:, :3] = b[:, :3]; d[:, 1, 0] = (b[:, 1, 0] + 1) % P; d[:, 2, 15] = (b[:, 2, 15] + 1) % P
    b[:, 3, 15] = rng.integers(0, P, (N, 1)); u[:, 4] = rng.integers(0, V, (N, 1, C))
    for q in range(N):
        v = PH * rng.permutation(I)[:I // 4]; u[q, 4][:, b[q, 4, 15, v] & (C - 1)] = v
    b[:, 5] = rng.integers(0, P, (N, 1, V)); d[:, 5] = rng.integers(0, P, (N, 1, V)); u[:, 6] = (V - 1) * rng.integers(0, 2, (N, 16, C))
    for q in range(N):
        v = PH * rng.permutation(I)[:I // 8]; c = b[q, 7, 15, v] & (C - 1); u[q, 7][:, c] = v; u[(q + 1) % N, 7][:, c] = v
    return pack(x, m, b, d, u)
def setup_inputs_spread(rng):
    x = (np.exp2(8 * rng.random((N, 8, 1, P))) * rng.random((N, 8, 16, P)) ** 3).astype(np.int64)
    m = (np.exp2(8 * rng.random((N, 8, 1, V))) * rng.random((N, 8, 16, V))).astype(np.int64)
    e = rng.choice(np.array([1.0, 2.0, 4.0, 8.0]), (3, N, 8, 1, 1))
    b = (P * rng.random((N, 8, 16, V)) ** e[0]).astype(np.int64); c = (P * rng.random((N, 8, 16, V)) ** e[1]).astype(np.int64)
    d = np.where(np.arange(16)[:, None] >= rng.integers(0, 17, (N, 8, 1, V)), c, b); u = (V * rng.random((N, 8, 16, C)) ** e[2]).astype(np.int64)
    return pack(np.clip(x, 0, 255), np.clip(m, 0, 255), np.clip(b, 0, P - 1), np.clip(d, 0, P - 1), np.clip(u, 0, V - 1))
def setup_inputs_ends(rng):
    def bits(p, n): return 255 * (rng.random((N, 8, 16, n)) < p)
    def lists(n, hi):
        k = rng.random((N, 8, 1, n)); a = hi * rng.integers(0, 2, (N, 8, 16, n))
        return np.where(k < 0.25, 0, np.where(k < 0.5, hi, np.where(k < 0.8, a, rng.integers(0, hi + 1, (N, 8, 16, n)))))
    k = rng.random((N, 8, 1, P)); x = np.where(k < 0.6, 0, np.where(k < 0.63, 255, bits(0.06, P)))
    k = rng.random((N, 8, 1, V)); m = np.where(k < 0.25, 0, np.where(k < 0.5, 255, bits(0.5, V)))
    b = lists(V, P - 1); d = np.where(np.arange(16)[:, None] >= rng.integers(0, 17, (N, 8, 1, V)), lists(V, P - 1), b); u = lists(C, V - 1)
    for t in range(RO):
        for c in (97 * t, 97 * t - 1):
            u[..., c & (C - 1)] = np.where(rng.random((N, 8, 16)) < 0.5, (V - 1) * rng.integers(0, 2, (N, 8, 16)), rng.integers(0, V, (N, 8, 16)))
    x[:, ::2, :, 0] = 255 * rng.integers(0, 2, (N, 4, 16)); x[:, ::2, :, P - 1] = 255 * rng.integers(0, 2, (N, 4, 16)); x[:, 1::2, :, 0] = 0; x[:, 1::2, :, P - 1] = 255
    lo, hi = PH - 1 + PH * (PH % 2), V - 1 - PH
    m[:, 1::2, :, :PH - 1] = 0; m[:, 1::2, :, V - PH:V - 1] = 255; m[..., V - 1] = 255
    m[:, 1::2, :, lo] = 0; m[:, 1::2, :, hi] = 0; m[:, ::2, :, lo] = 255; m[:, ::2, :, hi] = 255
    u[:, 1::2, :, 0] = np.where(np.arange(16) % 2 == 0, 0, V - 1); b[:, 1::2, :, 0] = 0; d[:, 1::2, :, 0] = P - 1
    u[..., C - 1] = np.where(np.arange(16) % 2 == 0, hi, lo)
    b[..., lo] = 0; d[..., lo] = P - 1; b[..., hi] = P - 1; d[..., hi] = 0; d[..., V - 1] = 0
    b[:, :, 15, V - 1] = ((C - 1 - 97 * (PH - 1)) & (C - 1)) + P - C
    return pack(x, m, b, d, u)
def check_inputs(d):
    bad = []
    for k, hi in (("mor", 255), ("mea", 255), ("bas", P - 1), ("der", P - 1), ("use", V - 1)):
        a = np.asarray(d[k]).astype(np.float64)
        if not np.all((a >= 0) & (a <= hi) & (a == np.floor(a))): bad.append("range of " + k)
    return bad
def pick(a, ix):
    return np.stack([np.take(a[g], ix[g], axis=1) for g in range(8)])
def model(kap, mv, own, m, b, d, u):
    c = pick(u, kap)
    s = np.add.reduce(np.abs(pick(m, c) - mv[:, :, None, :]), axis=1)
    k = np.minimum.reduce(np.where(c == own, 2 ** 24, s * 2048 + c), axis=1)
    ok = k < 2 ** 24; w = np.where(ok, k & 2047, 0); dm = pick(d, w)
    diff = pick(b, w) != dm; diff[:, 15] = True
    return ok, w, np.argmax(diff, axis=1), dm
def gap(x, l, mv):
    return np.add.reduce(np.abs(np.maximum.reduce(pick(x, l), axis=2) - mv), axis=1)
def reference(mor, mea, bas, der, use):
    x = mor.astype(np.float32).astype(np.int32).reshape(N, 8, 16, P); m = mea.astype(np.float32).astype(np.int32).reshape(N, 8, 16, V)
    b = bas.astype(np.int32).reshape(N, 8, 16, V); d = der.astype(np.int32).reshape(N, 8, 16, V); u = use.astype(np.int32).reshape(N, 8, 16, C)
    row = np.arange(16)[None, :, None]; i = np.arange(I); count = [0] * N
    for t in range(RO):
        v = PH * i + t % PH; todo = []
        for r in range(N):
            mv = m[r][:, :, v]; bv = b[r][:, :, v]; dv = d[r][:, :, v]; kap = (bv[:, 15] + 97 * t) & (C - 1); mar = count[r] & 127
            ok, w, f, dm = model(kap, mv, v, m[r], b[r], d[r], u[r])
            e = np.where(row < f[:, None, :], bv, dm); old = gap(x[r], dv, mv)
            ad = ok & (gap(x[r], e, mv) + mar < old)
            q = (r + 1 + t % (N - 1)) % N
            sel = np.argsort(ad, axis=1, kind="stable")[:, :CAP]
            asks = ~np.take_along_axis(ad, sel, 1); mv2 = pick(mv, sel)
            ok2, w2, f2, dm2 = model(np.take_along_axis(kap, sel, 1), mv2, -1, m[q], b[q], d[q], u[q])
            e2 = np.where(row < f2[:, None, :], pick(bv, sel), dm2)
            ad2 = asks & (gap(x[r], e2, mv2) + mar < np.take_along_axis(old, sel, 1))
            new = np.where(ad[:, None, :], e, dv); got = ad.copy()
            for g in range(8):
                new[g][:, sel[g][ad2[g]]] = e2[g][:, ad2[g]]; got[g, sel[g][ad2[g]]] = True
            todo.append((ad, w, new, got, (np.add.reduce((row + 1) * mv, axis=1) + t) & (Z - 1)))
        for r in range(N):
            ad, w, new, got, z = todo[r]; d[r][:, :, v] = new; count[r] = int(np.count_nonzero(got))
            for g in range(8):
                j = i[ad[g]]; u[r, g, (j + t) & 15, (j + 37 * t) & (C - 1)] = w[g][j] ^ 1
                j = i[got[g]]; x[r, g][:, S * j + z[g][j]] = m[r, g][:, v[j]]
    return {"yd": d.reshape(N, 128, V).astype(np.float32), "yu": u.reshape(N, 128, C).astype(np.float32), "ym": x.reshape(N, 128, P).astype(np.float32).astype(BF)}

@@ -1,0 +1,623 @@
+import numpy as np
+from concourse.mybir import AluOpType as A, ActivationFunctionType as F
+
+RO, CAP = 5, 64
+BIG = float(2 ** 23)
+CH = 4
+CL = 256 // CH
+SPATH = {"1": (3,), "2": (3,)}
+UPD = {1: (0, 1, 2), 2: (0, 1, 2, 3), 3: (0, 1)}
+SLOT = {}
+for _d in UPD:
+    for _t in UPD[_d]:
+        SLOT[(_d, _t)] = len(SLOT)
+
+SCRATCH = {}
+
+
+def _b(names, cols, dtype="float32", where="sbuf"):
+    for nm in names.split():
+        SCRATCH[nm] = (where, [128, cols], dtype)
+
+
+_b("K1 K2 DD CC WW NN UU DF", 512, "float32", "psum")
+_b("morS", 7168, "bfloat16")
+_b("meaS neq oneb m16", 1024, "bfloat16")
+_b("basI derI", 1024, "int32")
+_b("useI", 512, "int32")
+_b("basF derF Tt lane nbr", 1024)
+_b("useF", 512)
+_b("meaQ", 3072, "bfloat16")
+_b("useQ", 1536)
+_b("TQ", 3072)
+_b("lu lt", 256 * len(SLOT))
+_b("UN TN", 1024)
+_b("mvr", 16384, "bfloat16")
+_b("D16", 1024, "uint16")
+_b("cl of", 80, "uint16")
+_b("XX Y0 Y1 dd1 dd2 aa1 aa2", 4096, "bfloat16")
+_b("cU1 cU2 EU1 EU2", 256, "uint16")
+_b("cF1 cF2 SS1 SS2 EP1 EP2 val up p1 p2 p3 n4 mbig bigs", 256)
+_b("ZB1 ZB2 HH1 HH2 LT1 LT2 LZ LB one If nIf o16 hold", 128)
+_b("mu", 64, "uint16")
+_b("qi", 256, "int32")
+_b("eq ad aE1 aE2 cum zz ad1 got d1 old ge ab junk", 256, "bfloat16")
+_b("Ib nIb IB I14 nI14 tmb bo nbo tri k15", 128, "bfloat16")
+_b("W8 w8t tm8", 8, "bfloat16")
+_b("w64 t64 t65", 64, "bfloat16")
+_b("e15 mk8", 64)
+_b("RR rr0", 16)
+_b("ik8 il8", 64, "int32")
+_b("km", 260)
+_b("ikm ilm", 260, "int32")
+_b("nm bia", 8)
+_b("cnt", 1)
+_b("pw", 1)
+
+QS = ("V", "S", "P", "G")
+SEMAPHORES = list(QS) + ["ld%d" % i for i in range(6)] + ["mc%d" % t for t in range(RO)] + ["st", "sM", "sU", "sT", "sR"]
+for _d in UPD:
+    SEMAPHORES += ["aM%d" % _d, "aU%d" % _d, "aT%d" % _d]
+    for _t in UPD[_d]:
+        SEMAPHORES += ["au%d%d" % (_d, _t), "at%d%d" % (_d, _t)]
+
+CY = 1.04e-3
+GA = 1.56
+START = {"keys2": -21, "scanL1": -50, "D16": -33, "gsel": 62, "act": 28, "cF1": 3, "p1": -14, "gapL2": 13, "delta": 23, "min2": 34, "abs1": 22, "ad1": 34,
+         "useQ": 9, "old": 22, "out": -16, "diff": -36, "arrive": -18, "D16n": 33, "cF2": -8, "L1": 28, "E1": -8, "places": 13, "pe": 35, "cU1": 12, "TQ": 26,
+         "count": 35, "dmo": 28, "scand2": -22, "D": -26, "load": -10, "scanL2": 9, "tt": 4, "copy": 15, "T": -21, "E2": -39, "gapL1": 34, "keys1": 14, "": 32,
+         "send": 31, "mvr": -16, "up": 18, "cum": 26, "basF": -14, "scand1": 29, "L2": 1, "UN": -2, "g": -18, "T0": -22, "gapD": 6, "derF0": -55, "TN": 48,
+         "lists": -20, "eq": -2, "useF": 26, "kd": -16, "p2": 27, "cU2": -23, "ts": 36, "neq": -62, "cand1": 8, "scanD": -21, "val": 6, "cand2": -7, "min1": -5,
+         "abs2": -25, "got": -1}
+FOUND = {}
+
+
+def rank_program(g, core, T, topo):
+    rank = T.rank_of(core)
+    if rank is None:
+        return
+    n = len(T.cores)
+    sm = T.sem
+    ops, lastw, readers = [], {}, {}
+
+    def op(q, cost, calls, R=(), W=(), sem=None, inc=1, wake=0.0, label="", gat=0.0):
+        k = len(ops)
+        deps = {}
+
+        def dep(a, kind):
+            deps[a] = max(deps.get(a, 0), kind)
+        for r in R:
+            if r in lastw:
+                a = lastw[r]
+                dep(a, 1 if r[0] == "!" and q == "P" and ops[a]["q"] == "P" else 2)
+            if r[0] == "!":
+                for a in readers.get(r, ()):
+                    if ops[a]["q"] != q:
+                        dep(a, 1)
+        for w in W:
+            for a in ([lastw[w]] if w in lastw else []) + readers.get(w, []):
+                dep(a, 1)
+        for r in R:
+            readers.setdefault(r, []).append(k)
+        for w in W:
+            lastw[w] = k
+            readers[w] = []
+        ops.append({"q": q, "cost": cost, "gat": gat, "calls": calls, "deps": deps, "sem": sem, "inc": inc, "wake": wake, "label": label})
+        return k
+
+    def V(c, call, R, W, f=1.0, label=""):
+        op("V", 0.06 + max(64.0, c * f) * CY, [call], R, W, label=label, gat=c * CY if f == GA else 0.0)
+
+    def S(c, call, R, W, f=1.0, label=""):
+        op("S", 0.09 + c * f * CY, [call], R, W, label=label, gat=c * CY if f == GA else 0.0)
+
+    def P(c, mms, R, W, label="pe"):
+        def call(m):
+            return lambda e: e.matmul(m[0], m[1], m[2], m[3], m[4])
+        op("P", 0.02 + c * 0.85e-3, [call(m) for m in mms], R, W, label=label)
+
+    def G(c, call, R, W, label="g"):
+        op("G", 0.2 + 2 * c * CY, [call], R, W, label=label)
+
+    def sel(out, in_, pattern, opc, base, cm, R, W, c, label="gsel"):
+        G(c, lambda e: e.affine_select(out, in_, pattern, opc, 0.0, base, cm), R, W, label)
+
+    def gcopy(out, in_, R, W, c, label):
+        sel(out, in_, [[0, c]], A.is_ge, 0, 0, R, W, c, label)
+
+    def ts(out, in0, s1, op0, R, W, c, f=1.0, label="ts"):
+        V(c, lambda e: e.tensor_scalar(out, in0, s1, None, op0), R, W, f, label)
+
+    def tt(out, a, b, o, R, W, c, f=2.0, label="tt"):
+        V(c, lambda e: e.tensor_tensor(out, a, b, o), R, W, f, label)
+
+    def tc(out, a, R, W, c, f=1.0, label="tc"):
+        V(c, lambda e: e.tensor_copy(out, a), R, W, f, label)
+
+    def scan(out, d0, d1, o0, o1, R, W, c, f, label):
+        V(c, lambda e: e.tensor_tensor_scan(out, d0, d1, 0.0, o0, o1), R, W, f, label)
+
+    def act(out, in_, R, W, c, func=F.Copy, scale=1.0, f=1.0, label="act"):
+        S(c, lambda e: e.activation(out, in_, func, scale=scale), R, W, f, label)
+
+    def both(out, in_, R, W, c, label):
+        op("VS", 0.08 + c * GA * CY, [(lambda e: e.tensor_copy(out, in_), lambda e: e.activation(out, in_, F.Copy))], R, W, label=label, gat=c * CY)
+
+    def load(qn, i, out, in_, W, us):
+        op(qn, 0.1, [lambda e: e.dma_start(out, in_)], (), W, sem="ld%d" % i, inc=16, wake=us, label="load")
+    load("Y", 0, T.basI[:], T.bas[:], ["basI"], 3.5)
+    load("S", 1, T.meaS[:], T.mea[:], ["meaS"], 3.5)
+    load("Y", 2, T.useI[:], T.use[:], ["useI"], 4.0)
+    load("Y", 3, T.derI[:], T.der[:], ["derI"], 5.5)
+    load("S", 4, T.morS[:, 0:3072], T.mor[:], ["mor"], 8.0)
+    load("Y", 5, T.morS[:, 4096:7168], T.mor[:], ["morc"], 10.0)
+
+    V(128, lambda e: e.memset(T.one[:], 1.0), [], ["one"])
+    V(512, lambda e: e.memset(T.oneb[:], 1.0), [], ["oneb"])
+    V(256, lambda e: e.memset(T.bigs[:], 2.0 * BIG), [], ["bigs"])
+    sel(T.e15[:], T.one[:, 0:64], [[-16, 8], [0, 8]], A.is_equal, -15, 1, ["one"], ["e15"], 64)
+    G(64, lambda e: e.iota(T.ik8[:], [[0, 8], [-1, 8]], 128, 1), [], ["ik8"])
+    sel(T.rr0[:], T.one[:, 0:16], [[-8, 16]], A.is_ge, 0, 1, ["one"], ["rr0"], 16)
+    sel(T.RR[:], T.rr0[:], [[8, 16]], A.is_ge, 7, -1, ["rr0"], ["RR"], 16)
+    ts(T.il8[:], T.ik8[:], 7, A.bitwise_and, ["ik8"], ["il8"], 64)
+    ts(T.mk8[:], T.il8[:], 0.0, A.is_equal, ["il8"], ["mk8"], 64)
+    sel(T.If[:], T.one[:], [[-1, 128]], A.is_equal, 0, 1, ["one"], ["If"], 128)
+    sel(T.tm8[:], T.oneb[:, 0:8], [[-16, 8]], A.is_ge, 0, 1, ["oneb"], ["tm8"], 8)
+    sel(T.w8t[:], T.tm8[:], [[16, 8]], A.is_ge, 15, -1, ["tm8"], ["w8t"], 8)
+    act(T.W8[:], T.w8t[:], ["w8t"], ["W8"], 8, scale=2048.0)
+    for nm_, sc in (("Ib", 1.0), ("IB", BIG), ("nIb", -1.0), ("nIf", -1.0), ("I14", 16384.0), ("nI14", -32768.0)):
+        act(T[nm_][:], T.If[:], ["If"], [nm_], 128, scale=sc)
+    act(T.o16[:], T.one[:], ["one"], ["o16"], 128, scale=1.0 / 16)
+    sel(T.mbig[:], T.bigs[:], [[0, 16], [1, 16]], A.is_equal, 0, 0, ["bigs"], ["mbig"], 256)
+    sel(T.hold[:], T.one[:], [[0, 16], [1, 8]], A.not_equal, 0, 0, ["one"], ["hold"], 128)
+    sel(T.m16[:], T.oneb[:], [[0, 64], [1, 16]], A.not_equal, 0, 0, ["oneb"], ["m16"], 1024)
+    V(128, lambda e: e.memset(T.ZB1[:], 0.0), [], ["ZB1"])
+    V(128, lambda e: e.memset(T.ZB2[:], 0.0), [], ["ZB2"])
+    qi = [T.qi[:, 16 * i:16 * i + 16] for i in range(16)]
+    G(16, lambda e: e.iota(qi[0], [[0, 16]], 0, 1), [], ["pi"])
+    ts(qi[1], qi[0], 15, A.bitwise_and, ["pi"], ["pj"], 16)
+    ts(qi[2], qi[1], 12.0, A.mult, ["pj"], ["pk"], 16)
+    G(16, lambda e: e.iota(qi[3], [[192, 16]], 0, 0), [], ["s12"])
+    tt(qi[4], qi[2], qi[3], A.add, ["pk", "s12"], ["t12"], 16)
+    ts(T.pw[:], T.qi[:, 16:17], 1.0, A.add, ["pj"], ["pw"], 1)
+    sel(T.t64[:], T.oneb[:, 0:64], [[-16, 8], [0, 8]], A.is_ge, 0, 1, ["oneb"], ["t64"], 64)
+    sel(T.t65[:], T.t64[:], [[16, 8], [0, 8]], A.is_ge, 15, -1, ["t64"], ["t65"], 64)
+    ts(T.w64[:], T.t65[:], T.pw[:, 0:1], A.mult, ["t65", "pw"], ["w64"], 64)
+    sel(T.tmb[:], T.oneb[:, 0:128], [[-16, 8], [0, 16]], A.is_ge, 0, 1, ["oneb"], ["tmb"], 128)
+    sel(T.bo[:], T.tmb[:], [[16, 8], [0, 16]], A.is_ge, 15, -1, ["tmb"], ["bo"], 128)
+    act(T.nbo[:], T.bo[:], ["bo"], ["nbo"], 128, scale=-1.0)
+    sel(T.tmb[:], T.bo[:], [[1, 128]], A.is_ge, 0, -1, ["bo"], ["tmb"], 128)
+    act(T.tri[:], T.tmb[:], ["tmb"], ["tri"], 128, scale=8192.0)
+    sel(T.tmb[:], T.oneb[:, 0:128], [[0, 8], [1, 16]], A.is_equal, -15, 0, ["oneb"], ["tmb"], 128)
+    act(T.k15[:], T.tmb[:], ["tmb"], ["k15"], 128, scale=8192.0)
+    G(1024, lambda e: e.iota(T.lane[:], [[1, 1024]], 0, 0, allow_small_or_imprecise_dtypes=True), [], ["lane"])
+    G(1024, lambda e: e.iota(T.nbr[:], [[2, 512], [-1, 2]], 1, 0, allow_small_or_imprecise_dtypes=True), [], ["nbr"])
+    G(260, lambda e: e.iota(T.ikm[:], [[1, 260]], 128, -1), [], ["ikm"])
+    ts(T.ilm[:], T.ikm[:], 15, A.bitwise_and, ["ikm"], ["ilm"], 260)
+    ts(T.km[:], T.ilm[:], 0.0, A.is_equal, ["ilm"], ["km"], 260)
+    V(1, lambda e: e.memset(T.nm[:, 0:1], 0.0), [], ["nm0"])
+    V(1, lambda e: e.memset(T.bia[:, 0:1], 4096.0), [], ["bia"])
+
+    def plus4096(out, in_, R, W, c, label):
+        S(c, lambda e: e.activation(out, in_, F.Identity, bias=T.bia[:, 0:1]), R + ["bia"], W, 1.0, label)
+
+    for tau in range(4):
+        tc(T.basF[:, tau::4], T.basI[:, tau::4], ["basI"], ["basF%d" % tau], 256, label="basF")
+    tc(T.useF[:], T.useI[:], ["useI"], ["useF"], 512, label="useF")
+    derall = ["derF%d" % x for x in range(4)]
+    for tau in range(4):
+        tc(T.D16[:, 256 * tau:256 * tau + 256], T.derI[:, tau::4], ["derI"], ["D16_%d" % tau], 256, label="D16")
+
+    def mvrep(tau, k, q):
+        o, i_ = T.mvr[:, 4096 * tau + k:4096 * tau + 4096:16], T.meaS[:, tau::4]
+        w = ["mvr%d.%d" % (tau, k)]
+        if q == "V":
+            tc(o, i_, ["meaS"], w, 256, 0.5, "mvr")
+        elif q == "S":
+            act(o, i_, ["meaS"], w, 256, label="mvr")
+        else:
+            gcopy(o, i_, ["meaS"], w, 256, "mvr")
+    for k in range(16):
+        mvrep(0, k, "S" if k % 3 else "V")
+    tt(T.neq[:], T.basI[:], T.derI[:], A.not_equal, ["basI", "derI"], ["neq"], 1024, label="neq")
+    tc(T.derF[:], T.derI[:], ["derI"], derall, 1024, label="derF0")
+    Th = ["Th0", "Th1"]
+    for hf in range(2):
+        c0 = slice(512 * hf, 512 * hf + 512)
+        bank = ("NN", "UU")[hf]
+        P(1024, [(T[bank][:], T.tri[:], T.neq[:, c0], True, False), (T[bank][:], T.k15[0:1, :], T.oneb[0:1, 0:512], False, True)],
+          ["tri", "k15", "neq", "oneb"], ["!" + bank])
+        plus4096(T.Tt[:, c0], T.derF[:, c0], derall, ["Th%d" % hf], 512, "")
+        tt(T.Tt[:, c0], T.Tt[:, c0], T[bank][:], A.min, ["Th%d" % hf, "!" + bank], ["Th%d" % hf], 512, 1.0, "T0")
+
+    def lists(tau):
+        P(512, [(T.WW[:, 64 * h:64 * h + 64], T.basF[:, 4 * h + tau::8], T.e15[:], True, True) for h in range(2)], ["basF%d" % tau, "e15"], ["!WW"], "lists")
+        for h in range(2):
+            tt(T.LB[:, h::2], T.WW[:, 64 * h:64 * h + 64], T.mk8[:], A.mult, ["!WW", "mk8"], ["LB%d" % h], 64, 1.0, "lists")
+        P(256, [(T.WW[:, 128:144], T.LB[:], T.RR[:], True, True)], ["LB0", "LB1", "RR"], ["!WW"], "lists")
+        for t in [x for x in range(RO) if x % 4 == tau]:
+            ts(qi[5], T.WW[:, 128:144], float(97 * t), A.add, ["!WW"], ["q5"], 16, label="lists")
+            ts(qi[6], qi[5], 511, A.bitwise_and, ["q5"], ["q6"], 16, label="lists")
+            tc(T.cl[:, 16 * t:16 * t + 16], qi[6], ["q6"], ["cl%d" % t], 16, label="lists")
+
+    def places(tau):
+        P(128, [(T.WW[:, 64 * h:64 * h + 64], T.meaS[:, 4 * h + tau::8], T.w64[:], True, True) for h in range(2)], ["meaS", "w64"], ["!WW"], "places")
+        for h in range(2):
+            tt(T.LZ[:, h::2], T.WW[:, 64 * h:64 * h + 64], T.mk8[:], A.mult, ["!WW", "mk8"], ["LZ%d" % h], 64, 1.0, "places")
+        P(256, [(T.WW[:, 128:144], T.LZ[:], T.RR[:], True, True)], ["LZ0", "LZ1", "RR"], ["!WW"], "places")
+        for t in [x for x in range(RO) if x % 4 == tau]:
+            ts(qi[7], T.WW[:, 128:144], float(t), A.add, ["!WW"], ["q7"], 16, label="places")
+            ts(qi[8], qi[7], 7, A.bitwise_and, ["q7"], ["q8"], 16, label="places")
+            tt(qi[9], qi[8], qi[4], A.add, ["q8", "t12"], ["q9"], 16, label="places")
+            tc(T.of[:, 16 * t:16 * t + 16], qi[9], ["q9"], ["of%d" % t], 16, label="places")
+
+    peers = {d: T.cores[(rank - d) % n] for d in UPD}
+    common = [e for e in topo.engines(core, peers[1]) if all(e in topo.engines(core, p) for p in peers.values())]
+    mask = sum(1 << e for e in common)
+    ne = len(common)
+    sent, sends = {}, {}
+
+    def send(d, out, in_, asem, lsem, R):
+        rid, pid = topo.addr(peers[d])[:2]
+        sent[lsem] = sent.get(lsem, 0) + ne
+        sends[asem] = len(ops)
+        op("G", 0.4, [lambda e: e.remote_dma(out, in_, sm[asem], sm[lsem], pid, rid, mask)], R, (), sem=lsem, inc=0, wake=4.0, label="send")
+
+    def arrive(asem, W, us):
+        k = op("R", us, [], (), W, sem=asem, inc=ne, label="arrive")
+        ops[k]["deps"][sends[asem]] = 0
+
+    lists(0)
+    for d in (1, 2, 3):
+        uq, mq, tq = T.useQ[:, 512 * d - 512:512 * d], T.meaQ[:, 1024 * d - 1024:1024 * d], T.TQ[:, 1024 * d - 1024:1024 * d]
+        send(d, uq, T.useF[:], "aU%d" % d, "sU", ["useF"])
+        send(d, mq, T.meaS[:], "aM%d" % d, "sM", ["meaS"])
+        send(d, tq, T.Tt[:], "aT%d" % d, "sT", Th)
+        arrive("aU%d" % d, ["useQ%d" % d], 6.0)
+        arrive("aM%d" % d, ["meaQ%d" % d], 6.0)
+        arrive("aT%d" % d, ["TQ%d.%d" % (d, x) for x in range(4)], 8.0)
+
+    def find(c, t, use, useR, mea, meaR):
+        tau = t % 4
+        K, cU, cF, dd, aa = T["K" + c], T["cU" + c], T["cF" + c], T["dd" + c], T["aa" + c]
+        cl = T.cl[:, 16 * t:16 * t + 16]
+        V(256, lambda e: e.tensor_copy(cU[:], use.indirect(cl)), [useR, "cl%d" % t], ["cU" + c], GA, "cU" + c)
+        S(256, lambda e: e.activation(cF[:], use.indirect(cl), F.Copy), [useR, "cl%d" % t], ["cF" + c], GA, "cF" + c)
+        reps = ["mvr%d.%d" % (tau, k) for k in range(16)]
+
+        def gat(a, b, j):
+            return lambda e: e.tensor_tensor(dd[:, a:b], mea.indirect(cU[:, CL * j:CL * (j + 1)]), T.mvr[:, 4096 * tau + a:4096 * tau + b], A.subtract)
+        for j in range(CH):
+            a, b = 16 * CL * j, 16 * CL * (j + 1)
+            dR = "dd%s.%d" % (c, j)
+            if j in SPATH[c]:
+                act(dd[:, a:b], mea.indirect(cU[:, CL * j:CL * (j + 1)]), [meaR, "cU" + c], [dR], b - a, f=GA, label="scand" + c)
+                for a2 in range(a, b, 512):
+                    rep = T.mvr[:, 4096 * tau + a2:4096 * tau + a2 + 512]
+                    P(1024, [(T.CC[:], T.nIb[:], rep, True, False), (T.CC[:], T.Ib[:], dd[:, a2:a2 + 512], False, True)], ["Ib", "nIb", dR] + reps, ["!CC"], "scand" + c)
+                    act(aa[:, a2:a2 + 512], T.CC[:], ["!CC"], ["aa%s.%d" % (c, a2)], 512, F.Abs, label="scand" + c)
+                continue
+            V(b - a, gat(a, b, j), [meaR, "cU" + c] + reps, [dR], GA, "cand" + c)
+            act(aa[:, a:b], dd[:, a:b], [dR], ["aa%s.%d" % (c, x) for x in range(a, b, 512)], b - a, F.Abs, label="abs" + c)
+        if c == "1":
+            tt(T.eq[:], cF[:], T.lane[:, tau::4], A.is_equal, ["cF1", "lane"], ["eq"], 256, label="eq")
+        mm, R, cy = [], ["cF" + c, "If", "W8"] + ["aa%s.%d" % (c, x) for x in range(0, 4096, 512)], 0
+        for h in range(2):
+            o = K[:, 128 * h:128 * h + 128]
+            mm.append((o, cF[:, h::2], T.If[:], True, False))
+            cy += 512
+            if c == "1":
+                mm.append((o, T.eq[:, h::2], T.IB[:], False, False))
+                cy += 128
+            for k in range(16):
+                mm.append((K[:, 128 * h + k:128 * h + 128:16], aa[:, 16 * h + k::32], T.W8[:], False, k == 15))
+                cy += 64
+        if c == "1":
+            R += ["eq", "IB"]
+        P(cy, mm, R, ["!K" + c], "keys" + c)
+        SS, ZB, HH, LT = T["SS" + c], T["ZB" + c], T["HH" + c], T["LT" + c]
+        scan(SS[:], T.mbig[:], K[:, 0:256], A.max, A.min, ["!K" + c, "mbig"], ["SS" + c], 256, 1.0, "min" + c)
+        act(ZB[:, 0::8], SS[:, 15::16], ["SS" + c], ["ZB" + c], 16, label="min" + c)
+        scan(HH[:], T.hold[:], ZB[:], A.mult, A.add, ["ZB" + c, "hold"], ["HH" + c], 128, 1.0, "min" + c)
+        for h in range(2):
+            tt(LT[:, h::2], HH[:, 64 * h:64 * h + 64], T.mk8[:], A.mult, ["HH" + c, "mk8"], ["LT%s.%d" % (c, h)], 64, label="min" + c)
+        P(256, [(K[:, 256:272], LT[:], T.RR[:], True, True)], ["LT%s.0" % c, "LT%s.1" % c, "RR"], ["!K" + c], "keys" + c)
+        mi, mj, m = qi[8 + 2 * int(c)], qi[9 + 2 * int(c)], mu(c, t)
+        tc(mi, K[:, 256:272], ["!K" + c], ["mi" + c], 16, label="min" + c)
+        ts(mj, mi, 1023, A.bitwise_and, ["mi" + c], ["mj" + c], 16, label="min" + c)
+        tc(m[0], mj, ["mj" + c], [m[1]], 16, label="min" + c)
+
+    def mu(c, t):
+        k = 2 * int(c) - 2 + t % 2
+        return T.mu[:, 16 * k:16 * k + 16], "mu%d" % k
+
+    flip = [0]
+
+    def far(lst, lstR, window, winR, out, outW, tau, label):
+        y = flip[0] % 2
+        flip[0] += 1
+        X, Y = T.XX, T["Y%d" % y]
+        for j in range(CH):
+            a, b = 16 * CL * j, 16 * CL * (j + 1)
+            both(X[:, a:b], window.indirect(lst[:, CL * j:CL * (j + 1)]), [lstR] + winR, ["X.%d" % j], b - a, label)
+            scan(Y[:, a:b], T.m16[:, 0:b - a], X[:, a:b], A.mult, A.max, ["X.%d" % j, "m16"], ["Y%d.%d" % (y, j)], b - a, 0.5, "scan" + label)
+        P(512, [(T.DF[:, 0:256], T.nIb[:], T.meaS[:, tau::4], True, False), (T.DF[:, 0:256], T.Ib[:], Y[:, 15::16], False, True)],
+          ["nIb", "Ib", "meaS"] + ["Y%d.%d" % (y, j) for j in range(CH)], ["!DF"], "diff")
+        act(out[:], T.DF[:, 0:256], ["!DF"], [outW], 256, F.Abs, label="gap" + label)
+
+    def own(t):
+        find("1", t, T.useF[:], "useF", T.meaS[:], "meaS")
+
+    def ask(t):
+        d = 1 + t % 3
+        find("2", t, T.useQ[:, 512 * d - 512:512 * d], "useQ%d" % d, T.meaQ[:, 1024 * d - 1024:1024 * d], "meaQ%d" % d)
+
+    def build(c, t, tab, tabR):
+        tau = t % 4
+        EP, EU = T["EP" + c], T["EU" + c]
+        m = mu(c, t)
+        V(256, lambda e: e.tensor_tensor(EP[:], tab.indirect(m[0]), T.basF[:, tau::4], A.max), tabR + [m[1], "basF%d" % tau], ["EP" + c], GA, "E" + c)
+        tc(EU[:], EP[:], ["EP" + c], ["EU" + c], 256, label="E" + c)
+
+    own(0)
+    lists(1)
+    places(0)
+    places(1)
+    for k in range(16):
+        mvrep(1, k, "G")
+    ask(0)
+    lists(2)
+    lists(3)
+    places(2)
+    places(3)
+    for tau in (2, 3):
+        for k in range(16):
+            mvrep(tau, k, "G")
+
+    If, nIf, Ib, nIb = T.If[:], T.nIf[:], T.Ib[:], T.nIb[:]
+    D1, D2, N1 = T.DD[:, 0:256], T.DD[:, 256:512], T.NN[:, 0:256]
+    W1, W2, U1, U2 = T.WW[:, 0:256], T.WW[:, 256:512], T.UU[:, 0:256], T.UU[:, 256:512]
+    done = {}
+
+    def taken(dn, x):
+        if (dn, x) in done:
+            return
+        done[(dn, x)] = 1
+        arrive("au%d%d" % (dn, x), ["lu%d%d" % (dn, x)], 5.0)
+        arrive("at%d%d" % (dn, x), ["lt%d%d" % (dn, x)], 5.0)
+        s = 256 * SLOT[(dn, x)]
+        b = 512 * dn - 512 + 37 * x
+        gcopy(T.useQ[:, b:b + 256], T.lu[:, s:s + 256], ["lu%d%d" % (dn, x)], ["useQ%d" % dn], 256, "useQ")
+        gcopy(T.TQ[:, 1024 * dn - 1024 + x % 4:1024 * dn:4], T.lt[:, s:s + 256], ["lt%d%d" % (dn, x)], ["TQ%d.%d" % (dn, x % 4)], 256, "TQ")
+
+    def rnd(t):
+        tau, d, last = t % 4, 1 + t % 3, t + 1 == RO
+        nm, nmR = T.nm[:, t:t + 1], "nm%d" % t
+        derT, basT, derR, mv = T.derF[:, tau::4], T.basF[:, tau::4], "derF%d" % tau, T.meaS[:, tau::4]
+        off = T.of[:, 16 * t:16 * t + 16]
+        if t:
+            op("Y", 0.1, [lambda e: e.dma_start(T.morS[:, 4096:7168], T.morS[:, 0:3072])], ["mor"], ["morc"], sem="mc%d" % t, inc=16, wake=4.5, label="copy")
+        far(T.D16[:, 256 * tau:256 * tau + 256], "D16_%d" % tau, T.morS[:, 0:3072], ["mor"], T.ad, "ad", tau, "D")
+        P(256, [(D1, T.nbo[:], T.ad[:], True, False)], ["nbo", "ad"], ["!DD"], "delta")
+        build("1", t, T.Tt[:], Th)
+        far(T.EU1, "EU1", T.morS[:], ["mor", "morc"], T.aE1, "aE1", tau, "L1")
+        P(256, [(D1, T.bo[:], T.aE1[:], False, True)], ["bo", "aE1"], ["!DD"], "delta")
+        m = mu("1", t)
+        u0 = 37 * t
+        useT = T.useF[:, u0:u0 + 256]
+        S(256, lambda e: e.activation(T.val[:], T.nbr[:].indirect(m[0]), F.Copy), ["nbr", m[1]], ["val"], GA, "val")
+        P(2048, [(U1, If, T.val[:], True, False), (U1, nIf, useT, False, True)], ["If", "nIf", "val", "useF"], ["!UU"], "kd")
+        tt(U1, U1, T.km[:, t:t + 256], A.mult, ["!UU", "km"], ["!UU"], 256, 1.0, "kd")
+        ts(T.ad1[:], D1, nm, A.is_lt, ["!DD", nmR], ["ad1"], 256, label="ad1")
+        tt(T.up[:], U1, T.ad1[:], A.mult, ["!UU", "ad1"], ["up"], 256, 1.0, "up")
+        tt(useT, T.up[:], useT, A.add, ["useF", "up"], ["useF"], 256, label="up")
+        if not last:
+            UN = T.UN[:, 256 * t:256 * t + 256]
+            gcopy(UN, useT, ["useF"], ["UN%d" % t], 256, "UN")
+            for dn in UPD:
+                if t in UPD[dn]:
+                    s = 256 * SLOT[(dn, t)]
+                    send(dn, T.lu[:, s:s + 256], UN, "au%d%d" % (dn, t), "sR", ["UN%d" % t])
+            own(t + 1)
+        else:
+            op("Y", 0.1, [lambda e: e.dma_start(T.yu[:], T.useF[:])], ["useF"], ["yu"], sem="st", inc=16, wake=4.0, label="out")
+        scan(T.cum[:], T.oneb[:, 0:256], T.ad1[:], A.add, A.subtract, ["oneb", "ad1"], ["cum"], 256, 0.5, "cum")
+        ts(T.zz[:], T.cum[:], float(CAP), A.is_gt, ["cum"], ["zz"], 256, f=0.5, label="cum")
+        P(1024, [(D2, T.I14[:], T.zz[:], True, False), (D2, T.nI14[:], T.ad1[:], False, False), (D2, T.nbo[:], T.ad[:], False, False)],
+          ["I14", "nI14", "nbo", "zz", "ad1", "ad"], ["!DD"], "delta")
+        S(256, lambda e: e.activation(T.old[:], T.morS[:, 0:3072].indirect(off), F.Copy), ["mor", "of%d" % t], ["old"], GA, "old")
+        P(512, [(U2, Ib, mv, True, False), (U2, nIb, T.old[:], False, True)], ["Ib", "nIb", "meaS", "old"], ["!UU"], "dmo")
+        build("2", t, T.TQ[:, 1024 * d - 1024:1024 * d], ["TQ%d.%d" % (d, x) for x in range(4)])
+        far(T.EU2, "EU2", T.morS[:], ["mor", "morc"], T.aE2, "aE2", tau, "L2")
+        P(256, [(D2, T.bo[:], T.aE2[:], False, True)], ["bo", "aE2"], ["!DD"], "delta")
+        ts(T.got[:], D2, nm, A.is_lt, ["!DD", nmR], ["got"], 256, label="got")
+        tt(T.d1[:], U2, T.got[:], A.mult, ["!UU", "got"], ["d1"], 256, 1.0, "got")
+        V(256, lambda e: e.tensor_tensor(T.morS[:, 0:3072].indirect(off), T.d1[:], T.old[:], A.add), ["d1", "old", "of%d" % t], ["mor"], 3.5, "got")
+        if last:
+            op("Y", 0.1, [lambda e: e.dma_start(T.ym[:], T.morS[:, 0:3072])], ["mor"], ["ym"], sem="st", inc=16, wake=5.0, label="out")
+        tt(T.p1[:], T.EP1[:], T.ad1[:], A.mult, ["EP1", "ad1"], ["p1"], 256, label="p1")
+        P(1024, [(W1, Ib, T.got[:], True, False), (W1, nIb, T.ad1[:], False, True), (W2, Ib, T.oneb[:, 0:256], True, False), (W2, nIb, T.got[:], False, True)],
+          ["Ib", "nIb", "oneb", "got", "ad1"], ["!WW"], "p2")
+        tt(T.p2[:], W1, T.EP2[:], A.mult, ["!WW", "EP2"], ["p2"], 256, 1.0, "p2")
+        tt(T.p3[:], W2, derT, A.mult, ["!WW", derR], ["p3"], 256, 1.0, "p2")
+        P(3072, [(N1, If, T.p1[:], True, False), (N1, If, T.p2[:], False, False), (N1, If, T.p3[:], False, True)], ["If", "p1", "p2", "p3"], ["!NN"], "p2")
+        V(256, lambda e: e.tensor_scalar(T.ge[:], N1, 4096.0, -4096.0, A.is_ge, A.mult), ["!NN"], ["ge"], 1.0, "p2")
+        tt(derT, N1, T.ge[:], A.add, ["!NN", "ge"], [derR], 256, 1.0, "p2")
+        if t == 0:
+            tc(T.D16[:, 0:256], T.derF[:, 0::4], ["derF0"], ["D16_0"], 256, label="D16n")
+        if last:
+            op("Y", 0.1, [lambda e: e.dma_start(T.yd[:], T.derF[:])], derall, ["yd"], sem="st", inc=16, wake=5.0, label="out")
+            return
+        tt(T.ab[:], basT, derT, A.not_equal, ["basF%d" % tau, derR], ["ab"], 256, label="T")
+        plus4096(T.n4[:], derT, [derR], ["n4"], 256, "T")
+        P(512, [(N1, T.tri[:], T.ab[:], True, False), (N1, T.k15[0:1, :], T.oneb[0:1, 0:256], False, True)], ["tri", "k15", "oneb", "ab"], ["!NN"], "T")
+        tt(T.Tt[:, tau::4], N1, T.n4[:], A.min, ["!NN", "n4"], Th, 256, 1.0, "T")
+        TN = T.TN[:, 256 * t:256 * t + 256]
+        gcopy(TN, T.Tt[:, tau::4], Th, ["TN%d" % t], 256, "TN")
+        for dn in UPD:
+            if t in UPD[dn]:
+                s = 256 * SLOT[(dn, t)]
+                send(dn, T.lt[:, s:s + 256], TN, "at%d%d" % (dn, t), "sR", ["TN%d" % t])
+        S(256, lambda e: e.activation(T.junk[:], T.got[:], F.Copy, accum_out=T.cnt[:]), ["got"], ["cnt", "junk"], 1.0, "count")
+        P(64, [(T.DF[:, 256:257], T.o16[:], T.cnt[:], True, True)], ["o16", "cnt"], ["!DF"], "count")
+        tc(T.qi[:, 224:225], T.DF[:, 256:257], ["!DF"], ["ai"], 1, label="count")
+        ts(T.qi[:, 240:241], T.qi[:, 224:225], 127, A.bitwise_and, ["ai"], ["aj"], 1, label="count")
+        ts(T.nm[:, t + 1:t + 2], T.qi[:, 240:241], -1.0, A.mult, ["aj"], ["nm%d" % (t + 1)], 1, label="count")
+        dn = 1 + (t + 1) % 3
+        for x in UPD[dn]:
+            if x <= t:
+                taken(dn, x)
+        ask(t + 1)
+
+    for t in range(RO):
+        rnd(t)
+    emit(g, sm, ops, sent)
+
+
+def schedule(ops, bonus, ga, look, lag):
+    m = len(ops)
+    cost = [o["cost"] + o["gat"] * (ga - GA) for o in ops]
+    succ = [[] for _ in range(m)]
+    for k, o in enumerate(ops):
+        for a in o["deps"]:
+            succ[a].append(k)
+    prio = [0.0] * m
+    for k in range(m - 1, -1, -1):
+        o = ops[k]
+        best = 0.0
+        for s in succ[k]:
+            if prio[s] > best:
+                best = prio[s]
+        prio[k] = best + cost[k] + (0.0 if o["q"] == "R" else o["wake"] + 0.05)
+    eff = [prio[k] + bonus.get(ops[k]["label"], 0.0) for k in range(m)]
+    left = [len(o["deps"]) for o in ops]
+    ready_at = [0.0] * m
+    ready = {"V": [], "S": [], "P": [], "G": [], "Y": [], "R": []}
+    qs = [("V", "S") if o["q"] == "VS" else (o["q"],) for o in ops]
+    where = [""] * m
+    for k in range(m):
+        if left[k] == 0:
+            for q in qs[k]:
+                ready[q].append(k)
+    free = {q: 0.0 for q in ready}
+    end = [0.0] * m
+    order = []
+    while len(order) < m:
+        best = None
+        for q, rs in ready.items():
+            if not rs:
+                continue
+            f = free[q]
+            s0 = min([ready_at[k] for k in rs])
+            s0 = (f if f > s0 else s0) + look
+            k, ek = -1, 0.0
+            for j in rs:
+                if ready_at[j] <= s0 and (k < 0 or eff[j] > ek):
+                    if q == "V" and len(qs[j]) == 2 and free["S"] < max(f, ready_at[j]) + lag:
+                        continue
+                    k, ek = j, eff[j]
+            if k < 0:
+                continue
+            s = f if f > ready_at[k] else ready_at[k]
+            if best is None or s < best[0]:
+                best = (s, k, q)
+        s, k, q = best
+        o = ops[k]
+        where[k] = q
+        for q2 in qs[k]:
+            ready[q2].remove(k)
+        free[q] = 0.0 if q == "R" else s + cost[k]
+        end[k] = s + cost[k] + o["wake"]
+        order.append(k)
+        for j in succ[k]:
+            w = ops[j]["deps"][k]
+            r = end[k] + 0.08 if w == 2 or (w == 1 and (q != "P" or ops[j]["q"] != "P")) else s
+            if r > ready_at[j]:
+                ready_at[j] = r
+            left[j] -= 1
+            if left[j] == 0:
+                for q2 in qs[j]:
+                    ready[q2].append(j)
+    return order, max(end), where
+
+
+def find_order(ops, tries=600):
+    labels = sorted(set(o["label"] for o in ops))
+    rng = np.random.default_rng(7)
+
+    def total(b, lk, lg):
+        return sum(schedule(ops, b, ga, lk, lg)[1] for ga in (1.3, 1.8))
+    cur = (dict(START), 0.03, 2.4)
+    val = best = total(*cur)
+    top = cur
+    for i in range(tries):
+        b, lk, lg = dict(cur[0]), cur[1], cur[2]
+        for _ in range(int(rng.integers(1, 3))):
+            lb = labels[int(rng.integers(0, len(labels)))]
+            b[lb] = float(rng.uniform(-40.0, 40.0)) if rng.random() < 0.5 else b.get(lb, 0.0) + float(rng.normal(0.0, 6.0))
+        if rng.random() < 0.1:
+            lk = float(rng.uniform(0.0, 0.8))
+        if rng.random() < 0.1:
+            lg = float(rng.uniform(-1.0, 4.0))
+        v = total(b, lk, lg)
+        if v <= val + rng.exponential(0.5) * (1.0 - i / tries):
+            val, cur = v, (b, lk, lg)
+            if v < best:
+                best, top = v, cur
+    FOUND["best"], FOUND["top"] = best, top
+    return schedule(ops, top[0], GA, top[1], top[2])
+
+
+def emit(g, sem, ops, sent):
+    if "order" not in FOUND:
+        FOUND["order"], FOUND["span"], FOUND["where"] = find_order(ops)
+    where = FOUND["where"]
+    eng = {"V": g.vector, "S": g.scalar, "P": g.tensor, "G": g, "Y": g.sync}
+    count = {}
+    at = {}
+    known = {q: {} for q in eng}
+    snap = {}
+    for k in FOUND["order"]:
+        o = ops[k]
+        q = where[k]
+        if q == "R":
+            at[k] = (o["sem"], o["inc"])
+            continue
+        need = {}
+        for a in o["deps"]:
+            w = o["deps"][a]
+            if w == 2 or (w == 1 and (q != "P" or where[a] != "P")):
+                s, v = at[a]
+                need[s] = max(need.get(s, 0), v)
+        e, kn = eng[q], known[q]
+        for s in need:
+            v = need[s]
+            if kn.get(s, 0) >= v:
+                continue
+            if any(s2 != s and kn.get(s2, 0) < need[s2] and snap.get((s2, need[s2]), {}).get(s, 0) >= v for s2 in need):
+                continue
+            e.wait_ge(sem[s], v)
+            kn[s] = v
+            for s3, v3 in snap.get((s, v), {}).items():
+                if kn.get(s3, 0) < v3:
+                    kn[s3] = v3
+        for s in need:
+            if kn.get(s, 0) < need[s]:
+                e.wait_ge(sem[s], need[s])
+                kn[s] = need[s]
+        for c in o["calls"]:
+            ins = (c["VS".index(q)] if o["q"] == "VS" else c)(e)
+            s = q if o["sem"] is None else o["sem"]
+            if o["inc"]:
+                count[s] = count.get(s, 0) + o["inc"]
+                ins.then_inc(sem[s], o["inc"])
+        if o["inc"]:
+            at[k] = (s, count[s])
+            snap[at[k]] = dict(kn)
+        else:
+            at[k] = (o["sem"], sent[o["sem"]])
+    for s in list(count) + list(sent):
+        v = sent[s] if s in sent else count[s]
+        if known["Y"].get(s, 0) < v:
+            eng["Y"].wait_ge(sem[s], v)
+            known["Y"][s] = v

@@ -3,14 +3,11 @@ from concourse.mybir import AluOpType as A, ActivationFunctionType as F
 
 RO, CAP = 5, 64
 BIG = float(2 ** 23)
-CH = 4
-CL = 256 // CH
-SPATH = {"1": (3,), "2": (3,)}
-UPD = {1: (0, 1, 2), 2: (0, 1, 2, 3), 3: (0, 1)}
-SLOT = {}
-for _d in UPD:
-    for _t in UPD[_d]:
-        SLOT[(_d, _t)] = len(SLOT)
+HUGE = float(2 ** 30)
+ROUND = 1.5 * 2 ** 34
+PAD = 256 + CAP
+OPT = {"far": (64, 64, 64, 32, 32), "cand": (32,) * 8, "spath": (0, 4), "spath0": (0, 1, 4, 5), "relu2": (), "tail": 1, "ns": 3, "neq": "P", "kd": "P",
+       "vf": 0.04, "sf": 0.07, "pe": 0.6e-3, "wake": 0.16, "look": 0.2, "lag": 0.7, "tries": 2000, "seed": 1, "noise": 0.4, "heat": 1.0}
 
 SCRATCH = {}
 
@@ -20,55 +17,54 @@ def _b(names, cols, dtype="float32", where="sbuf"):
         SCRATCH[nm] = (where, [128, cols], dtype)
 
 
-_b("K1 K2 DD CC WW NN UU DF", 512, "float32", "psum")
-_b("morS", 7168, "bfloat16")
-_b("meaS neq oneb m16", 1024, "bfloat16")
+_b("K1 K2 CC WW DD DF NN HI", 512, "float32", "psum")
+_b("morS meaQ", 3072, "bfloat16")
+_b("meaS neq m16 dd2 aa2 X2 Y2", 1024, "bfloat16")
+_b("oneb", 512, "bfloat16")
+_b("meaT", 1024 + CAP, "bfloat16")
 _b("basI derI", 1024, "int32")
 _b("useI", 512, "int32")
-_b("basF derF Tt lane nbr", 1024)
+PW = 1024
+_b("Pt", PW)
+_b("lane nbr ydS", 1024)
+_b("nbT", 1024 + CAP)
 _b("useF", 512)
-_b("meaQ", 3072, "bfloat16")
-_b("useQ", 1536)
-_b("TQ", 3072)
-_b("lu lt", 256 * len(SLOT))
-_b("UN TN", 1024)
+_b("useQ", 512 * RO)
+_b("PQ", PW * RO)
 _b("mvr", 16384, "bfloat16")
 _b("D16", 1024, "uint16")
 _b("cl of", 80, "uint16")
-_b("XX Y0 Y1 dd1 dd2 aa1 aa2", 4096, "bfloat16")
-_b("cU1 cU2 EU1 EU2", 256, "uint16")
-_b("cF1 cF2 SS1 SS2 EP1 EP2 val up p1 p2 p3 n4 mbig bigs", 256)
-_b("ZB1 ZB2 HH1 HH2 LT1 LT2 LZ LB one If nIf o16 hold", 128)
-_b("mu", 64, "uint16")
-_b("qi", 256, "int32")
-_b("eq ad aE1 aE2 cum zz ad1 got d1 old ge ab junk", 256, "bfloat16")
-_b("Ib nIb IB I14 nI14 tmb bo nbo tri k15", 128, "bfloat16")
-_b("W8 w8t tm8", 8, "bfloat16")
-_b("w64 t64 t65", 64, "bfloat16")
-_b("e15 mk8", 64)
-_b("RR rr0", 16)
-_b("ik8 il8", 64, "int32")
+_b("XD YD XL YL dd1 aa1", 4096, "bfloat16")
+_b("cU1 EU1", 256, "uint16")
+_b("cU2 EU2 mu", 64, "uint16")
+_b("sel", 8, "uint16")
+_b("cF1 SS1 EP1 val xm dec mk8 mbig", 256)
+_b("hi", 32)
+_b("cA EE", PAD)
+_b("cF2 nb2 EP2 E2 e15", 64)
+_b("LZ LB", 512)
+_b("SS2 ZB1 ZB2 LT1 LT2 one If nIf o16 hold", 128)
+_b("qi ik8", 256, "int32")
+_b("qa qc qd s16 t12 c97 c1", 80, "int32")
+_b("eq aE1 d1 old ab", 256, "bfloat16")
+_b("ad got cum", PAD, "bfloat16")
+_b("le lc mseg", 2 * PAD, "bfloat16")
+_b("junk", 4 * PAD, "bfloat16")
+_b("ad2 aE2 got2 mv2 w64 t65", 64, "bfloat16")
+_b("Ib nIb IB IH nIH nH no16 tmb bo nbo tri k15", 128, "bfloat16")
+_b("W8 nW8 w8t", 8, "bfloat16")
+_b("RR", 16)
 _b("km", 260)
-_b("ikm ilm", 260, "int32")
-_b("nm bia", 8)
-_b("cnt", 1)
-_b("pw", 1)
+_b("ikm", 260, "int32")
+_b("nm b8 sc cnt", 8)
 
 QS = ("V", "S", "P", "G")
-SEMAPHORES = list(QS) + ["ld%d" % i for i in range(6)] + ["mc%d" % t for t in range(RO)] + ["st", "sM", "sU", "sT", "sR"]
-for _d in UPD:
-    SEMAPHORES += ["aM%d" % _d, "aU%d" % _d, "aT%d" % _d]
-    for _t in UPD[_d]:
-        SEMAPHORES += ["au%d%d" % (_d, _t), "at%d%d" % (_d, _t)]
+SEMAPHORES = list(QS) + ["ld%d" % i for i in range(5)] + ["st"]
+for _n in ["M%d" % d for d in (1, 2, 3)] + ["U%d" % t for t in range(RO)] + ["P%d" % t for t in range(RO)]:
+    SEMAPHORES += ["a" + _n, "s" + _n]
 
-CY = 1.04e-3
-GA = 1.56
-START = {"keys2": -21, "scanL1": -50, "D16": -33, "gsel": 62, "act": 28, "cF1": 3, "p1": -14, "gapL2": 13, "delta": 23, "min2": 34, "abs1": 22, "ad1": 34,
-         "useQ": 9, "old": 22, "out": -16, "diff": -36, "arrive": -18, "D16n": 33, "cF2": -8, "L1": 28, "E1": -8, "places": 13, "pe": 35, "cU1": 12, "TQ": 26,
-         "count": 35, "dmo": 28, "scand2": -22, "D": -26, "load": -10, "scanL2": 9, "tt": 4, "copy": 15, "T": -21, "E2": -39, "gapL1": 34, "keys1": 14, "": 32,
-         "send": 31, "mvr": -16, "up": 18, "cum": 26, "basF": -14, "scand1": 29, "L2": 1, "UN": -2, "g": -18, "T0": -22, "gapD": 6, "derF0": -55, "TN": 48,
-         "lists": -20, "eq": -2, "useF": 26, "kd": -16, "p2": 27, "cU2": -23, "ts": 36, "neq": -62, "cand1": 8, "scanD": -21, "val": 6, "cand2": -7, "min1": -5,
-         "abs2": -25, "got": -1}
+CY, WAKE = 0.9e-3, 0.08
+GA, SC = 1.4, 3.5
 FOUND = {}
 
 
@@ -80,7 +76,7 @@ def rank_program(g, core, T, topo):
     sm = T.sem
     ops, lastw, readers = [], {}, {}
 
-    def op(q, cost, calls, R=(), W=(), sem=None, inc=1, wake=0.0, label="", gat=0.0):
+    def op(q, cost, calls, R=(), W=(), sem=None, inc=1, wake=0.0, label="", gat=0.0, more=0.0):
         k = len(ops)
         deps = {}
 
@@ -92,7 +88,7 @@ def rank_program(g, core, T, topo):
                 dep(a, 1 if r[0] == "!" and q == "P" and ops[a]["q"] == "P" else 2)
             if r[0] == "!":
                 for a in readers.get(r, ()):
-                    if ops[a]["q"] != q:
+                    if ops[a]["q"] != q or q == "VS":
                         dep(a, 1)
         for w in W:
             for a in ([lastw[w]] if w in lastw else []) + readers.get(w, []):
@@ -102,19 +98,25 @@ def rank_program(g, core, T, topo):
         for w in W:
             lastw[w] = k
             readers[w] = []
-        ops.append({"q": q, "cost": cost, "gat": gat, "calls": calls, "deps": deps, "sem": sem, "inc": inc, "wake": wake, "label": label})
+        ops.append({"q": q, "cost": cost, "gat": gat, "more": more, "calls": calls, "deps": deps, "sem": sem, "inc": inc, "wake": wake, "label": label})
         return k
 
     def V(c, call, R, W, f=1.0, label=""):
-        op("V", 0.06 + max(64.0, c * f) * CY, [call], R, W, label=label, gat=c * CY if f == GA else 0.0)
+        op("V", OPT["vf"] + max(64.0, c * f) * CY, [call], R, W, label=label, gat=c * CY if f == GA else 0.0)
 
     def S(c, call, R, W, f=1.0, label=""):
-        op("S", 0.09 + c * f * CY, [call], R, W, label=label, gat=c * CY if f == GA else 0.0)
+        op("S", OPT["sf"] + c * f * CY, [call], R, W, label=label, gat=c * CY if f == GA else 0.0)
 
     def P(c, mms, R, W, label="pe"):
         def call(m):
             return lambda e: e.matmul(m[0], m[1], m[2], m[3], m[4])
-        op("P", 0.02 + c * 0.85e-3, [call(m) for m in mms], R, W, label=label)
+        per = max(1, len(mms) * 512 // max(c, 512))
+        for i in range(0, len(mms), per):
+            part = mms[i:i + per]
+            op("P", len(part) * (0.005 + c * OPT["pe"] / len(mms)), [call(m) for m in part], R, W, label=label)
+
+    def halves(out, w, x, start, stop):
+        return [(out[:, 0:128], w, x[:, 0:128], start, False), (out[:, 128:256], w, x[:, 128:256], False, stop)]
 
     def G(c, call, R, W, label="g"):
         op("G", 0.2 + 2 * c * CY, [call], R, W, label=label)
@@ -125,8 +127,17 @@ def rank_program(g, core, T, topo):
     def gcopy(out, in_, R, W, c, label):
         sel(out, in_, [[0, c]], A.is_ge, 0, 0, R, W, c, label)
 
-    def ts(out, in0, s1, op0, R, W, c, f=1.0, label="ts"):
-        V(c, lambda e: e.tensor_scalar(out, in0, s1, None, op0), R, W, f, label)
+    def iota(out, pattern, base, cm, W, c):
+        if out.dtype == T.qi.dtype:
+            G(c, lambda e: e.iota(out, pattern, base, cm), [], W)
+        else:
+            G(c, lambda e: e.iota(out, pattern, base, cm, allow_small_or_imprecise_dtypes=True), [], W)
+
+    def ts(out, in0, s1, op0, R, W, c, f=1.0, label="ts", s2=None, op1=None):
+        if op1 is None:
+            V(c, lambda e: e.tensor_scalar(out, in0, s1, None, op0), R, W, f, label)
+        else:
+            V(c, lambda e: e.tensor_scalar(out, in0, s1, s2, op0, op1), R, W, f, label)
 
     def tt(out, a, b, o, R, W, c, f=2.0, label="tt"):
         V(c, lambda e: e.tensor_tensor(out, a, b, o), R, W, f, label)
@@ -134,438 +145,482 @@ def rank_program(g, core, T, topo):
     def tc(out, a, R, W, c, f=1.0, label="tc"):
         V(c, lambda e: e.tensor_copy(out, a), R, W, f, label)
 
+    def fill(out, x, W, c):
+        V(c, lambda e: e.memset(out, x), [], W, label="fill")
+
     def scan(out, d0, d1, o0, o1, R, W, c, f, label):
         V(c, lambda e: e.tensor_tensor_scan(out, d0, d1, 0.0, o0, o1), R, W, f, label)
 
     def act(out, in_, R, W, c, func=F.Copy, scale=1.0, f=1.0, label="act"):
         S(c, lambda e: e.activation(out, in_, func, scale=scale), R, W, f, label)
 
-    def both(out, in_, R, W, c, label):
-        op("VS", 0.08 + c * GA * CY, [(lambda e: e.tensor_copy(out, in_), lambda e: e.activation(out, in_, F.Copy))], R, W, label=label, gat=c * CY)
+    def both(out, in_, R, W, c, label, f=GA):
+        cv, cs = OPT["vf"] + max(64.0, c * f) * CY, OPT["sf"] + c * max(f, 1.0) * CY
+        op("VS", cv, [(lambda e: e.tensor_copy(out, in_), lambda e: e.activation(out, in_, F.Copy))], R, W, label=label, gat=c * CY if f == GA else 0.0, more=cs - cv)
+
+    def store(out, in_, R, us):
+        op("Y", 0.1, [lambda e: e.dma_start(out, in_)], R, [], sem="st", inc=16, wake=us, label="out")
 
     def load(qn, i, out, in_, W, us):
         op(qn, 0.1, [lambda e: e.dma_start(out, in_)], (), W, sem="ld%d" % i, inc=16, wake=us, label="load")
-    load("Y", 0, T.basI[:], T.bas[:], ["basI"], 3.5)
+    load("Y", 0, T.basI[:], T.bas[:], ["basI"], 3.0)
     load("S", 1, T.meaS[:], T.mea[:], ["meaS"], 3.5)
-    load("Y", 2, T.useI[:], T.use[:], ["useI"], 4.0)
-    load("Y", 3, T.derI[:], T.der[:], ["derI"], 5.5)
-    load("S", 4, T.morS[:, 0:3072], T.mor[:], ["mor"], 8.0)
-    load("Y", 5, T.morS[:, 4096:7168], T.mor[:], ["morc"], 10.0)
+    load("S", 2, T.useI[:], T.use[:], ["useI"], 4.5)
+    load("Y", 3, T.derI[:], T.der[:], ["derI"], 6.0)
+    load("Y", 4, T.morS[:], T.mor[:], ["mor"], 8.0)
+    for k in range(1, 5):
+        ops[k]["deps"][k - 1] = 0
 
-    V(128, lambda e: e.memset(T.one[:], 1.0), [], ["one"])
-    V(512, lambda e: e.memset(T.oneb[:], 1.0), [], ["oneb"])
-    V(256, lambda e: e.memset(T.bigs[:], 2.0 * BIG), [], ["bigs"])
+    fill(T.one[:], 1.0, ["one"], 128)
+    fill(T.oneb[:], 1.0, ["oneb"], 512)
     sel(T.e15[:], T.one[:, 0:64], [[-16, 8], [0, 8]], A.is_equal, -15, 1, ["one"], ["e15"], 64)
-    G(64, lambda e: e.iota(T.ik8[:], [[0, 8], [-1, 8]], 128, 1), [], ["ik8"])
-    sel(T.rr0[:], T.one[:, 0:16], [[-8, 16]], A.is_ge, 0, 1, ["one"], ["rr0"], 16)
-    sel(T.RR[:], T.rr0[:], [[8, 16]], A.is_ge, 7, -1, ["rr0"], ["RR"], 16)
-    ts(T.il8[:], T.ik8[:], 7, A.bitwise_and, ["ik8"], ["il8"], 64)
-    ts(T.mk8[:], T.il8[:], 0.0, A.is_equal, ["il8"], ["mk8"], 64)
+    iota(T.ik8[:], [[0, 32], [-1, 8]], 128, 1, ["ik8"], 256)
+    sel(T.RR[:], T.one[:, 0:16], [[-8, 16]], A.is_ge, 0, 1, ["one"], ["RR"], 16)
+    sel(T.RR[:], T.RR[:], [[8, 16]], A.is_ge, 7, -1, ["RR"], ["RR"], 16)
+    ts(T.ik8[:], T.ik8[:], 7, A.bitwise_and, ["ik8"], ["ik8"], 256)
+    ts(T.mk8[:], T.ik8[:], 0.0, A.is_equal, ["ik8"], ["mk8"], 256)
     sel(T.If[:], T.one[:], [[-1, 128]], A.is_equal, 0, 1, ["one"], ["If"], 128)
-    sel(T.tm8[:], T.oneb[:, 0:8], [[-16, 8]], A.is_ge, 0, 1, ["oneb"], ["tm8"], 8)
-    sel(T.w8t[:], T.tm8[:], [[16, 8]], A.is_ge, 15, -1, ["tm8"], ["w8t"], 8)
+    sel(T.w8t[:], T.oneb[:, 0:8], [[-16, 8]], A.is_ge, 0, 1, ["oneb"], ["w8t"], 8)
+    sel(T.w8t[:], T.w8t[:], [[16, 8]], A.is_ge, 15, -1, ["w8t"], ["w8t"], 8)
     act(T.W8[:], T.w8t[:], ["w8t"], ["W8"], 8, scale=2048.0)
-    for nm_, sc in (("Ib", 1.0), ("IB", BIG), ("nIb", -1.0), ("nIf", -1.0), ("I14", 16384.0), ("nI14", -32768.0)):
-        act(T[nm_][:], T.If[:], ["If"], [nm_], 128, scale=sc)
+    act(T.b8[:], T.w8t[:], ["w8t"], ["b8"], 8)
+    for nm_, sc_ in (("Ib", 1.0), ("IB", BIG), ("nIb", -1.0), ("nIf", -1.0), ("IH", HUGE), ("nIH", -HUGE)):
+        act(T[nm_][:], T.If[:], ["If"], [nm_], 128, scale=sc_)
     act(T.o16[:], T.one[:], ["one"], ["o16"], 128, scale=1.0 / 16)
-    sel(T.mbig[:], T.bigs[:], [[0, 16], [1, 16]], A.is_equal, 0, 0, ["bigs"], ["mbig"], 256)
-    sel(T.hold[:], T.one[:], [[0, 16], [1, 8]], A.not_equal, 0, 0, ["one"], ["hold"], 128)
-    sel(T.m16[:], T.oneb[:], [[0, 64], [1, 16]], A.not_equal, 0, 0, ["oneb"], ["m16"], 1024)
-    V(128, lambda e: e.memset(T.ZB1[:], 0.0), [], ["ZB1"])
-    V(128, lambda e: e.memset(T.ZB2[:], 0.0), [], ["ZB2"])
+    act(T.no16[:], T.one[:], ["one"], ["no16"], 128, scale=-1.0 / 16)
+    act(T.nH[:], T.one[:], ["one"], ["nH"], 128, scale=-HUGE)
+    NS = OPT["ns"]
+    NV = 4 - NS
+    for nm_, x, y, first, c in (("mbig", -2.0 * BIG, 2.0 * BIG, T.mbig[:, 0::16], 256), ("m16", 1.0, 0.0, T.m16[:, 0::16], 512), ("hold", 1.0, 0.0, T.hold[:, 0::8], 128),
+                                ("mseg", 1.0, 0.0, T.mseg[:, 0::PAD], PAD)):
+        fill(T[nm_][:], x, [nm_], c)
+        fill(first, y, [nm_], 64)
+    fill(T.ZB1[:], 0.0, ["ZB1"], 128)
+    fill(T.ZB2[:], 0.0, ["ZB2"], 128)
+    for nm_, a in (("cA", 256), ("EE", 256), ("ad", 256), ("got", 256), ("meaT", 1024), ("nbT", 1024)):
+        fill(T[nm_][:, a:a + CAP], 0.0, [nm_ + "pad"], CAP)
     qi = [T.qi[:, 16 * i:16 * i + 16] for i in range(16)]
-    G(16, lambda e: e.iota(qi[0], [[0, 16]], 0, 1), [], ["pi"])
+    pw = T.sc[:, 0:1]
+    iota(qi[0], [[0, 16]], 0, 1, ["pi"], 16)
     ts(qi[1], qi[0], 15, A.bitwise_and, ["pi"], ["pj"], 16)
-    ts(qi[2], qi[1], 12.0, A.mult, ["pj"], ["pk"], 16)
-    G(16, lambda e: e.iota(qi[3], [[192, 16]], 0, 0), [], ["s12"])
-    tt(qi[4], qi[2], qi[3], A.add, ["pk", "s12"], ["t12"], 16)
-    ts(T.pw[:], T.qi[:, 16:17], 1.0, A.add, ["pj"], ["pw"], 1)
-    sel(T.t64[:], T.oneb[:, 0:64], [[-16, 8], [0, 8]], A.is_ge, 0, 1, ["oneb"], ["t64"], 64)
-    sel(T.t65[:], T.t64[:], [[16, 8], [0, 8]], A.is_ge, 15, -1, ["t64"], ["t65"], 64)
-    ts(T.w64[:], T.t65[:], T.pw[:, 0:1], A.mult, ["t65", "pw"], ["w64"], 64)
+    ts(pw, T.qi[:, 16:17], 1.0, A.add, ["pj"], ["pw"], 1)
+    iota(T.s16[:], [[0, 5], [16, 16]], -1, 0, ["s16"], 80)
+    ts(T.t12[:], T.s16[:], pw, A.add, ["pw", "s16"], ["t12"], 80, s2=12.0, op1=A.mult)
+    ts(T.sc[:, 4:8], T.s16[:, 0:4], pw, A.add, ["pw", "s16"], ["sc"], 4, s2=0.5, op1=A.add)
+    iota(T.c97[:], [[97, 5], [0, 16]], 0, 0, ["c97"], 80)
+    iota(T.c1[:], [[1, 5], [0, 16]], 0, 0, ["c1"], 80)
+    sel(T.t65[:], T.oneb[:, 0:64], [[-16, 8], [0, 8]], A.is_ge, 0, 1, ["oneb"], ["t65"], 64)
+    sel(T.t65[:], T.t65[:], [[16, 8], [0, 8]], A.is_ge, 15, -1, ["t65"], ["t65"], 64)
+    ts(T.w64[:], T.t65[:], pw, A.mult, ["t65", "pw"], ["w64"], 64)
     sel(T.tmb[:], T.oneb[:, 0:128], [[-16, 8], [0, 16]], A.is_ge, 0, 1, ["oneb"], ["tmb"], 128)
     sel(T.bo[:], T.tmb[:], [[16, 8], [0, 16]], A.is_ge, 15, -1, ["tmb"], ["bo"], 128)
     act(T.nbo[:], T.bo[:], ["bo"], ["nbo"], 128, scale=-1.0)
+    act(T.nW8[:], T.w8t[:], ["w8t"], ["nW8"], 8, scale=-2048.0)
     sel(T.tmb[:], T.bo[:], [[1, 128]], A.is_ge, 0, -1, ["bo"], ["tmb"], 128)
     act(T.tri[:], T.tmb[:], ["tmb"], ["tri"], 128, scale=8192.0)
     sel(T.tmb[:], T.oneb[:, 0:128], [[0, 8], [1, 16]], A.is_equal, -15, 0, ["oneb"], ["tmb"], 128)
-    act(T.k15[:], T.tmb[:], ["tmb"], ["k15"], 128, scale=8192.0)
-    G(1024, lambda e: e.iota(T.lane[:], [[1, 1024]], 0, 0, allow_small_or_imprecise_dtypes=True), [], ["lane"])
-    G(1024, lambda e: e.iota(T.nbr[:], [[2, 512], [-1, 2]], 1, 0, allow_small_or_imprecise_dtypes=True), [], ["nbr"])
-    G(260, lambda e: e.iota(T.ikm[:], [[1, 260]], 128, -1), [], ["ikm"])
-    ts(T.ilm[:], T.ikm[:], 15, A.bitwise_and, ["ikm"], ["ilm"], 260)
-    ts(T.km[:], T.ilm[:], 0.0, A.is_equal, ["ilm"], ["km"], 260)
-    V(1, lambda e: e.memset(T.nm[:, 0:1], 0.0), [], ["nm0"])
-    V(1, lambda e: e.memset(T.bia[:, 0:1], 4096.0), [], ["bia"])
-
-    def plus4096(out, in_, R, W, c, label):
-        S(c, lambda e: e.activation(out, in_, F.Identity, bias=T.bia[:, 0:1]), R + ["bia"], W, 1.0, label)
+    ts(T.k15[:], T.tmb[:], 8192.0, A.mult, ["tmb"], ["k15"], 128, 0.5, s2=-4096.0, op1=A.add)
+    for tau in range(4):
+        iota(T.lane[:, 256 * tau:256 * tau + 256], [[4, 256]], tau, 0, ["lane%d" % tau], 256)
+    iota(T.nbr[:], [[2, 512], [-1, 2]], 1, 0, ["nbr"], 1024)
+    iota(T.ikm[:], [[1, 260]], 128, -1, ["ikm"], 260)
+    ts(T.ikm[:], T.ikm[:], 15, A.bitwise_and, ["ikm"], ["ikm"], 260)
+    ts(T.km[:], T.ikm[:], 0.0, A.is_equal, ["ikm"], ["km"], 260)
+    fill(T.nm[:, 0:1], 0.0, ["nm0"], 1)
 
     for tau in range(4):
-        tc(T.basF[:, tau::4], T.basI[:, tau::4], ["basI"], ["basF%d" % tau], 256, label="basF")
+        ts(T.nbT[:, 256 * tau:256 * tau + 256], T.basI[:, tau::4], -1.0, A.mult, ["basI"], ["nbT%d" % tau], 256, label="nbT")
     tc(T.useF[:], T.useI[:], ["useI"], ["useF"], 512, label="useF")
-    derall = ["derF%d" % x for x in range(4)]
     for tau in range(4):
         tc(T.D16[:, 256 * tau:256 * tau + 256], T.derI[:, tau::4], ["derI"], ["D16_%d" % tau], 256, label="D16")
+        gcopy(T.meaT[:, 256 * tau:256 * tau + 256], T.meaS[:, tau::4], ["meaS"], ["meaT%d" % tau], 256, "meaT")
 
-    def mvrep(tau, k, q):
-        o, i_ = T.mvr[:, 4096 * tau + k:4096 * tau + 4096:16], T.meaS[:, tau::4]
-        w = ["mvr%d.%d" % (tau, k)]
-        if q == "V":
-            tc(o, i_, ["meaS"], w, 256, 0.5, "mvr")
-        elif q == "S":
-            act(o, i_, ["meaS"], w, 256, label="mvr")
-        else:
-            gcopy(o, i_, ["meaS"], w, 256, "mvr")
-    for k in range(16):
-        mvrep(0, k, "S" if k % 3 else "V")
-    tt(T.neq[:], T.basI[:], T.derI[:], A.not_equal, ["basI", "derI"], ["neq"], 1024, label="neq")
-    tc(T.derF[:], T.derI[:], ["derI"], derall, 1024, label="derF0")
-    Th = ["Th0", "Th1"]
+    def wide(nm_, tau):
+        return T[nm_][:, 256 * tau:256 * tau + PAD], [nm_ + str(tau), nm_ + (str(tau + 1) if tau < 3 else "pad")]
+
+    def mvrep(tau):
+        for k in range(16):
+            o, i_ = T.mvr[:, 4096 * tau + k:4096 * tau + 4096:16], T.meaS[:, tau::4]
+            if tau:
+                gcopy(o, i_, ["meaS"], ["mvr%d.%d" % (tau, k)], 256, "mvrg")
+            else:
+                both(o, i_, ["meaS"], ["mvr%d.%d" % (tau, k)], 256, "mvr", 0.5)
+    mvrep(0)
+    Ph = ["Ph0", "Ph1"]
     for hf in range(2):
         c0 = slice(512 * hf, 512 * hf + 512)
-        bank = ("NN", "UU")[hf]
-        P(1024, [(T[bank][:], T.tri[:], T.neq[:, c0], True, False), (T[bank][:], T.k15[0:1, :], T.oneb[0:1, 0:512], False, True)],
-          ["tri", "k15", "neq", "oneb"], ["!" + bank])
-        plus4096(T.Tt[:, c0], T.derF[:, c0], derall, ["Th%d" % hf], 512, "")
-        tt(T.Tt[:, c0], T.Tt[:, c0], T[bank][:], A.min, ["Th%d" % hf, "!" + bank], ["Th%d" % hf], 512, 1.0, "T0")
+        bank = ("NN", "DF")[hf]
+        tt(T.neq[:, c0], T.basI[:, c0], T.derI[:, c0], A.not_equal, ["basI", "derI"], ["neq%d" % hf], 512, label="neq")
+        P(1024, [(T[bank][:], T.k15[0:1, :], T.oneb[0:1, 0:512], True, False), (T[bank][:], T.tri[:], T.neq[:, c0], False, True)],
+          ["tri", "k15", "neq%d" % hf, "oneb"], ["!" + bank])
+        tt(T.Pt[:, c0], T.derI[:, c0], T[bank][:], A.min, ["derI", "!" + bank], ["Ph%d" % hf], 512, 1.0, "P0")
 
-    def lists(tau):
-        P(512, [(T.WW[:, 64 * h:64 * h + 64], T.basF[:, 4 * h + tau::8], T.e15[:], True, True) for h in range(2)], ["basF%d" % tau, "e15"], ["!WW"], "lists")
+    def bylane(name, taus, rounds, src, srcR, pick, pickR, cy, bank):
+        w, B, L = len(taus), T[bank], T["L" + name]
+        P(2 * w * cy, [(B[:, 64 * (w * h + j):64 * (w * h + j) + 64], src(tau, h), pick, True, True) for h in range(2) for j, tau in enumerate(taus)],
+          srcR + [pickR], ["!" + bank], name)
         for h in range(2):
-            tt(T.LB[:, h::2], T.WW[:, 64 * h:64 * h + 64], T.mk8[:], A.mult, ["!WW", "mk8"], ["LB%d" % h], 64, 1.0, "lists")
-        P(256, [(T.WW[:, 128:144], T.LB[:], T.RR[:], True, True)], ["LB0", "LB1", "RR"], ["!WW"], "lists")
-        for t in [x for x in range(RO) if x % 4 == tau]:
-            ts(qi[5], T.WW[:, 128:144], float(97 * t), A.add, ["!WW"], ["q5"], 16, label="lists")
-            ts(qi[6], qi[5], 511, A.bitwise_and, ["q5"], ["q6"], 16, label="lists")
-            tc(T.cl[:, 16 * t:16 * t + 16], qi[6], ["q6"], ["cl%d" % t], 16, label="lists")
+            tt(L[:, h:128 * w:2], B[:, 64 * w * h:64 * w * (h + 1)], T.mk8[:, 0:64 * w], A.mult, ["!" + bank, "mk8"], ["L%s%d" % (name, h)], 64 * w, 1.0, name)
+        P(256 * len(rounds), [(B[:, 16 * j:16 * j + 16], L[:, 128 * taus.index(t % 4):128 * taus.index(t % 4) + 128], T.RR[:], True, True) for j, t in enumerate(rounds)],
+          ["L%s0" % name, "L%s1" % name, "RR"], ["!" + bank], name)
+        return B[:, 0:16 * len(rounds)], slice(16 * rounds[0], 16 * rounds[-1] + 16), 16 * len(rounds)
 
-    def places(tau):
-        P(128, [(T.WW[:, 64 * h:64 * h + 64], T.meaS[:, 4 * h + tau::8], T.w64[:], True, True) for h in range(2)], ["meaS", "w64"], ["!WW"], "places")
-        for h in range(2):
-            tt(T.LZ[:, h::2], T.WW[:, 64 * h:64 * h + 64], T.mk8[:], A.mult, ["!WW", "mk8"], ["LZ%d" % h], 64, 1.0, "places")
-        P(256, [(T.WW[:, 128:144], T.LZ[:], T.RR[:], True, True)], ["LZ0", "LZ1", "RR"], ["!WW"], "places")
-        for t in [x for x in range(RO) if x % 4 == tau]:
-            ts(qi[7], T.WW[:, 128:144], float(t), A.add, ["!WW"], ["q7"], 16, label="places")
-            ts(qi[8], qi[7], 7, A.bitwise_and, ["q7"], ["q8"], 16, label="places")
-            tt(qi[9], qi[8], qi[4], A.add, ["q8", "t12"], ["q9"], 16, label="places")
-            tc(T.of[:, 16 * t:16 * t + 16], qi[9], ["q9"], ["of%d" % t], 16, label="places")
+    def lists(taus, rounds, bank):
+        x, c, w = bylane("B", taus, rounds, lambda tau, h: T.nbT[:, 256 * tau + h:256 * tau + 256:2], ["nbT%d" % tau for tau in taus], T.e15[:], "e15", 256, bank)
+        tt(T.qa[:, c], T.c97[:, c], x, A.subtract, ["!" + bank, "c97"], ["qa"], w, 1.0, "B")
+        ts(T.qa[:, c], T.qa[:, c], 511, A.bitwise_and, ["qa"], ["qa"], w, label="B")
+        tc(T.cl[:, c], T.qa[:, c], ["qa"], ["cl%d" % t for t in rounds], w, label="B")
 
-    peers = {d: T.cores[(rank - d) % n] for d in UPD}
-    common = [e for e in topo.engines(core, peers[1]) if all(e in topo.engines(core, p) for p in peers.values())]
-    mask = sum(1 << e for e in common)
-    ne = len(common)
-    sent, sends = {}, {}
+    def places(taus, rounds, bank):
+        x, c, w = bylane("Z", taus, rounds, lambda tau, h: T.meaS[:, 4 * h + tau::8], ["meaS"], T.w64[:], "w64", 64, bank)
+        tt(T.qc[:, c], T.c1[:, c], x, A.add, ["!" + bank, "c1"], ["qc"], w, 1.0, "Z")
+        ts(T.qd[:, c], T.qc[:, c], 7, A.bitwise_and, ["qc"], ["qd"], w, label="Z")
+        tt(T.qc[:, c], T.qd[:, c], T.t12[:, c], A.add, ["qd", "t12"], ["qc"], w, label="Z")
+        tc(T.of[:, c], T.qc[:, c], ["qc"], ["of%d" % t for t in rounds], w, label="Z")
 
-    def send(d, out, in_, asem, lsem, R):
-        rid, pid = topo.addr(peers[d])[:2]
-        sent[lsem] = sent.get(lsem, 0) + ne
-        sends[asem] = len(ops)
-        op("G", 0.4, [lambda e: e.remote_dma(out, in_, sm[asem], sm[lsem], pid, rid, mask)], R, (), sem=lsem, inc=0, wake=4.0, label="send")
+    sent = {}
 
-    def arrive(asem, W, us):
-        k = op("R", us, [], (), W, sem=asem, inc=ne, label="arrive")
-        ops[k]["deps"][sends[asem]] = 0
+    def send(d, buf, in_, name, R, us):
+        to, frm = T.cores[(rank - d) % n], T.cores[(rank + d) % n]
+        rid, pid = topo.addr(to)[:2]
+        mask = topo.mask(core, to)
+        sent["s" + name] = len(topo.engines(core, to))
+        k = op("G", 0.5 if len(sent) > 1 else 3.0, [lambda e: e.remote_dma(buf, in_, sm["a" + name], sm["s" + name], pid, rid, mask)], R, (), sem="s" + name, inc=0, wake=us, label="send")
+        j = op("R", us, [], (), ["Q" + name], sem="a" + name, inc=len(topo.engines(frm, core)), label="arrive")
+        ops[j]["deps"][k] = 0
 
-    lists(0)
-    for d in (1, 2, 3):
-        uq, mq, tq = T.useQ[:, 512 * d - 512:512 * d], T.meaQ[:, 1024 * d - 1024:1024 * d], T.TQ[:, 1024 * d - 1024:1024 * d]
-        send(d, uq, T.useF[:], "aU%d" % d, "sU", ["useF"])
-        send(d, mq, T.meaS[:], "aM%d" % d, "sM", ["meaS"])
-        send(d, tq, T.Tt[:], "aT%d" % d, "sT", Th)
-        arrive("aU%d" % d, ["useQ%d" % d], 6.0)
-        arrive("aM%d" % d, ["meaQ%d" % d], 6.0)
-        arrive("aT%d" % d, ["TQ%d.%d" % (d, x) for x in range(4)], 8.0)
+    def send_use(t):
+        send(1 + t % 3, T.useQ[:, 512 * t:512 * t + 512], T.useF[:], "U%d" % t, ["useF"], 6.0)
 
-    def find(c, t, use, useR, mea, meaR):
-        tau = t % 4
-        K, cU, cF, dd, aa = T["K" + c], T["cU" + c], T["cF" + c], T["dd" + c], T["aa" + c]
-        cl = T.cl[:, 16 * t:16 * t + 16]
-        V(256, lambda e: e.tensor_copy(cU[:], use.indirect(cl)), [useR, "cl%d" % t], ["cU" + c], GA, "cU" + c)
-        S(256, lambda e: e.activation(cF[:], use.indirect(cl), F.Copy), [useR, "cl%d" % t], ["cF" + c], GA, "cF" + c)
-        reps = ["mvr%d.%d" % (tau, k) for k in range(16)]
+    def send_P(t):
+        send(1 + t % 3, T.PQ[:, PW * t:PW * t + PW], T.Pt[:], "P%d" % t, Ph + ["Ppad"], 9.0)
 
-        def gat(a, b, j):
-            return lambda e: e.tensor_tensor(dd[:, a:b], mea.indirect(cU[:, CL * j:CL * (j + 1)]), T.mvr[:, 4096 * tau + a:4096 * tau + b], A.subtract)
-        for j in range(CH):
-            a, b = 16 * CL * j, 16 * CL * (j + 1)
-            dR = "dd%s.%d" % (c, j)
-            if j in SPATH[c]:
-                act(dd[:, a:b], mea.indirect(cU[:, CL * j:CL * (j + 1)]), [meaR, "cU" + c], [dR], b - a, f=GA, label="scand" + c)
-                for a2 in range(a, b, 512):
-                    rep = T.mvr[:, 4096 * tau + a2:4096 * tau + a2 + 512]
-                    P(1024, [(T.CC[:], T.nIb[:], rep, True, False), (T.CC[:], T.Ib[:], dd[:, a2:a2 + 512], False, True)], ["Ib", "nIb", dR] + reps, ["!CC"], "scand" + c)
-                    act(aa[:, a2:a2 + 512], T.CC[:], ["!CC"], ["aa%s.%d" % (c, a2)], 512, F.Abs, label="scand" + c)
-                continue
-            V(b - a, gat(a, b, j), [meaR, "cU" + c] + reps, [dR], GA, "cand" + c)
-            act(aa[:, a:b], dd[:, a:b], [dR], ["aa%s.%d" % (c, x) for x in range(a, b, 512)], b - a, F.Abs, label="abs" + c)
-        if c == "1":
-            tt(T.eq[:], cF[:], T.lane[:, tau::4], A.is_equal, ["cF1", "lane"], ["eq"], 256, label="eq")
-        mm, R, cy = [], ["cF" + c, "If", "W8"] + ["aa%s.%d" % (c, x) for x in range(0, 4096, 512)], 0
-        for h in range(2):
-            o = K[:, 128 * h:128 * h + 128]
-            mm.append((o, cF[:, h::2], T.If[:], True, False))
-            cy += 512
-            if c == "1":
-                mm.append((o, T.eq[:, h::2], T.IB[:], False, False))
-                cy += 128
-            for k in range(16):
-                mm.append((K[:, 128 * h + k:128 * h + 128:16], aa[:, 16 * h + k::32], T.W8[:], False, k == 15))
-                cy += 64
-        if c == "1":
-            R += ["eq", "IB"]
-        P(cy, mm, R, ["!K" + c], "keys" + c)
-        SS, ZB, HH, LT = T["SS" + c], T["ZB" + c], T["HH" + c], T["LT" + c]
-        scan(SS[:], T.mbig[:], K[:, 0:256], A.max, A.min, ["!K" + c, "mbig"], ["SS" + c], 256, 1.0, "min" + c)
-        act(ZB[:, 0::8], SS[:, 15::16], ["SS" + c], ["ZB" + c], 16, label="min" + c)
-        scan(HH[:], T.hold[:], ZB[:], A.mult, A.add, ["ZB" + c, "hold"], ["HH" + c], 128, 1.0, "min" + c)
-        for h in range(2):
-            tt(LT[:, h::2], HH[:, 64 * h:64 * h + 64], T.mk8[:], A.mult, ["HH" + c, "mk8"], ["LT%s.%d" % (c, h)], 64, label="min" + c)
-        P(256, [(K[:, 256:272], LT[:], T.RR[:], True, True)], ["LT%s.0" % c, "LT%s.1" % c, "RR"], ["!K" + c], "keys" + c)
-        mi, mj, m = qi[8 + 2 * int(c)], qi[9 + 2 * int(c)], mu(c, t)
-        tc(mi, K[:, 256:272], ["!K" + c], ["mi" + c], 16, label="min" + c)
-        ts(mj, mi, 1023, A.bitwise_and, ["mi" + c], ["mj" + c], 16, label="min" + c)
-        tc(m[0], mj, ["mj" + c], [m[1]], 16, label="min" + c)
-
-    def mu(c, t):
-        k = 2 * int(c) - 2 + t % 2
-        return T.mu[:, 16 * k:16 * k + 16], "mu%d" % k
+    def send_mea(d):
+        send(d, T.meaQ[:, 1024 * d - 1024:1024 * d], T.meaS[:], "M%d" % d, ["meaS"], 6.0)
 
     flip = [0]
 
-    def far(lst, lstR, window, winR, out, outW, tau, label):
-        y = flip[0] % 2
-        flip[0] += 1
-        X, Y = T.XX, T["Y%d" % y]
-        for j in range(CH):
-            a, b = 16 * CL * j, 16 * CL * (j + 1)
-            both(X[:, a:b], window.indirect(lst[:, CL * j:CL * (j + 1)]), [lstR] + winR, ["X.%d" % j], b - a, label)
-            scan(Y[:, a:b], T.m16[:, 0:b - a], X[:, a:b], A.mult, A.max, ["X.%d" % j, "m16"], ["Y%d.%d" % (y, j)], b - a, 0.5, "scan" + label)
-        P(512, [(T.DF[:, 0:256], T.nIb[:], T.meaS[:, tau::4], True, False), (T.DF[:, 0:256], T.Ib[:], Y[:, 15::16], False, True)],
-          ["nIb", "Ib", "meaS"] + ["Y%d.%d" % (y, j) for j in range(CH)], ["!DF"], "diff")
-        act(out[:], T.DF[:, 0:256], ["!DF"], [outW], 256, F.Abs, label="gap" + label)
+    def cands(c, cuts, spath, mea, meaR, rep, repR):
+        cU, dd, aa = T["cU" + c], T["dd" + c], T["aa" + c]
+        l0 = 0
+        for j, w in enumerate(cuts):
+            a, b, dR, aR = 16 * l0, 16 * (l0 + w), "dd%s.%d" % (c, j), ["aa%s.%d" % (c, x) for x in range(l0 // 16, (l0 + w) // 16)]
+            src = mea.indirect(cU[:, l0:l0 + w])
+            l0 += w
+            if j in spath:
+                flip[0] = 1 - flip[0]
+                bank = ("CC", "WW")[flip[0]]
+                o = T[bank][:, 0:b - a]
+                act(dd[:, a:b], src, [meaR, "cU" + c], [dR], b - a, f=GA, label="scand" + c)
+                P(b - a, [(o, T.nIb[:], rep[:, a:b], True, False)], ["nIb"] + repR, ["!" + bank], "scand" + c)
+                P(b - a, [(o, T.Ib[:], dd[:, a:b], False, True)], ["Ib", dR], ["!" + bank], "scand" + c)
+                act(aa[:, a:b], o, ["!" + bank], aR, b - a, F.Abs, label="scand" + c)
+            else:
+                tt(dd[:, a:b], src, rep[:, a:b], A.subtract, [meaR, "cU" + c] + repR, [dR], b - a, GA, "cand" + c)
+                act(aa[:, a:b], dd[:, a:b], [dR], aR, b - a, F.Abs, label="abs" + c)
+
+    def least(c, bank, p, w, run, hold, holdR):
+        K, SS, ZB, hi = T[bank], T["SS" + c], T["ZB" + c], T.hi[0:p, 16 * int(c) - 16:16 * int(c) - 16 + w // 16]
+        scan(SS[0:p, :], T.mbig[0:p, 0:w], K[0:p, 0:w], A.max, A.min, ["!" + bank, "mbig"], ["SS" + c], w, 1.0, "min" + c)
+        ts(hi, SS[0:p, 15::16], ROUND, A.add, ["SS" + c], ["hi" + c], 16, label="min" + c, s2=ROUND, op1=A.subtract)
+        tt(ZB[0:p, 0::run], SS[0:p, 15::16], hi, A.subtract, ["SS" + c, "hi" + c], ["ZB" + c], 16, label="min" + c)
+        scan(K[0:p, w:w + 128], hold, ZB[0:p, :], A.mult, A.add, ["ZB" + c, holdR], ["!" + bank], 128, 1.0, "min" + c)
+
+    def mu(t):
+        return T.mu[:, 16 * (t % 2):16 * (t % 2) + 16], "mu%d" % (t % 2)
+
+    def own_lists(t):
+        tau = t % 4
+        use, cl, clR = T.useF[:], T.cl[:, 16 * t:16 * t + 16], ["useF", "cl%d" % t]
+        tc(T.cU1[:], use.indirect(cl), clR, ["cU1"], 256, GA, "cU1")
+        both(T.cF1[:], use.indirect(cl), clR, ["cF1"], 256, "cF1")
+        tt(T.eq[:], use.indirect(cl), T.lane[:, 256 * tau:256 * tau + 256], A.is_equal, clR + ["lane%d" % tau], ["eq"], 256, GA, "eq")
 
     def own(t):
-        find("1", t, T.useF[:], "useF", T.meaS[:], "meaS")
+        tau = t % 4
+        cands("1", OPT["cand"], OPT["spath0" if t == 0 else "spath"], T.meaS[:], "meaS", T.mvr[:, 4096 * tau:4096 * tau + 4096], ["mvr%d.%d" % (tau, k) for k in range(16)])
+        K = T.K1
+        P(1280, [(K[:, 128 * h:128 * h + 128], x[:, h::2], y[:], i + h == 0, False) for i, (x, y) in enumerate(((T.cF1, T.If), (T.eq, T.IB))) for h in range(2)],
+          ["cF1", "If", "eq", "IB"], ["!K1"], "keys1")
+        P(2048, [(K[:, 128 * h + k:128 * h + 128:16], T.aa1[:, 16 * h + k::32], T.W8[:], False, h == 1 and k == 15) for h in range(2) for k in range(16)],
+          ["W8"] + ["aa1.%d" % x for x in range(16)], ["!K1"], "keys1")
+        least("1", "K1", 128, 256, 8, T.hold[:], "hold")
+        for h in range(2):
+            tt(T.LT1[:, h::2], K[:, 256 + 64 * h:320 + 64 * h], T.mk8[:, 0:64], A.mult, ["!K1", "mk8"], ["LT1.%d" % h], 64, 1.0, "min1")
+        P(256, [(K[:, 0:16], T.LT1[:], T.RR[:], True, True)], ["LT1.0", "LT1.1", "RR"], ["!K1"], "keys1")
+        tc(mu(t)[0], K[:, 0:16], ["!K1"], [mu(t)[1]], 16, label="min1")
 
     def ask(t):
-        d = 1 + t % 3
-        find("2", t, T.useQ[:, 512 * d - 512:512 * d], "useQ%d" % d, T.meaQ[:, 1024 * d - 1024:1024 * d], "meaQ%d" % d)
+        tau, d, K = t % 4, 1 + t % 3, T.K2
+        sl, mea, mv2 = T.sel[:, 0:4], T.meaQ[:, 1024 * d - 1024:1024 * d], T.mv2[:]
+        tc(T.cU2[:], T.cA[:].indirect(sl), ["cA", "cApad", "sel"], ["cU2"], 64, GA, "cU2")
+        win, wR = wide("meaT", tau)
+        both(mv2, win.indirect(sl), wR + ["sel"], ["mv2"], 64, "mv2")
+        both(T.cF2[:], T.cA[:].indirect(sl), ["cA", "cApad", "sel"], ["cF2"], 64, "cF2")
+        P(512, [(K[0:64, 0:128], T.cF2[:], T.If[:], True, False)], ["cF2", "If"], ["!K2"], "keys2")
+        for h, bank in enumerate(("CC", "WW")):
+            B, c = T[bank], slice(512 * h, 512 * h + 512)
+            both(T.dd2[:, c], mea.indirect(T.cU2[:, 32 * h:32 * h + 32]), ["QM%d" % d, "cU2"], ["dd2.%d" % h], 512, "cand2")
+            P(1024, [(B[:, k::16], T.nIb[:], T.mv2[:, 32 * h:32 * h + 32], k == 0, False) for k in range(16)], ["nIb", "mv2"], ["!" + bank], "cand2")
+            P(512, [(B[:], T.Ib[:], T.dd2[:, c], False, True)], ["Ib", "dd2.%d" % h], ["!" + bank], "cand2")
+            o = [K[32 * h:32 * h + 32, k:128:16] for k in range(16)]
+            if h in OPT["relu2"]:
+                P(512, [(o[k], T.dd2[:, 512 * h + k:512 * h + 512:16], T.nW8[:], False, False) for k in range(16)], ["nW8", "dd2.%d" % h], ["!K2"], "keys2")
+                ts(T.aa2[:, c], B[:], 0.0, A.max, ["!" + bank], ["aa2.%d" % h], 512, label="abs2", s2=2.0, op1=A.mult)
+            else:
+                act(T.aa2[:, c], B[:], ["!" + bank], ["aa2.%d" % h], 512, F.Abs, label="abs2")
+            P(512, [(o[k], T.aa2[:, 512 * h + k:512 * h + 512:16], T.W8[:], False, k == 15) for k in range(16)], ["W8", "aa2.%d" % h], ["!K2"], "keys2")
+        least("2", "K2", 64, 128, 16, T.m16[0:64, 0:128], "m16")
+        tt(T.LT2[0:64, :], K[0:64, 128:256], T.km[0:64, 0:128], A.mult, ["!K2", "km"], ["LT2"], 128, 1.0, "min2")
+        P(256, [(K[:, 0:4], T.LT2[0:64, :], T.b8[0:64, 0:4], True, True)], ["LT2", "b8"], ["!K2"], "keys2")
+        tc(T.mu[:, 32:36], K[:, 0:4], ["!K2"], ["mu2"], 4, label="min2")
 
-    def build(c, t, tab, tabR):
-        tau = t % 4
-        EP, EU = T["EP" + c], T["EU" + c]
-        m = mu(c, t)
-        V(256, lambda e: e.tensor_tensor(EP[:], tab.indirect(m[0]), T.basF[:, tau::4], A.max), tabR + [m[1], "basF%d" % tau], ["EP" + c], GA, "E" + c)
-        tc(EU[:], EP[:], ["EP" + c], ["EU" + c], 256, label="E" + c)
+    def far(nm_, lst, lstR, cuts, tail, mv, mvR, gap, out, sign, stop):
+        X, Y, at = T["X" + nm_], T["Y" + nm_], [sum(cuts[:j]) for j in range(len(cuts) + 1)]
+        for j in range(len(cuts)):
+            a, b = 16 * at[j], 16 * at[j + 1]
+            both(X[:, a:b], T.morS[:].indirect(lst[:, at[j]:at[j + 1]]), [lstR, "mor"], ["X%s.%d" % (nm_, j)], b - a, nm_)
+            scan(Y[:, a:b], T.m16[:, 0:b - a], X[:, a:b], A.mult, A.max, ["X%s.%d" % (nm_, j), "m16"], ["Y%s.%d" % (nm_, j)], b - a, 0.5, "scan" + nm_)
+        parts = [(0, len(cuts) - tail), (len(cuts) - tail, len(cuts))] if tail else [(0, len(cuts))]
+        for i, (j0, j1) in enumerate(parts):
+            a, b, gR = at[j0], at[j1], "gap%s.%d" % (nm_, i)
+            P(b - a, [(T.DF[:, a:b], T.nIb[:], mv[:, a:b], True, False)], ["nIb", mvR] + (["YD.0"] if nm_ == "D" else []), ["!DF"], "diff")
+            P(b - a, [(T.DF[:, a:b], T.Ib[:], Y[:, 16 * a + 15:16 * b:16], False, True)], ["Ib"] + ["Y%s.%d" % (nm_, j) for j in range(j0, j1)], ["!DF"], "diff")
+            act(gap[:, a:b], T.DF[:, a:b], ["!DF"], [gR], b - a, F.Abs, label="gap" + nm_)
+            P(b - a, [(out[:, a:b], T[sign][:], gap[:, a:b], not stop, stop and j1 == len(cuts))], [sign, gR], ["!DD"], "delta")
 
+    def decode(tau):
+        tt(T.dec[:], T.Pt[:, tau:1024:4], T.nbT[:, 256 * tau:256 * tau + 256], A.max, Ph + ["nbT%d" % tau], ["dec"], 256, label="dec")
+        act(T.ydS[:, tau::4], T.dec[:], ["dec"], ["yd%d" % tau], 256, F.Abs, label="dec")
+
+    lists([0], [0], "WW")
+    send_mea(1)
+    send_use(0)
+    send_P(0)
+    own_lists(0)
     own(0)
-    lists(1)
-    places(0)
-    places(1)
-    for k in range(16):
-        mvrep(1, k, "G")
-    ask(0)
-    lists(2)
-    lists(3)
-    places(2)
-    places(3)
-    for tau in (2, 3):
-        for k in range(16):
-            mvrep(tau, k, "G")
+    places([0, 1, 2, 3], [0, 1, 2, 3, 4], "K2")
+    lists([0, 1, 2, 3], [1, 2, 3, 4], "WW")
+    send_mea(2)
+    mvrep(1)
+    send_mea(3)
+    mvrep(2)
+    mvrep(3)
 
     If, nIf, Ib, nIb = T.If[:], T.nIf[:], T.Ib[:], T.nIb[:]
-    D1, D2, N1 = T.DD[:, 0:256], T.DD[:, 256:512], T.NN[:, 0:256]
-    W1, W2, U1, U2 = T.WW[:, 0:256], T.WW[:, 256:512], T.UU[:, 0:256], T.UU[:, 256:512]
-    done = {}
-
-    def taken(dn, x):
-        if (dn, x) in done:
-            return
-        done[(dn, x)] = 1
-        arrive("au%d%d" % (dn, x), ["lu%d%d" % (dn, x)], 5.0)
-        arrive("at%d%d" % (dn, x), ["lt%d%d" % (dn, x)], 5.0)
-        s = 256 * SLOT[(dn, x)]
-        b = 512 * dn - 512 + 37 * x
-        gcopy(T.useQ[:, b:b + 256], T.lu[:, s:s + 256], ["lu%d%d" % (dn, x)], ["useQ%d" % dn], 256, "useQ")
-        gcopy(T.TQ[:, 1024 * dn - 1024 + x % 4:1024 * dn:4], T.lt[:, s:s + 256], ["lt%d%d" % (dn, x)], ["TQ%d.%d" % (dn, x % 4)], 256, "TQ")
+    D1, D2, Lo, Hi = T.DD[:, 0:256], T.DD[:, 256:320], T.NN[:, 0:256], T.HI[:, 0:256]
+    U1, U2, U3 = T.K1[:, 256:512], T.K2[:, 256:512], T.NN[:, 256:512]
+    row = T.oneb[0:1, 0:256]
 
     def rnd(t):
-        tau, d, last = t % 4, 1 + t % 3, t + 1 == RO
+        tau, last = t % 4, t + 1 == RO
         nm, nmR = T.nm[:, t:t + 1], "nm%d" % t
-        derT, basT, derR, mv = T.derF[:, tau::4], T.basF[:, tau::4], "derF%d" % tau, T.meaS[:, tau::4]
-        off = T.of[:, 16 * t:16 * t + 16]
-        if t:
-            op("Y", 0.1, [lambda e: e.dma_start(T.morS[:, 4096:7168], T.morS[:, 0:3072])], ["mor"], ["morc"], sem="mc%d" % t, inc=16, wake=4.5, label="copy")
-        far(T.D16[:, 256 * tau:256 * tau + 256], "D16_%d" % tau, T.morS[:, 0:3072], ["mor"], T.ad, "ad", tau, "D")
-        P(256, [(D1, T.nbo[:], T.ad[:], True, False)], ["nbo", "ad"], ["!DD"], "delta")
-        build("1", t, T.Tt[:], Th)
-        far(T.EU1, "EU1", T.morS[:], ["mor", "morc"], T.aE1, "aE1", tau, "L1")
-        P(256, [(D1, T.bo[:], T.aE1[:], False, True)], ["bo", "aE1"], ["!DD"], "delta")
-        m = mu("1", t)
-        u0 = 37 * t
-        useT = T.useF[:, u0:u0 + 256]
-        S(256, lambda e: e.activation(T.val[:], T.nbr[:].indirect(m[0]), F.Copy), ["nbr", m[1]], ["val"], GA, "val")
-        P(2048, [(U1, If, T.val[:], True, False), (U1, nIf, useT, False, True)], ["If", "nIf", "val", "useF"], ["!UU"], "kd")
-        tt(U1, U1, T.km[:, t:t + 256], A.mult, ["!UU", "km"], ["!UU"], 256, 1.0, "kd")
-        ts(T.ad1[:], D1, nm, A.is_lt, ["!DD", nmR], ["ad1"], 256, label="ad1")
-        tt(T.up[:], U1, T.ad1[:], A.mult, ["!UU", "ad1"], ["up"], 256, 1.0, "up")
-        tt(useT, T.up[:], useT, A.add, ["useF", "up"], ["useF"], 256, label="up")
-        if not last:
-            UN = T.UN[:, 256 * t:256 * t + 256]
-            gcopy(UN, useT, ["useF"], ["UN%d" % t], 256, "UN")
-            for dn in UPD:
-                if t in UPD[dn]:
-                    s = 256 * SLOT[(dn, t)]
-                    send(dn, T.lu[:, s:s + 256], UN, "au%d%d" % (dn, t), "sR", ["UN%d" % t])
-            own(t + 1)
+        nb, nbR, mv = T.nbT[:, 256 * tau:256 * tau + 256], "nbT%d" % tau, T.meaS[:, tau::4]
+        off, sl, got, E = T.of[:, 16 * t:16 * t + 16], T.sel[:, 0:4], T.got[:, 0:256], T.EE[:, 0:256]
+        keep, keepR = (T.ydS[:, tau::4], ["yd%d" % tau]) if last else (T.Pt[:, tau:1024:4], Ph)
+        P(1024, halves(Hi, If, keep, True, False), ["If"] + keepR, ["!HI"], "Hi")
+        if last:
+            P(256, [(Lo, T.nH[0:1, :], row, True, False)], ["nH", "oneb"], ["!NN"], "Hi")
+        elif OPT["neq"] == "P":
+            P(1024, halves(U3, If, nb, True, False), ["If", nbR], ["!NN"], "Hi")
+        far("D", T.D16[:, 256 * tau:256 * tau + 256], "D16_%d" % tau, OPT["far"], 0, mv, "meaS", T.ad, D1, "nbo", False)
+        m = mu(t)
+        tt(T.EP1[:], T.Pt[:, 0:1024].indirect(m[0]), nb, A.max, Ph + [m[1], nbR], ["EP1"], 256, GA, "E1")
+        act(E, T.EP1[:], ["EP1"], ["EE"], 256, F.Abs, label="E1")
+        tc(T.EU1[:], E, ["EE"], ["EU1"], 256, label="E1")
+        useT = T.useF[:, 37 * t:37 * t + 256]
+        if OPT["kd"] == "P":
+            both(T.val[:], T.nbr[:].indirect(m[0]), ["nbr", m[1]], ["val"], 256, "val")
+            P(2048, halves(U1, nIf, useT, True, False) + halves(U1, If, T.val[:], False, True), ["If", "nIf", "val", "useF"], ["!K1"], "kd")
+            tt(U1, U1, T.km[:, t:t + 256], A.mult, ["!K1", "km"], ["!K1"], 256, 1.0, "kd")
         else:
-            op("Y", 0.1, [lambda e: e.dma_start(T.yu[:], T.useF[:])], ["useF"], ["yu"], sem="st", inc=16, wake=4.0, label="out")
-        scan(T.cum[:], T.oneb[:, 0:256], T.ad1[:], A.add, A.subtract, ["oneb", "ad1"], ["cum"], 256, 0.5, "cum")
-        ts(T.zz[:], T.cum[:], float(CAP), A.is_gt, ["cum"], ["zz"], 256, f=0.5, label="cum")
-        P(1024, [(D2, T.I14[:], T.zz[:], True, False), (D2, T.nI14[:], T.ad1[:], False, False), (D2, T.nbo[:], T.ad[:], False, False)],
-          ["I14", "nI14", "nbo", "zz", "ad1", "ad"], ["!DD"], "delta")
-        S(256, lambda e: e.activation(T.old[:], T.morS[:, 0:3072].indirect(off), F.Copy), ["mor", "of%d" % t], ["old"], GA, "old")
-        P(512, [(U2, Ib, mv, True, False), (U2, nIb, T.old[:], False, True)], ["Ib", "nIb", "meaS", "old"], ["!UU"], "dmo")
-        build("2", t, T.TQ[:, 1024 * d - 1024:1024 * d], ["TQ%d.%d" % (d, x) for x in range(4)])
-        far(T.EU2, "EU2", T.morS[:], ["mor", "morc"], T.aE2, "aE2", tau, "L2")
-        P(256, [(D2, T.bo[:], T.aE2[:], False, True)], ["bo", "aE2"], ["!DD"], "delta")
-        ts(T.got[:], D2, nm, A.is_lt, ["!DD", nmR], ["got"], 256, label="got")
-        tt(T.d1[:], U2, T.got[:], A.mult, ["!UU", "got"], ["d1"], 256, 1.0, "got")
-        V(256, lambda e: e.tensor_tensor(T.morS[:, 0:3072].indirect(off), T.d1[:], T.old[:], A.add), ["d1", "old", "of%d" % t], ["mor"], 3.5, "got")
+            tt(T.val[:], T.nbr[:].indirect(m[0]), useT, A.subtract, ["nbr", m[1], "useF"], ["val"], 256, GA, "val")
+            tt(U1, T.val[:], T.km[:, t:t + 256], A.mult, ["val", "km"], ["!K1"], 256, 2.0, "kd")
+        far("L", T.EU1, "EU1", OPT["far"], OPT["tail"], mv, "meaS", T.aE1, D1, "bo", True)
+        both(T.cA[:, 0:256], T.useQ[:, 512 * t:512 * t + 512].indirect(T.cl[:, 16 * t:16 * t + 16]), ["QU%d" % t, "cl%d" % t], ["cA"], 256, "cA")
+        both(T.old[:], T.morS[:].indirect(off), ["mor", "of%d" % t], ["old"], 256, "old")
+        P(512, [(U2, Ib, mv, True, False), (U2, nIb, T.old[:], False, True)], ["Ib", "nIb", "meaS", "old"], ["!K2"], "dmo")
+        ts(got, D1, nm, A.is_lt, ["!DD", nmR], ["got"], 256, label="ad1")
+        scan(T.cum[:], T.oneb[:, 0:PAD], T.got[:], A.add, A.subtract, ["oneb", "got", "gotpad"], ["cum"], PAD, 0.5, "cum")
+        for c in range(NS):
+            S(PAD + 20, lambda e, c=c: e.activation(T.junk[:, PAD * c:PAD * c + PAD], T.cum[:], F.Sign, bias=T.sc[:, 4 + c:5 + c], scale=-1.0, accum_out=T.cnt[:, c:c + 1]),
+              ["cum", "sc"], ["cnt%d" % c], 1.0, "count")
+        if NV:
+            for c in range(NV):
+                ts(T.le[:, PAD * c:PAD * c + PAD], T.cum[:], T.sc[:, 4 + NS + c:5 + NS + c], A.is_lt, ["cum", "sc"], ["le%d" % c], PAD, 0.5, "count", -0.5, A.add)
+            scan(T.lc[:, 0:NV * PAD], T.mseg[:, 0:NV * PAD], T.le[:, 0:NV * PAD], A.mult, A.add, ["mseg"] + ["le%d" % c for c in range(NV)], ["lc"], NV * PAD, 0.5, "count")
+            ts(T.sel[:, NS:4], T.lc[:, PAD - 1:NV * PAD:PAD], PAD / 2.0, A.add, ["lc"], ["selV", "sel"], NV, label="count")
+        ts(T.sel[:, 0:NS], T.cnt[:, 0:NS], float(PAD), A.add, ["cnt%d" % c for c in range(NS)] + (["selV"] if NV else []), ["sel"], NS, label="count", s2=0.5, op1=A.mult)
+        tt(U1, got, U1, A.mult, ["!K1", "got"], ["!K1"], 256, 1.0, "up")
+        tt(useT, useT, U1, A.add, ["useF", "!K1"], ["useF"], 256, 1.0, "up")
         if last:
-            op("Y", 0.1, [lambda e: e.dma_start(T.ym[:], T.morS[:, 0:3072])], ["mor"], ["ym"], sem="st", inc=16, wake=5.0, label="out")
-        tt(T.p1[:], T.EP1[:], T.ad1[:], A.mult, ["EP1", "ad1"], ["p1"], 256, label="p1")
-        P(1024, [(W1, Ib, T.got[:], True, False), (W1, nIb, T.ad1[:], False, True), (W2, Ib, T.oneb[:, 0:256], True, False), (W2, nIb, T.got[:], False, True)],
-          ["Ib", "nIb", "oneb", "got", "ad1"], ["!WW"], "p2")
-        tt(T.p2[:], W1, T.EP2[:], A.mult, ["!WW", "EP2"], ["p2"], 256, 1.0, "p2")
-        tt(T.p3[:], W2, derT, A.mult, ["!WW", derR], ["p3"], 256, 1.0, "p2")
-        P(3072, [(N1, If, T.p1[:], True, False), (N1, If, T.p2[:], False, False), (N1, If, T.p3[:], False, True)], ["If", "p1", "p2", "p3"], ["!NN"], "p2")
-        V(256, lambda e: e.tensor_scalar(T.ge[:], N1, 4096.0, -4096.0, A.is_ge, A.mult), ["!NN"], ["ge"], 1.0, "p2")
-        tt(derT, N1, T.ge[:], A.add, ["!NN", "ge"], [derR], 256, 1.0, "p2")
-        if t == 0:
-            tc(T.D16[:, 0:256], T.derF[:, 0::4], ["derF0"], ["D16_0"], 256, label="D16n")
+            store(T.yu[:], T.useF[:], ["useF"], 3.0)
+        else:
+            send_use(t + 1)
+            own_lists(t + 1)
+        ask(t)
+        if not last:
+            own(t + 1)
+        win, wR = wide("nbT", tau)
+        both(T.nb2[:], win.indirect(sl), wR + ["sel"], ["nb2"], 64, "nb2")
+        both(T.ad2[:], T.ad[:].indirect(sl), ["gapD.0", "adpad", "sel"], ["ad2"], 64, "ad2")
+        P(64, [(D2, T.nbo[:], T.ad2[:], True, False)], ["nbo", "ad2"], ["!DD"], "delta")
+        tt(T.EP2[:], T.PQ[:, PW * t:PW * t + 1024].indirect(T.mu[:, 32:36]), T.nb2[:], A.max, ["QP%d" % t, "mu2", "nb2"], ["EP2"], 64, GA, "E2")
+        act(T.E2[:], T.EP2[:], ["EP2"], ["E2"], 64, F.Abs, label="E2")
+        tc(T.EU2[:], T.E2[:], ["E2"], ["EU2"], 64, label="E2")
+        far("2", T.EU2, "EU2", (32, 32), 0, T.mv2, "mv2", T.aE2, D2, "bo", True)
+        tc(T.EE[:].indirect(sl), T.E2[:], ["E2", "sel", "EEpad"], ["EE"], 64, SC, "EE")
+        if not last:
+            if OPT["neq"] == "P":
+                P(1024, halves(U3, If, E, False, True), ["If", "EE"], ["!NN"], "P")
+                act(T.ab[:], U3, ["!NN"], ["ab"], 256, F.Abs, label="P")
+            else:
+                tt(T.ab[:], E, T.basI[:, tau::4], A.not_equal, ["EE", "basI"], ["ab"], 256, label="P")
+            P(512, [(Lo, T.k15[0:1, :], row, True, False), (Lo, T.nH[0:1, :], row, False, False)], ["k15", "nH", "oneb"], ["!NN"], "P")
+            P(256, [(Lo, T.tri[:], T.ab[:], False, False)], ["tri", "ab"], ["!NN"], "P")
+        ts(T.got2[:], D2, nm, A.is_lt, ["!DD", nmR], ["got2"], 64, label="got")
+        tc(T.got[:].indirect(sl), T.got2[:], ["got2", "sel", "gotpad"], ["got"], 64, SC, "got")
+        tt(T.d1[:], U2, got, A.mult, ["!K2", "got"], ["d1"], 256, 1.0, "got")
+        tt(T.morS[:].indirect(off), T.d1[:], T.old[:], A.add, ["d1", "old", "of%d" % t], ["mor"], 256, SC, "got")
+        P(256 * (1 + last), [(Lo, T.IH[:], got, False, i == last) for i in range(1 + last)], ["IH", "got"], ["!NN"], "P2")
+        P(256, [(Hi, T.nIH[:], got, False, True)], ["nIH", "got"], ["!HI"], "P2")
+        tt(T.xm[:], E, Lo, A.min, ["EE", "!NN"], ["xm"], 256, 1.0, "P2")
+        tt(keep, T.xm[:], Hi, A.max, ["xm", "!HI"], keepR, 256, 1.0, "P2")
         if last:
-            op("Y", 0.1, [lambda e: e.dma_start(T.yd[:], T.derF[:])], derall, ["yd"], sem="st", inc=16, wake=5.0, label="out")
+            store(T.ym[:], T.morS[:], ["mor"], 4.0)
+            store(T.yd[:], T.ydS[:], ["yd%d" % x for x in range(4)], 3.5)
             return
-        tt(T.ab[:], basT, derT, A.not_equal, ["basF%d" % tau, derR], ["ab"], 256, label="T")
-        plus4096(T.n4[:], derT, [derR], ["n4"], 256, "T")
-        P(512, [(N1, T.tri[:], T.ab[:], True, False), (N1, T.k15[0:1, :], T.oneb[0:1, 0:256], False, True)], ["tri", "k15", "oneb", "ab"], ["!NN"], "T")
-        tt(T.Tt[:, tau::4], N1, T.n4[:], A.min, ["!NN", "n4"], Th, 256, 1.0, "T")
-        TN = T.TN[:, 256 * t:256 * t + 256]
-        gcopy(TN, T.Tt[:, tau::4], Th, ["TN%d" % t], 256, "TN")
-        for dn in UPD:
-            if t in UPD[dn]:
-                s = 256 * SLOT[(dn, t)]
-                send(dn, T.lt[:, s:s + 256], TN, "at%d%d" % (dn, t), "sR", ["TN%d" % t])
-        S(256, lambda e: e.activation(T.junk[:], T.got[:], F.Copy, accum_out=T.cnt[:]), ["got"], ["cnt", "junk"], 1.0, "count")
-        P(64, [(T.DF[:, 256:257], T.o16[:], T.cnt[:], True, True)], ["o16", "cnt"], ["!DF"], "count")
-        tc(T.qi[:, 224:225], T.DF[:, 256:257], ["!DF"], ["ai"], 1, label="count")
-        ts(T.qi[:, 240:241], T.qi[:, 224:225], 127, A.bitwise_and, ["ai"], ["aj"], 1, label="count")
-        ts(T.nm[:, t + 1:t + 2], T.qi[:, 240:241], -1.0, A.mult, ["aj"], ["nm%d" % (t + 1)], 1, label="count")
-        dn = 1 + (t + 1) % 3
-        for x in UPD[dn]:
-            if x <= t:
-                taken(dn, x)
-        ask(t + 1)
+        send_P(t + 1)
+        decode(tau)
+        if t == 0:
+            tc(T.D16[:, 0:256], T.ydS[:, 0::4], ["yd0"], ["D16_0"], 256, label="D16n")
+        S(84, lambda e: e.activation(T.aE2[:], T.got2[:], F.Copy, accum_out=T.cnt[:, 4:5]), ["got2"], ["n2", "gap2.0"], 1.0, "margin")
+        P(320, [(T.DD[:, 320:321], T.no16[:], T.cum[:, 255:256], True, False), (T.DD[:, 320:321], T.o16[:], T.cnt[:, 4:5], False, True)],
+          ["o16", "no16", "cum", "n2"], ["!DD"], "margin")
+        ts(T.qi[:, 224:225], T.DD[:, 320:321], 2048.0, A.add, ["!DD"], ["ai"], 1, label="margin")
+        ts(T.qi[:, 240:241], T.qi[:, 224:225], 127, A.bitwise_and, ["ai"], ["aj"], 1, label="margin")
+        ts(T.nm[:, t + 1:t + 2], T.qi[:, 240:241], -1.0, A.mult, ["aj"], ["nm%d" % (t + 1)], 1, label="margin")
 
     for t in range(RO):
         rnd(t)
     emit(g, sm, ops, sent)
 
 
-def schedule(ops, bonus, ga, look, lag):
-    m = len(ops)
-    cost = [o["cost"] + o["gat"] * (ga - GA) for o in ops]
-    succ = [[] for _ in range(m)]
-    for k, o in enumerate(ops):
-        for a in o["deps"]:
-            succ[a].append(k)
-    prio = [0.0] * m
-    for k in range(m - 1, -1, -1):
-        o = ops[k]
-        best = 0.0
-        for s in succ[k]:
-            if prio[s] > best:
-                best = prio[s]
-        prio[k] = best + cost[k] + (0.0 if o["q"] == "R" else o["wake"] + 0.05)
-    eff = [prio[k] + bonus.get(ops[k]["label"], 0.0) for k in range(m)]
-    left = [len(o["deps"]) for o in ops]
-    ready_at = [0.0] * m
-    ready = {"V": [], "S": [], "P": [], "G": [], "Y": [], "R": []}
-    qs = [("V", "S") if o["q"] == "VS" else (o["q"],) for o in ops]
-    where = [""] * m
+def one_pass(cost, more, nxt, qs, due, look, lag):
+    m = len(cost)
+    left = [0] * m
+    for a in range(m):
+        for b, _ in nxt[a]:
+            left[b] += 1
+    at, start, where, order = [0.0] * m, [0.0] * m, [""] * m, []
+    ready = {q: [] for q in "VSPGYR"}
+    free = {q: 0.0 for q in ready}
     for k in range(m):
-        if left[k] == 0:
+        if not left[k]:
             for q in qs[k]:
                 ready[q].append(k)
-    free = {q: 0.0 for q in ready}
-    end = [0.0] * m
-    order = []
+    span = 0.0
     while len(order) < m:
-        best = None
+        bs, bk, bq = 1e9, -1, ""
         for q, rs in ready.items():
             if not rs:
                 continue
             f = free[q]
-            s0 = min([ready_at[k] for k in rs])
+            s0 = min([at[k] for k in rs])
             s0 = (f if f > s0 else s0) + look
-            k, ek = -1, 0.0
+            k, dk = -1, 1e9
             for j in rs:
-                if ready_at[j] <= s0 and (k < 0 or eff[j] > ek):
-                    if q == "V" and len(qs[j]) == 2 and free["S"] < max(f, ready_at[j]) + lag:
+                if at[j] <= s0 and due[j] < dk:
+                    if q == "V" and len(qs[j]) == 2 and free["S"] < max(f, at[j]) + lag[j] * cost[j] - more[j]:
                         continue
-                    k, ek = j, eff[j]
-            if k < 0:
-                continue
-            s = f if f > ready_at[k] else ready_at[k]
-            if best is None or s < best[0]:
-                best = (s, k, q)
-        s, k, q = best
-        o = ops[k]
-        where[k] = q
-        for q2 in qs[k]:
-            ready[q2].remove(k)
-        free[q] = 0.0 if q == "R" else s + cost[k]
-        end[k] = s + cost[k] + o["wake"]
-        order.append(k)
-        for j in succ[k]:
-            w = ops[j]["deps"][k]
-            r = end[k] + 0.08 if w == 2 or (w == 1 and (q != "P" or ops[j]["q"] != "P")) else s
-            if r > ready_at[j]:
-                ready_at[j] = r
-            left[j] -= 1
-            if left[j] == 0:
-                for q2 in qs[j]:
-                    ready[q2].append(j)
-    return order, max(end), where
+                    k, dk = j, due[j]
+            if k >= 0:
+                s = f if f > at[k] else at[k]
+                if s < bs:
+                    bs, bk, bq = s, k, q
+        if bk < 0:
+            lag = [-1e9] * m
+            continue
+        start[bk], where[bk] = bs, bq
+        order.append(bk)
+        for q in qs[bk]:
+            ready[q].remove(bk)
+        e = bs + cost[bk] + (more[bk] if bq == "S" else 0.0)
+        if bq != "R":
+            free[bq] = e
+        if e > span:
+            span = e
+        for b, d in nxt[bk]:
+            if e + d > at[b]:
+                at[b] = e + d
+            left[b] -= 1
+            if not left[b]:
+                for q in qs[b]:
+                    ready[q].append(b)
+    return order, start, where, span
 
 
-def find_order(ops, tries=600):
-    labels = sorted(set(o["label"] for o in ops))
-    rng = np.random.default_rng(7)
+def replay(order, where, cost, more, nxt):
+    at, free, span = [0.0] * len(cost), {q: 0.0 for q in "VSPGYR"}, 0.0
+    for k in order:
+        q = where[k]
+        e = max(at[k], free[q]) + cost[k] + (more[k] if q == "S" else 0.0)
+        if q != "R":
+            free[q] = e
+        span = max(span, e)
+        for b, d in nxt[k]:
+            if e + d > at[b]:
+                at[b] = e + d
+    return span
 
-    def total(b, lk, lg):
-        return sum(schedule(ops, b, ga, lk, lg)[1] for ga in (1.3, 1.8))
-    cur = (dict(START), 0.03, 2.4)
-    val = best = total(*cur)
+
+def find_order(ops):
+    m = len(ops) + 1
+    nxt, prv = [[] for _ in range(m)], [[] for _ in range(m)]
+    for k, o in enumerate(ops):
+        for a, w in o["deps"].items():
+            d = ops[a]["wake"] + OPT["wake"] if w == 2 or (w == 1 and (o["q"] != "P" or ops[a]["q"] != "P")) else 0.0
+            nxt[a].append((k, d))
+            prv[k].append((a, d))
+        if o["wake"]:
+            nxt[k].append((m - 1, o["wake"]))
+            prv[m - 1].append((k, o["wake"]))
+    costs = [[(o["cost"] + o["gat"] * (ga - GA)) * (f if o["q"] in "VSPG" else 1.0) for o in ops] + [0.0] for ga, f in ((GA, 1.0), (1.2, 0.92), (1.8, 1.2))]
+    cost, more = costs[0], [o["more"] for o in ops] + [0.0]
+    qs = [("V", "S") if o["q"] == "VS" else (o["q"],) for o in ops] + [("R",)]
+    due = [0.0] * m
+    for k in range(m - 1, -1, -1):
+        due[k] = min([due[b] - d for b, d in nxt[k]] + [0.0]) - cost[k]
+    FOUND["dbg"] = (due, cost, nxt, ops)
+    rng = np.random.default_rng(OPT["seed"])
+    look, one = OPT["look"], [0.0] * m
+
+    def forward(due, lag):
+        order, start, where, span = one_pass(cost, more, nxt, qs, due, look, lag)
+        return span + sum(replay(order, where, c, more, nxt) for c in costs[1:]), order, start, where, span
+
+    def backward(start, where):
+        ends = [s + c + (x if q == "S" else 0.0) for s, c, x, q in zip(start, cost, more, where)]
+        _, back, _, bspan = one_pass(cost, more, prv, [(q,) for q in where], [-x for x in ends], look, one)
+        return [bspan - b - (e - s) for b, e, s in zip(back, ends, start)]
+    lag = [OPT["lag"]] * m
+    cur = forward(due, lag)
     top = cur
-    for i in range(tries):
-        b, lk, lg = dict(cur[0]), cur[1], cur[2]
-        for _ in range(int(rng.integers(1, 3))):
-            lb = labels[int(rng.integers(0, len(labels)))]
-            b[lb] = float(rng.uniform(-40.0, 40.0)) if rng.random() < 0.5 else b.get(lb, 0.0) + float(rng.normal(0.0, 6.0))
-        if rng.random() < 0.1:
-            lk = float(rng.uniform(0.0, 0.8))
-        if rng.random() < 0.1:
-            lg = float(rng.uniform(-1.0, 4.0))
-        v = total(b, lk, lg)
-        if v <= val + rng.exponential(0.5) * (1.0 - i / tries):
-            val, cur = v, (b, lk, lg)
-            if v < best:
-                best, top = v, cur
-    FOUND["best"], FOUND["top"] = best, top
-    return schedule(ops, top[0], GA, top[1], top[2])
+    for i in range(OPT["tries"]):
+        if i % 8 == 0:
+            d2, l2 = backward(cur[2], cur[3]), lag
+        else:
+            a, x = float(rng.uniform(-5.0, cur[4])), rng.normal(0.0, 1.0, (2, m)).tolist()
+            w, s = float(rng.uniform(3.0, 12.0)), OPT["noise"] * float(rng.uniform(0.3, 2.0))
+            d2 = [d + s * y if a <= t < a + w else d for d, t, y in zip(due, cur[2], x[0])]
+            l2 = [OPT["lag"] + 0.6 * y if a <= t < a + w and y * y > 1.0 else z for z, t, y in zip(lag, cur[2], x[1])]
+        new = forward(d2, l2)
+        if new[0] <= cur[0] + OPT["heat"] * (1.0 - i / OPT["tries"]) or i == 0:
+            cur, due, lag = new, d2, l2
+            if cur[0] < top[0]:
+                top = cur
+    top = (top[1], top[4], top[3])
+    return [k for k in top[0] if k < m - 1], top[1], top[2]
 
 
 def emit(g, sem, ops, sent):

@@ -6,8 +6,10 @@ BIG = float(2 ** 23)
 HUGE = float(2 ** 30)
 ROUND = 1.5 * 2 ** 34
 PAD = 256 + CAP
-OPT = {"far": (64, 64, 64, 32, 32), "cand": (32,) * 8, "spath": (0, 4), "spath0": (0, 1, 4, 5), "relu2": (), "tail": 1, "ns": 3, "neq": "P", "kd": "P",
-       "vf": 0.04, "sf": 0.07, "pe": 0.6e-3, "wake": 0.16, "look": 0.2, "lag": 0.7, "tries": 2000, "seed": 1, "noise": 0.4, "heat": 1.0}
+OPT = {"far": (64, 64, 64, 32, 32), "farD": (64, 64, 64, 32, 32), "cand": (32,) * 8, "spath": (4, 5, 6, 7), "spath0": (4, 5, 6, 7), "vl": 128, "relu2": (), "p16": False, "far_links": 1.2,
+       "models": ((1.4, 0.93, 0.85, -0.01, 0.03), (1.7, 1.1, 1.4, 0.01, -0.04)), "dec": "P", "gconv": True,
+       "lists": [([0], [0]), ([0, 1, 2, 3], [1, 2, 3, 4])], "tail": 1, "ns": 3, "neq": "V", "kd": "P",
+       "vf": 0.04, "sf": 0.07, "pe": 0.6e-3, "wake": 0.16, "look": 0.2, "lag": 0.7, "tries": 100, "seed": 1, "noise": 0.4, "heat": 1.0, "steps": 140000, "temp": 0.35}
 
 SCRATCH = {}
 
@@ -18,49 +20,63 @@ def _b(names, cols, dtype="float32", where="sbuf"):
 
 
 _b("K1 K2 CC WW DD DF NN HI", 512, "float32", "psum")
-_b("morS meaQ", 3072, "bfloat16")
+_b("morS", 12 * PAD, "bfloat16")
+_b("meaQ", 3072, "bfloat16")
 _b("meaS neq m16 dd2 aa2 X2 Y2", 1024, "bfloat16")
 _b("oneb", 512, "bfloat16")
 _b("meaT", 1024 + CAP, "bfloat16")
-_b("basI derI", 1024, "int32")
+_b("basI derI b15", 1024, "int32")
 _b("useI", 512, "int32")
 PW = 1024
 _b("Pt", PW)
 _b("lane nbr ydS", 1024)
 _b("nbT", 1024 + CAP)
 _b("useF", 512)
-_b("useQ", 512 * RO)
-_b("PQ", PW * RO)
+_b("PQ", 1024 if OPT["p16"] else 1024 * RO)
 _b("mvr", 16384, "bfloat16")
+_b("mvt", 2048, "bfloat16")
+_b("mvx", 128, "bfloat16")
 _b("D16", 1024, "uint16")
 _b("cl of", 80, "uint16")
 _b("XD YD XL YL dd1 aa1", 4096, "bfloat16")
 _b("cU1 EU1", 256, "uint16")
 _b("cU2 EU2 mu", 64, "uint16")
 _b("sel", 8, "uint16")
-_b("cF1 SS1 EP1 val xm dec mk8 mbig", 256)
+_b("EP1 xm mk8", 256)
+_b("cF1 val", 256, "float16")
+_b("SS", 384)
+_b("ZB LT", 408, "float16")
+_b("th", 128, "bfloat16")
+_b("Ih", 128 + 16, "float16")
+_b("cF2", 64, "float16")
 _b("hi", 32)
-_b("cA EE", PAD)
-_b("cF2 nb2 EP2 E2 e15", 64)
+_b("EE", PAD)
+_b("cA", PAD * RO)
+_b("cS", 512)
+_b("clQ", 256, "uint16")
+if OPT["p16"]:
+    _b("P16", 1024, "float16")
+    _b("PL", 1024 * RO, "float16")
+_b("nb2 EP2 E2 e15", 64)
 _b("LZ LB", 512)
-_b("SS2 ZB1 ZB2 LT1 LT2 one If nIf o16 hold", 128)
+_b("LT3 one If nIf n2If o16 mbig", 128)
 _b("qi ik8", 256, "int32")
 _b("qa qc qd s16 t12 c97 c1", 80, "int32")
 _b("eq aE1 d1 old ab", 256, "bfloat16")
 _b("ad got cum", PAD, "bfloat16")
 _b("le lc mseg", 2 * PAD, "bfloat16")
 _b("junk", 4 * PAD, "bfloat16")
-_b("ad2 aE2 got2 mv2 w64 t65", 64, "bfloat16")
-_b("Ib nIb IB IH nIH nH no16 tmb bo nbo tri k15", 128, "bfloat16")
-_b("W8 nW8 w8t", 8, "bfloat16")
+_b("ad2 aE2 got2 old2 d2", 64, "bfloat16")
+_b("n8k Ib nIb IB IH nIH nH no16 tmb bo bo2 nbo w128 tri k15", 128, "bfloat16")
+_b("W8 w8t", 8, "bfloat16")
 _b("RR", 16)
 _b("km", 260)
 _b("ikm", 260, "int32")
 _b("nm b8 sc cnt", 8)
 
 QS = ("V", "S", "P", "G")
-SEMAPHORES = list(QS) + ["ld%d" % i for i in range(5)] + ["st"]
-for _n in ["M%d" % d for d in (1, 2, 3)] + ["U%d" % t for t in range(RO)] + ["P%d" % t for t in range(RO)]:
+SEMAPHORES = list(QS) + ["ld%d" % i for i in range(6)] + ["st"]
+for _n in ["M%d" % d for d in (1, 2, 3)] + ["C%d" % d for d in range(4)] + ["U%d" % t for t in range(RO)] + ["P%d" % t for t in range(RO)]:
     SEMAPHORES += ["a" + _n, "s" + _n]
 
 CY, WAKE = 0.9e-3, 0.08
@@ -163,17 +179,20 @@ def rank_program(g, core, T, topo):
 
     def load(qn, i, out, in_, W, us):
         op(qn, 0.1, [lambda e: e.dma_start(out, in_)], (), W, sem="ld%d" % i, inc=16, wake=us, label="load")
-    load("Y", 0, T.basI[:], T.bas[:], ["basI"], 3.0)
-    load("S", 1, T.meaS[:], T.mea[:], ["meaS"], 3.5)
-    load("S", 2, T.useI[:], T.use[:], ["useI"], 4.5)
-    load("Y", 3, T.derI[:], T.der[:], ["derI"], 6.0)
-    load("Y", 4, T.morS[:], T.mor[:], ["mor"], 8.0)
-    for k in range(1, 5):
+    mor = T.morS[:, 0:3072]
+    load("S", 5, T.b15[0:8, :], T.bas[15::16, :], ["b15"], 2.3)
+    load("Y", 1, T.meaS[:], T.mea[:], ["meaS"], 3.2)
+    load("Y", 2, T.useI[:], T.use[:], ["useI"], 4.2)
+    load("Y", 3, T.derI[:], T.der[:], ["derI"], 6.2)
+    load("Y", 0, T.basI[:], T.bas[:], ["basI"], 8.2)
+    load("Y", 4, mor, T.mor[:], ["mor"], 11.0)
+    for k in range(1, 6):
         ops[k]["deps"][k - 1] = 0
 
     fill(T.one[:], 1.0, ["one"], 128)
     fill(T.oneb[:], 1.0, ["oneb"], 512)
-    sel(T.e15[:], T.one[:, 0:64], [[-16, 8], [0, 8]], A.is_equal, -15, 1, ["one"], ["e15"], 64)
+    sel(T.e15[:], T.one[:, 0:64], [[-1, 8], [0, 8]], A.is_equal, 0, 1, ["one"], ["e15"], 64)
+    tc(T.ydS[0:8, :], T.b15[0:8, :], ["b15"], ["yd0", "yd1", "yd2", "yd3"], 1024, label="B")
     iota(T.ik8[:], [[0, 32], [-1, 8]], 128, 1, ["ik8"], 256)
     sel(T.RR[:], T.one[:, 0:16], [[-8, 16]], A.is_ge, 0, 1, ["one"], ["RR"], 16)
     sel(T.RR[:], T.RR[:], [[8, 16]], A.is_ge, 7, -1, ["RR"], ["RR"], 16)
@@ -184,55 +203,65 @@ def rank_program(g, core, T, topo):
     sel(T.w8t[:], T.w8t[:], [[16, 8]], A.is_ge, 15, -1, ["w8t"], ["w8t"], 8)
     act(T.W8[:], T.w8t[:], ["w8t"], ["W8"], 8, scale=2048.0)
     act(T.b8[:], T.w8t[:], ["w8t"], ["b8"], 8)
-    for nm_, sc_ in (("Ib", 1.0), ("IB", BIG), ("nIb", -1.0), ("nIf", -1.0), ("IH", HUGE), ("nIH", -HUGE)):
+    gcopy(T.Ih[:, 128:136], T.w8t[:], ["w8t"], ["b8h"], 8, "gsel")
+    gcopy(T.Ih[:, 0:128], T.If[:], ["If"], ["Ih"], 128, "gsel")
+    for nm_, sc_ in (("Ib", 1.0), ("IB", BIG), ("nIb", -1.0), ("nIf", -1.0), ("n2If", -2.0), ("IH", HUGE), ("nIH", -HUGE)):
         act(T[nm_][:], T.If[:], ["If"], [nm_], 128, scale=sc_)
     act(T.o16[:], T.one[:], ["one"], ["o16"], 128, scale=1.0 / 16)
     act(T.no16[:], T.one[:], ["one"], ["no16"], 128, scale=-1.0 / 16)
     act(T.nH[:], T.one[:], ["one"], ["nH"], 128, scale=-HUGE)
+    act(T.n8k[:], T.one[:], ["one"], ["n8k"], 128, scale=-8192.0)
     NS = OPT["ns"]
     NV = 4 - NS
-    for nm_, x, y, first, c in (("mbig", -2.0 * BIG, 2.0 * BIG, T.mbig[:, 0::16], 256), ("m16", 1.0, 0.0, T.m16[:, 0::16], 512), ("hold", 1.0, 0.0, T.hold[:, 0::8], 128),
+    for nm_, x, y, first, c in (("mbig", -2.0 * BIG, 2.0 * BIG, T.mbig[:, 0::16], 128), ("m16", 1.0, 0.0, T.m16[:, 0::16], 512),
                                 ("mseg", 1.0, 0.0, T.mseg[:, 0::PAD], PAD)):
         fill(T[nm_][:], x, [nm_], c)
         fill(first, y, [nm_], 64)
-    fill(T.ZB1[:], 0.0, ["ZB1"], 128)
-    fill(T.ZB2[:], 0.0, ["ZB2"], 128)
-    for nm_, a in (("cA", 256), ("EE", 256), ("ad", 256), ("got", 256), ("meaT", 1024), ("nbT", 1024)):
+    ts(T.ZB[:], T.oneb[:, 0:408], 0.0, A.mult, ["oneb"], ["ZB0", "ZB1", "ZB2"], 408, 0.5)
+    ts(T.LT[:, 128::136], T.oneb[:, 0:3], 0.0, A.mult, ["oneb"], ["LTpad"], 3)
+    act(T.Ih[:, 136:144], T.w8t[:], ["w8t"], ["nb8h"], 8, scale=-1.0)
+    for t in range(RO):
+        fill(T.cA[:, PAD * t + 256:PAD * t + PAD], 0.0, ["cApad%d" % t], CAP)
+    fill(T.sc[:, 1:2], 1024.0, ["k1"], 1)
+    for nm_, a in (("EE", 256), ("ad", 256), ("got", 256), ("meaT", 1024), ("nbT", 1024)):
         fill(T[nm_][:, a:a + CAP], 0.0, [nm_ + "pad"], CAP)
     qi = [T.qi[:, 16 * i:16 * i + 16] for i in range(16)]
     pw = T.sc[:, 0:1]
     iota(qi[0], [[0, 16]], 0, 1, ["pi"], 16)
     ts(qi[1], qi[0], 15, A.bitwise_and, ["pi"], ["pj"], 16)
     ts(pw, T.qi[:, 16:17], 1.0, A.add, ["pj"], ["pw"], 1)
+    iota(T.th[:], [[0, 8], [1, 16]], 0, 0, ["th"], 128)
+    ts(T.th[:], T.th[:], pw, A.is_lt, ["th", "pw"], ["th"], 128, 0.5)
+    fill(T.th[:, 0::16], 0.0, ["th"], 8)
     iota(T.s16[:], [[0, 5], [16, 16]], -1, 0, ["s16"], 80)
     ts(T.t12[:], T.s16[:], pw, A.add, ["pw", "s16"], ["t12"], 80, s2=12.0, op1=A.mult)
     ts(T.sc[:, 4:8], T.s16[:, 0:4], pw, A.add, ["pw", "s16"], ["sc"], 4, s2=0.5, op1=A.add)
     iota(T.c97[:], [[97, 5], [0, 16]], 0, 0, ["c97"], 80)
     iota(T.c1[:], [[1, 5], [0, 16]], 0, 0, ["c1"], 80)
-    sel(T.t65[:], T.oneb[:, 0:64], [[-16, 8], [0, 8]], A.is_ge, 0, 1, ["oneb"], ["t65"], 64)
-    sel(T.t65[:], T.t65[:], [[16, 8], [0, 8]], A.is_ge, 15, -1, ["t65"], ["t65"], 64)
-    ts(T.w64[:], T.t65[:], pw, A.mult, ["t65", "pw"], ["w64"], 64)
     sel(T.tmb[:], T.oneb[:, 0:128], [[-16, 8], [0, 16]], A.is_ge, 0, 1, ["oneb"], ["tmb"], 128)
     sel(T.bo[:], T.tmb[:], [[16, 8], [0, 16]], A.is_ge, 15, -1, ["tmb"], ["bo"], 128)
     act(T.nbo[:], T.bo[:], ["bo"], ["nbo"], 128, scale=-1.0)
-    act(T.nW8[:], T.w8t[:], ["w8t"], ["nW8"], 8, scale=-2048.0)
+    act(T.bo2[:], T.bo[:], ["bo"], ["bo2"], 128, scale=2.0)
+    ts(T.w128[:], T.bo[:], pw, A.mult, ["bo", "pw"], ["w128"], 128, 0.5)
+    fill(T.morS[:, 3072:3840], 0.0, ["morpad"], 384)
     sel(T.tmb[:], T.bo[:], [[1, 128]], A.is_ge, 0, -1, ["bo"], ["tmb"], 128)
     act(T.tri[:], T.tmb[:], ["tmb"], ["tri"], 128, scale=8192.0)
     sel(T.tmb[:], T.oneb[:, 0:128], [[0, 8], [1, 16]], A.is_equal, -15, 0, ["oneb"], ["tmb"], 128)
     ts(T.k15[:], T.tmb[:], 8192.0, A.mult, ["tmb"], ["k15"], 128, 0.5, s2=-4096.0, op1=A.add)
-    for tau in range(4):
-        iota(T.lane[:, 256 * tau:256 * tau + 256], [[4, 256]], tau, 0, ["lane%d" % tau], 256)
-    iota(T.nbr[:], [[2, 512], [-1, 2]], 1, 0, ["nbr"], 1024)
     iota(T.ikm[:], [[1, 260]], 128, -1, ["ikm"], 260)
     ts(T.ikm[:], T.ikm[:], 15, A.bitwise_and, ["ikm"], ["ikm"], 260)
     ts(T.km[:], T.ikm[:], 0.0, A.is_equal, ["ikm"], ["km"], 260)
     fill(T.nm[:, 0:1], 0.0, ["nm0"], 1)
+    early = range(6, len(ops) + 1)
+    for tau in range(4):
+        iota(T.lane[:, 256 * tau:256 * tau + 256], [[4, 256]], tau, 0, ["lane%d" % tau], 256)
+    iota(T.nbr[:], [[2, 512], [-1, 2]], 1, 0, ["nbr"], 1024)
 
     for tau in range(4):
         ts(T.nbT[:, 256 * tau:256 * tau + 256], T.basI[:, tau::4], -1.0, A.mult, ["basI"], ["nbT%d" % tau], 256, label="nbT")
-    tc(T.useF[:], T.useI[:], ["useI"], ["useF"], 512, label="useF")
+    (gcopy if OPT["gconv"] else tc)(T.useF[:], T.useI[:], ["useI"], ["useF"], 512, label="useF")
     for tau in range(4):
-        tc(T.D16[:, 256 * tau:256 * tau + 256], T.derI[:, tau::4], ["derI"], ["D16_%d" % tau], 256, label="D16")
+        (gcopy if OPT["gconv"] and tau else tc)(T.D16[:, 256 * tau:256 * tau + 256], T.derI[:, tau::4], ["derI"], ["D16_%d" % tau], 256, label="D16")
         gcopy(T.meaT[:, 256 * tau:256 * tau + 256], T.meaS[:, tau::4], ["meaS"], ["meaT%d" % tau], 256, "meaT")
 
     def wide(nm_, tau):
@@ -240,17 +269,26 @@ def rank_program(g, core, T, topo):
 
     def mvrep(tau):
         for k in range(16):
-            o, i_ = T.mvr[:, 4096 * tau + k:4096 * tau + 4096:16], T.meaS[:, tau::4]
+            o, i_ = T.mvr[:, 4096 * tau + k:4096 * tau + 16 * VL:16], T.meaS[:, tau:4 * VL:4]
             if tau:
-                gcopy(o, i_, ["meaS"], ["mvr%d.%d" % (tau, k)], 256, "mvrg")
+                gcopy(o, i_, ["meaS"], ["mvr%d.%d" % (tau, k)], VL, "mvrg")
             else:
-                both(o, i_, ["meaS"], ["mvr%d.%d" % (tau, k)], 256, "mvr", 0.5)
+                both(o, i_, ["meaS"], ["mvr%d.%d" % (tau, k)], VL, "mvr", 0.5)
+        for k in range(2 * (VL < 256)):
+            o, i_ = T.mvt[:, 512 * tau + 2 * VL + k:512 * tau + 512:2], T.meaS[:, 4 * VL + tau::4]
+            if tau:
+                gcopy(o, i_, ["meaS"], ["mvt%d.%d" % (tau, k)], 256 - VL, "mvrg")
+            else:
+                both(o, i_, ["meaS"], ["mvt%d.%d" % (tau, k)], 256 - VL, "mvr", 0.5)
+    VL = OPT["vl"]
     mvrep(0)
     Ph = ["Ph0", "Ph1"]
     for hf in range(2):
         c0 = slice(512 * hf, 512 * hf + 512)
         bank = ("NN", "DF")[hf]
-        tt(T.neq[:, c0], T.basI[:, c0], T.derI[:, c0], A.not_equal, ["basI", "derI"], ["neq%d" % hf], 512, label="neq")
+        P(2048, [(T[bank][:, tau::4], T.nIf[:], T.nbT[:, 256 * tau + 128 * hf:256 * tau + 128 * hf + 128], tau == 0, tau == 3) for tau in range(4)],
+          ["nIf"] + ["nbT%d" % tau for tau in range(4)], ["!" + bank])
+        tt(T.neq[:, c0], T.derI[:, c0], T[bank][:], A.not_equal, ["!" + bank, "derI"], ["neq%d" % hf], 512, 1.0, "neq")
         P(1024, [(T[bank][:], T.k15[0:1, :], T.oneb[0:1, 0:512], True, False), (T[bank][:], T.tri[:], T.neq[:, c0], False, True)],
           ["tri", "k15", "neq%d" % hf, "oneb"], ["!" + bank])
         tt(T.Pt[:, c0], T.derI[:, c0], T[bank][:], A.min, ["derI", "!" + bank], ["Ph%d" % hf], 512, 1.0, "P0")
@@ -266,41 +304,63 @@ def rank_program(g, core, T, topo):
         return B[:, 0:16 * len(rounds)], slice(16 * rounds[0], 16 * rounds[-1] + 16), 16 * len(rounds)
 
     def lists(taus, rounds, bank):
-        x, c, w = bylane("B", taus, rounds, lambda tau, h: T.nbT[:, 256 * tau + h:256 * tau + 256:2], ["nbT%d" % tau for tau in taus], T.e15[:], "e15", 256, bank)
-        tt(T.qa[:, c], T.c97[:, c], x, A.subtract, ["!" + bank, "c97"], ["qa"], w, 1.0, "B")
+        x, c, w = bylane("B", taus, rounds, lambda tau, h: T.ydS[0:8, 4 * h + tau::8], ["yd%d" % tau for tau in taus], T.e15[0:8, :], "e15", 256, bank)
+        tt(T.qa[:, c], T.c97[:, c], x, A.add, ["!" + bank, "c97"], ["qa"], w, 1.0, "B")
         ts(T.qa[:, c], T.qa[:, c], 511, A.bitwise_and, ["qa"], ["qa"], w, label="B")
         tc(T.cl[:, c], T.qa[:, c], ["qa"], ["cl%d" % t for t in rounds], w, label="B")
 
     def places(taus, rounds, bank):
-        x, c, w = bylane("Z", taus, rounds, lambda tau, h: T.meaS[:, 4 * h + tau::8], ["meaS"], T.w64[:], "w64", 64, bank)
+        x, c, w = bylane("Z", taus, rounds, lambda tau, h: T.meaS[:, 4 * h + tau::8], ["meaS"], T.w128[:, 0::2], "w128", 64, bank)
         tt(T.qc[:, c], T.c1[:, c], x, A.add, ["!" + bank, "c1"], ["qc"], w, 1.0, "Z")
         ts(T.qd[:, c], T.qc[:, c], 7, A.bitwise_and, ["qc"], ["qd"], w, label="Z")
         tt(T.qc[:, c], T.qd[:, c], T.t12[:, c], A.add, ["qd", "t12"], ["qc"], w, label="Z")
         tc(T.of[:, c], T.qc[:, c], ["qc"], ["of%d" % t for t in rounds], w, label="Z")
 
-    sent = {}
+    sent, issued = {}, {}
 
     def send(d, buf, in_, name, R, us):
         to, frm = T.cores[(rank - d) % n], T.cores[(rank + d) % n]
         rid, pid = topo.addr(to)[:2]
         mask = topo.mask(core, to)
         sent["s" + name] = len(topo.engines(core, to))
-        k = op("G", 0.5 if len(sent) > 1 else 3.0, [lambda e: e.remote_dma(buf, in_, sm["a" + name], sm["s" + name], pid, rid, mask)], R, (), sem="s" + name, inc=0, wake=us, label="send")
+        k = op("G", 0.7 if len(sent) > 1 else 3.5, [lambda e: e.remote_dma(buf, in_, sm["a" + name], sm["s" + name], pid, rid, mask)], R, (), sem="s" + name, inc=0, wake=us, label="send")
         j = op("R", us, [], (), ["Q" + name], sem="a" + name, inc=len(topo.engines(frm, core)), label="arrive")
         ops[j]["deps"][k] = 0
+        issued[name] = k
+        for a in early:
+            if ops[a]["q"] == "G":
+                ops[k]["deps"].setdefault(a, 0)
+
+    def after(*names):
+        for x in names:
+            if x in issued:
+                ops[-1]["deps"].setdefault(issued[x], 0)
+
+    def send_classes(j):
+        c = slice(16, 80) if j else slice(0, 16)
+        send(-max(j, 1), T.clQ[:, 64 * j:64 * j + c.stop - c.start], T.cl[:, c], "C%d" % j, ["cl%d" % t for t in range(RO) if (t > 0) == (j > 0)], 3.0)
 
     def send_use(t):
-        send(1 + t % 3, T.useQ[:, 512 * t:512 * t + 512], T.useF[:], "U%d" % t, ["useF"], 6.0)
+        d, s = 1 + t % 3, T.cS[:, 256 * (t % 2):256 * (t % 2) + 256]
+        lst = T.clQ[:, 64 * d + 16 * t - 16:64 * d + 16 * t] if t else T.clQ[:, 0:16]
+        both(s, T.useF[:].indirect(lst), ["useF", "QC%d" % (d if t else 0)], ["cS%d" % (t % 2)], 256, "cA")
+        send(d, T.cA[:, PAD * t:PAD * t + 256], s, "U%d" % t, ["cS%d" % (t % 2)], 4.5)
 
     def send_P(t):
-        send(1 + t % 3, T.PQ[:, PW * t:PW * t + PW], T.Pt[:], "P%d" % t, Ph + ["Ppad"], 9.0)
+        if OPT["p16"]:
+            c = slice((t - 1) % 4, 1024, 4) if t else slice(0, 1024)
+            ts(T.P16[:, c], T.Pt[:, c], -1024.0, A.add, Ph, ["P16"], 256 if t else 1024, label="P16")
+            send(1 + t % 3, T.PL[:, 1024 * t:1024 * t + 1024], T.P16[:], "P%d" % t, ["P16"], 6.0)
+            gcopy(T.PQ[:, 0:1024], T.PL[:, 1024 * t:1024 * t + 1024], ["QP%d" % t], ["PQ"], 1024, "PQ")
+        else:
+            send(1 + t % 3, T.PQ[:, 1024 * t:1024 * t + 1024], T.Pt[:], "P%d" % t, Ph, 9.0)
 
     def send_mea(d):
         send(d, T.meaQ[:, 1024 * d - 1024:1024 * d], T.meaS[:], "M%d" % d, ["meaS"], 6.0)
 
     flip = [0]
 
-    def cands(c, cuts, spath, mea, meaR, rep, repR):
+    def cands(c, cuts, spath, mea, meaR, rep, repR, own):
         cU, dd, aa = T["cU" + c], T["dd" + c], T["aa" + c]
         l0 = 0
         for j, w in enumerate(cuts):
@@ -312,56 +372,65 @@ def rank_program(g, core, T, topo):
                 bank = ("CC", "WW")[flip[0]]
                 o = T[bank][:, 0:b - a]
                 act(dd[:, a:b], src, [meaR, "cU" + c], [dR], b - a, f=GA, label="scand" + c)
-                P(b - a, [(o, T.nIb[:], rep[:, a:b], True, False)], ["nIb"] + repR, ["!" + bank], "scand" + c)
+                if l0 <= VL:
+                    P(b - a, [(o, T.nIb[:], rep[:, a:b], True, False)], ["nIb"] + repR, ["!" + bank], "scand" + c)
+                else:
+                    P(512, [(o[:, k::8], T.nIb[:], own[0][:, 2 * (l0 - w):2 * l0], k == 0, False) for k in range(8)], ["nIb"] + own[1], ["!" + bank], "scand" + c)
                 P(b - a, [(o, T.Ib[:], dd[:, a:b], False, True)], ["Ib", dR], ["!" + bank], "scand" + c)
                 act(aa[:, a:b], o, ["!" + bank], aR, b - a, F.Abs, label="scand" + c)
             else:
                 tt(dd[:, a:b], src, rep[:, a:b], A.subtract, [meaR, "cU" + c] + repR, [dR], b - a, GA, "cand" + c)
                 act(aa[:, a:b], dd[:, a:b], [dR], aR, b - a, F.Abs, label="abs" + c)
 
-    def least(c, bank, p, w, run, hold, holdR):
-        K, SS, ZB, hi = T[bank], T["SS" + c], T["ZB" + c], T.hi[0:p, 16 * int(c) - 16:16 * int(c) - 16 + w // 16]
-        scan(SS[0:p, :], T.mbig[0:p, 0:w], K[0:p, 0:w], A.max, A.min, ["!" + bank, "mbig"], ["SS" + c], w, 1.0, "min" + c)
-        ts(hi, SS[0:p, 15::16], ROUND, A.add, ["SS" + c], ["hi" + c], 16, label="min" + c, s2=ROUND, op1=A.subtract)
-        tt(ZB[0:p, 0::run], SS[0:p, 15::16], hi, A.subtract, ["SS" + c, "hi" + c], ["ZB" + c], 16, label="min" + c)
-        scan(K[0:p, w:w + 128], hold, ZB[0:p, :], A.mult, A.add, ["ZB" + c, holdR], ["!" + bank], 128, 1.0, "min" + c)
+    def least(j, bank, p, out, outW):
+        K, c, lb = T[bank], slice(128 * j, 128 * j + 128), "min%d" % (j // 2 + 1)
+        c0, c1 = slice(136 * j, 136 * j + 128), slice(136 * j + 1, 136 * j + 129)
+        SS, ZB, LT, hi = T.SS[0:p, c], T.ZB[0:p, c0], T.LT[0:p, c0], T.hi[0:p, 8 * j:8 * j + 8]
+        scan(SS, T.mbig[0:p, :], K[0:p, 0:128], A.max, A.min, ["!" + bank, "mbig"], ["SS%d" % j], 128, 1.0, lb)
+        ts(hi, SS[:, 15::16], ROUND, A.add, ["SS%d" % j], ["hi%d" % j], 8, label=lb, s2=ROUND, op1=A.subtract)
+        tt(ZB[:, 0::16], SS[:, 15::16], hi, A.subtract, ["SS%d" % j, "hi%d" % j], ["ZB%d" % j], 8, label=lb)
+        scan(LT, T.th[0:p, :], ZB, A.mult, A.add, ["ZB%d" % j, "th"], ["LT%d" % j], 128, 0.5, lb)
+        o, pos, neg = K[:, 0:p // 16], T.Ih[0:p, 128:128 + p // 16], T.Ih[0:p, 136:136 + p // 16]
+        P(64, [(o, T.ZB[0:p, c1], pos, True, False)], ["ZB%d" % j, "b8h"], ["!" + bank], lb)
+        P(128, [(o, LT, pos, False, False), (o, T.LT[0:p, c1], neg, False, True)], ["LT%d" % j, "b8h", "nb8h", "LTpad"], ["!" + bank], lb)
+        tc(out, K[:, 0:p // 16], ["!" + bank], [outW], 8, label=lb)
 
     def mu(t):
-        return T.mu[:, 16 * (t % 2):16 * (t % 2) + 16], "mu%d" % (t % 2)
+        return T.mu[:, 16 * (t % 2):16 * (t % 2) + 16], ["mu%d.%d" % (t % 2, h) for h in range(2)]
 
     def own_lists(t):
         tau = t % 4
-        use, cl, clR = T.useF[:], T.cl[:, 16 * t:16 * t + 16], ["useF", "cl%d" % t]
+        use, cl, clR = T.useF[:] if t else T.useI[:], T.cl[:, 16 * t:16 * t + 16], ["useF" if t else "useI", "cl%d" % t]
         tc(T.cU1[:], use.indirect(cl), clR, ["cU1"], 256, GA, "cU1")
         both(T.cF1[:], use.indirect(cl), clR, ["cF1"], 256, "cF1")
+        for a in early if t == 0 else ():
+            ops[-1]["deps"].setdefault(a, 0)
         tt(T.eq[:], use.indirect(cl), T.lane[:, 256 * tau:256 * tau + 256], A.is_equal, clR + ["lane%d" % tau], ["eq"], 256, GA, "eq")
 
     def own(t):
         tau = t % 4
-        cands("1", OPT["cand"], OPT["spath0" if t == 0 else "spath"], T.meaS[:], "meaS", T.mvr[:, 4096 * tau:4096 * tau + 4096], ["mvr%d.%d" % (tau, k) for k in range(16)])
-        K = T.K1
-        P(1280, [(K[:, 128 * h:128 * h + 128], x[:, h::2], y[:], i + h == 0, False) for i, (x, y) in enumerate(((T.cF1, T.If), (T.eq, T.IB))) for h in range(2)],
-          ["cF1", "If", "eq", "IB"], ["!K1"], "keys1")
-        P(2048, [(K[:, 128 * h + k:128 * h + 128:16], T.aa1[:, 16 * h + k::32], T.W8[:], False, h == 1 and k == 15) for h in range(2) for k in range(16)],
-          ["W8"] + ["aa1.%d" % x for x in range(16)], ["!K1"], "keys1")
-        least("1", "K1", 128, 256, 8, T.hold[:], "hold")
-        for h in range(2):
-            tt(T.LT1[:, h::2], K[:, 256 + 64 * h:320 + 64 * h], T.mk8[:, 0:64], A.mult, ["!K1", "mk8"], ["LT1.%d" % h], 64, 1.0, "min1")
-        P(256, [(K[:, 0:16], T.LT1[:], T.RR[:], True, True)], ["LT1.0", "LT1.1", "RR"], ["!K1"], "keys1")
-        tc(mu(t)[0], K[:, 0:16], ["!K1"], [mu(t)[1]], 16, label="min1")
+        cands("1", OPT["cand"], OPT["spath0" if t == 0 else "spath"], T.meaS[:], "meaS", T.mvr[:, 4096 * tau:4096 * tau + 4096], ["mvr%d.%d" % (tau, k) for k in range(16)], (T.mvt[:, 512 * tau:512 * tau + 512], ["mvt%d.%d" % (tau, k) for k in range(2)]))
+        for h, bank in enumerate(("K1", "DF")):
+            K, c = T[bank], slice(128 * h, 128 * h + 128)
+            P(256, [(K[:, 0:128], T.cF1[:, c], T.Ih[:, 0:128], True, False), (K[:, 0:128], T.eq[:, c], T.IB[:], False, False)], ["cF1", "Ih", "eq", "IB"], ["!" + bank], "keys1")
+            P(1024, [(K[:, k:128:16], T.aa1[:, 2048 * h + k:2048 * h + 2048:16], T.W8[:], False, k == 15) for k in range(16)],
+              ["W8"] + ["aa1.%d" % x for x in range(8 * h, 8 * h + 8)], ["!" + bank], "keys1")
+            least(h, bank, 128, mu(t)[0][:, 8 * h:8 * h + 8], mu(t)[1][h])
 
     def ask(t):
         tau, d, K = t % 4, 1 + t % 3, T.K2
-        sl, mea, mv2 = T.sel[:, 0:4], T.meaQ[:, 1024 * d - 1024:1024 * d], T.mv2[:]
-        tc(T.cU2[:], T.cA[:].indirect(sl), ["cA", "cApad", "sel"], ["cU2"], 64, GA, "cU2")
+        sl, mea, mv2 = T.sel[:, 0:4], T.meaQ[:, 1024 * d - 1024:1024 * d], T.mvx[:, 0::2]
+        cA, cR = T.cA[:, PAD * t:PAD * t + PAD], ["QU%d" % t, "cApad%d" % t, "sel"]
+        tc(T.cU2[:], cA.indirect(sl), cR, ["cU2"], 64, GA, "cU2")
         win, wR = wide("meaT", tau)
         both(mv2, win.indirect(sl), wR + ["sel"], ["mv2"], 64, "mv2")
-        both(T.cF2[:], T.cA[:].indirect(sl), ["cA", "cApad", "sel"], ["cF2"], 64, "cF2")
-        P(512, [(K[0:64, 0:128], T.cF2[:], T.If[:], True, False)], ["cF2", "If"], ["!K2"], "keys2")
+        both(T.mvx[:, 1::2], win.indirect(sl), wR + ["sel"], ["mv3"], 64, "mv2")
+        both(T.cF2[:], cA.indirect(sl), cR, ["cF2"], 64, "cF2")
+        P(128, [(K[0:64, 0:128], T.cF2[:], T.Ih[:, 0:128], True, False)], ["cF2", "Ih"], ["!K2"], "keys2")
         for h, bank in enumerate(("CC", "WW")):
             B, c = T[bank], slice(512 * h, 512 * h + 512)
             both(T.dd2[:, c], mea.indirect(T.cU2[:, 32 * h:32 * h + 32]), ["QM%d" % d, "cU2"], ["dd2.%d" % h], 512, "cand2")
-            P(1024, [(B[:, k::16], T.nIb[:], T.mv2[:, 32 * h:32 * h + 32], k == 0, False) for k in range(16)], ["nIb", "mv2"], ["!" + bank], "cand2")
+            P(512, [(B[:, k::8], T.nIb[:], T.mvx[:, 64 * h:64 * h + 64], k == 0, False) for k in range(8)], ["nIb", "mv2", "mv3"], ["!" + bank], "cand2")
             P(512, [(B[:], T.Ib[:], T.dd2[:, c], False, True)], ["Ib", "dd2.%d" % h], ["!" + bank], "cand2")
             o = [K[32 * h:32 * h + 32, k:128:16] for k in range(16)]
             if h in OPT["relu2"]:
@@ -370,37 +439,53 @@ def rank_program(g, core, T, topo):
             else:
                 act(T.aa2[:, c], B[:], ["!" + bank], ["aa2.%d" % h], 512, F.Abs, label="abs2")
             P(512, [(o[k], T.aa2[:, 512 * h + k:512 * h + 512:16], T.W8[:], False, k == 15) for k in range(16)], ["W8", "aa2.%d" % h], ["!K2"], "keys2")
-        least("2", "K2", 64, 128, 16, T.m16[0:64, 0:128], "m16")
-        tt(T.LT2[0:64, :], K[0:64, 128:256], T.km[0:64, 0:128], A.mult, ["!K2", "km"], ["LT2"], 128, 1.0, "min2")
-        P(256, [(K[:, 0:4], T.LT2[0:64, :], T.b8[0:64, 0:4], True, True)], ["LT2", "b8"], ["!K2"], "keys2")
-        tc(T.mu[:, 32:36], K[:, 0:4], ["!K2"], ["mu2"], 4, label="min2")
+        least(2, "K2", 64, T.mu[:, 32:36], "mu2")
 
     def far(nm_, lst, lstR, cuts, tail, mv, mvR, gap, out, sign, stop):
         X, Y, at = T["X" + nm_], T["Y" + nm_], [sum(cuts[:j]) for j in range(len(cuts) + 1)]
         for j in range(len(cuts)):
             a, b = 16 * at[j], 16 * at[j + 1]
-            both(X[:, a:b], T.morS[:].indirect(lst[:, at[j]:at[j + 1]]), [lstR, "mor"], ["X%s.%d" % (nm_, j)], b - a, nm_)
+            both(X[:, a:b], mor.indirect(lst[:, at[j]:at[j + 1]]), [lstR % (at[j] // 128) if "%" in lstR else lstR, "mor"], ["X%s.%d" % (nm_, j)], b - a, nm_)
             scan(Y[:, a:b], T.m16[:, 0:b - a], X[:, a:b], A.mult, A.max, ["X%s.%d" % (nm_, j), "m16"], ["Y%s.%d" % (nm_, j)], b - a, 0.5, "scan" + nm_)
         parts = [(0, len(cuts) - tail), (len(cuts) - tail, len(cuts))] if tail else [(0, len(cuts))]
         for i, (j0, j1) in enumerate(parts):
             a, b, gR = at[j0], at[j1], "gap%s.%d" % (nm_, i)
+            if a == b:
+                continue
+            if i:
+                yR = ["Y%s.%d" % (nm_, j) for j in range(j0, j1)]
+                P(64, [(out[:, a:b], T.nbo[:], mv[:, a:b], False, False)], ["nbo", mvR], ["!DD"], "delta")
+                tt(gap[:, a:b], Y[:, 16 * a + 15:16 * b:16], mv[:, a:b], A.max, yR + [mvR], [gR], b - a, label="gap" + nm_)
+                P(64, [(out[:, a:b], T.nbo[:], Y[:, 16 * a + 15:16 * b:16], False, False)], ["nbo"] + yR, ["!DD"], "delta")
+                P(64, [(out[:, a:b], T.bo2[:], gap[:, a:b], False, True)], ["bo2", gR], ["!DD"], "delta")
+                continue
             P(b - a, [(T.DF[:, a:b], T.nIb[:], mv[:, a:b], True, False)], ["nIb", mvR] + (["YD.0"] if nm_ == "D" else []), ["!DF"], "diff")
             P(b - a, [(T.DF[:, a:b], T.Ib[:], Y[:, 16 * a + 15:16 * b:16], False, True)], ["Ib"] + ["Y%s.%d" % (nm_, j) for j in range(j0, j1)], ["!DF"], "diff")
             act(gap[:, a:b], T.DF[:, a:b], ["!DF"], [gR], b - a, F.Abs, label="gap" + nm_)
             P(b - a, [(out[:, a:b], T[sign][:], gap[:, a:b], not stop, stop and j1 == len(cuts))], [sign, gR], ["!DD"], "delta")
 
     def decode(tau):
-        tt(T.dec[:], T.Pt[:, tau:1024:4], T.nbT[:, 256 * tau:256 * tau + 256], A.max, Ph + ["nbT%d" % tau], ["dec"], 256, label="dec")
-        act(T.ydS[:, tau::4], T.dec[:], ["dec"], ["yd%d" % tau], 256, F.Abs, label="dec")
+        x, o = T.Pt[:, tau:1024:4], T.DF[:, 256:512]
+        if OPT["dec"] == "V":
+            tt(T.xm[:], x, T.nbT[:, 256 * tau:256 * tau + 256], A.max, Ph + ["nbT%d" % tau], ["xm"], 256, label="dec")
+            act(T.ydS[:, tau::4], T.xm[:], ["xm"], ["yd%d" % tau], 256, F.Abs, label="dec")
+            return
+        P(2304, halves(o, T.nIf[:], T.nbT[:, 256 * tau:256 * tau + 256], True, False) + [(o, T.n8k[0:1, :], T.oneb[0:1, 0:256], False, False)], ["nIf", "n8k", "oneb", "nbT%d" % tau], ["!DF"], "dec")
+        P(1024, halves(o, T.n2If[:], x, False, True), ["n2If"] + Ph, ["!DF"], "dec")
+        tt(T.ydS[:, tau::4], x, o, A.max, Ph + ["!DF"], ["yd%d" % tau], 256, 1.0, "dec")
 
-    lists([0], [0], "WW")
+    for taus, rounds in OPT["lists"]:
+        lists(taus, rounds, "WW")
     send_mea(1)
+    for j in range(4):
+        send_classes(j)
+        after("M1")
+        ops[-2]["deps"][issued["M1"]] = 0
     send_use(0)
     send_P(0)
     own_lists(0)
     own(0)
     places([0, 1, 2, 3], [0, 1, 2, 3, 4], "K2")
-    lists([0, 1, 2, 3], [1, 2, 3, 4], "WW")
     send_mea(2)
     mvrep(1)
     send_mea(3)
@@ -410,7 +495,7 @@ def rank_program(g, core, T, topo):
     If, nIf, Ib, nIb = T.If[:], T.nIf[:], T.Ib[:], T.nIb[:]
     D1, D2, Lo, Hi = T.DD[:, 0:256], T.DD[:, 256:320], T.NN[:, 0:256], T.HI[:, 0:256]
     U1, U2, U3 = T.K1[:, 256:512], T.K2[:, 256:512], T.NN[:, 256:512]
-    row = T.oneb[0:1, 0:256]
+    row, EE = T.oneb[0:1, 0:256], ["EE.0", "EE.1"]
 
     def rnd(t):
         tau, last = t % 4, t + 1 == RO
@@ -423,24 +508,28 @@ def rank_program(g, core, T, topo):
             P(256, [(Lo, T.nH[0:1, :], row, True, False)], ["nH", "oneb"], ["!NN"], "Hi")
         elif OPT["neq"] == "P":
             P(1024, halves(U3, If, nb, True, False), ["If", nbR], ["!NN"], "Hi")
-        far("D", T.D16[:, 256 * tau:256 * tau + 256], "D16_%d" % tau, OPT["far"], 0, mv, "meaS", T.ad, D1, "nbo", False)
+        far("D", T.D16[:, 256 * tau:256 * tau + 256], "D16_%d" % tau, OPT["farD"], 0, mv, "meaS", T.ad, D1, "nbo", False)
         m = mu(t)
-        tt(T.EP1[:], T.Pt[:, 0:1024].indirect(m[0]), nb, A.max, Ph + [m[1], nbR], ["EP1"], 256, GA, "E1")
-        act(E, T.EP1[:], ["EP1"], ["EE"], 256, F.Abs, label="E1")
-        tc(T.EU1[:], E, ["EE"], ["EU1"], 256, label="E1")
+        for h in range(2):
+            c = slice(128 * h, 128 * h + 128)
+            tt(T.EP1[:, c], T.Pt[:, 0:1024].indirect(m[0][:, 8 * h:8 * h + 8]), nb[:, c], A.max, Ph + [m[1][h], nbR], ["EP1.%d" % h], 128, GA, "E1")
+            act(E[:, c], T.EP1[:, c], ["EP1.%d" % h], [EE[h]], 128, F.Abs, label="E1")
+            tc(T.EU1[:, c], E[:, c], [EE[h]], ["EU1.%d" % h], 128, label="E1")
+        after(*(["P%d" % t, "M3"] if t else ["U0", "M1", "C1", "C2", "C3"]))
         useT = T.useF[:, 37 * t:37 * t + 256]
         if OPT["kd"] == "P":
-            both(T.val[:], T.nbr[:].indirect(m[0]), ["nbr", m[1]], ["val"], 256, "val")
-            P(2048, halves(U1, nIf, useT, True, False) + halves(U1, If, T.val[:], False, True), ["If", "nIf", "val", "useF"], ["!K1"], "kd")
+            both(T.val[:], T.nbr[:].indirect(m[0]), ["nbr"] + m[1], ["val"], 256, "val")
+            P(1024, halves(U1, nIf, useT, True, False), ["nIf", "useF"] + m[1], ["!K1"], "kd")
+            P(256, [(U1, T.Ih[:, 0:128], T.val[:], False, True)], ["Ih", "val"], ["!K1"], "kd")
             tt(U1, U1, T.km[:, t:t + 256], A.mult, ["!K1", "km"], ["!K1"], 256, 1.0, "kd")
         else:
-            tt(T.val[:], T.nbr[:].indirect(m[0]), useT, A.subtract, ["nbr", m[1], "useF"], ["val"], 256, GA, "val")
+            tt(T.val[:], T.nbr[:].indirect(m[0]), useT, A.subtract, ["nbr", "useF"] + m[1], ["val"], 256, GA, "val")
             tt(U1, T.val[:], T.km[:, t:t + 256], A.mult, ["val", "km"], ["!K1"], 256, 2.0, "kd")
-        far("L", T.EU1, "EU1", OPT["far"], OPT["tail"], mv, "meaS", T.aE1, D1, "bo", True)
-        both(T.cA[:, 0:256], T.useQ[:, 512 * t:512 * t + 512].indirect(T.cl[:, 16 * t:16 * t + 16]), ["QU%d" % t, "cl%d" % t], ["cA"], 256, "cA")
-        both(T.old[:], T.morS[:].indirect(off), ["mor", "of%d" % t], ["old"], 256, "old")
+        far("L", T.EU1, "EU1.%d", OPT["far"], OPT["tail"], mv, "meaS", T.aE1, D1, "bo", True)
+        both(T.old[:], mor.indirect(off), ["mor", "of%d" % t], ["old"], 256, "old")
         P(512, [(U2, Ib, mv, True, False), (U2, nIb, T.old[:], False, True)], ["Ib", "nIb", "meaS", "old"], ["!K2"], "dmo")
         ts(got, D1, nm, A.is_lt, ["!DD", nmR], ["got"], 256, label="ad1")
+        after("P0", "M2")
         scan(T.cum[:], T.oneb[:, 0:PAD], T.got[:], A.add, A.subtract, ["oneb", "got", "gotpad"], ["cum"], PAD, 0.5, "cum")
         for c in range(NS):
             S(PAD + 20, lambda e, c=c: e.activation(T.junk[:, PAD * c:PAD * c + PAD], T.cum[:], F.Sign, bias=T.sc[:, 4 + c:5 + c], scale=-1.0, accum_out=T.cnt[:, c:c + 1]),
@@ -459,42 +548,64 @@ def rank_program(g, core, T, topo):
             send_use(t + 1)
             own_lists(t + 1)
         ask(t)
+        tt(T.d1[:], U2, got, A.mult, ["!K2", "got"], ["d1"], 256, 1.0, "d1")
+        of2, z, s12, U4 = T.sel[:, 4:8], T.qi[:, 32:36], T.qi[:, 48:52], T.DD[:, 384:448]
+        mv2 = T.mvx[:, 0::2]
+        P(128, [(T.DF[0:64, 0:128], mv2, T.w128[:], True, True)], ["mv2", "w128"], ["!DF"], "of2")
+        tt(T.LT3[0:64, :], T.DF[0:64, 0:128], T.km[0:64, 0:128], A.mult, ["!DF", "km"], ["LT3"], 128, 1.0, "of2")
+        P(256, [(T.DF[:, 0:4], T.LT3[0:64, :], T.b8[0:64, 0:4], True, True)], ["LT3", "b8"], ["!DF"], "of2")
+        ts(z, T.DF[:, 0:4], float(t), A.add, ["!DF"], ["z"], 4, label="of2")
+        ts(z, z, 7, A.bitwise_and, ["z"], ["z"], 4, label="of2")
+        ts(s12, sl, 12.0, A.mult, ["sel"], ["s12"], 4, label="of2")
+        tt(z, z, s12, A.add, ["z", "s12"], ["z"], 4, label="of2")
+        tc(of2, z, ["z"], ["of2"], 4, label="of2")
+        both(T.old2[:], T.morS[:].indirect(of2), ["mor", "morpad", "of2"], ["old2"], 64, "of2")
+        P(128, [(U4, Ib, mv2, True, False), (U4, nIb, T.old2[:], False, True)], ["Ib", "nIb", "mv2", "old2"], ["!DD"], "of2")
         if not last:
             own(t + 1)
         win, wR = wide("nbT", tau)
-        both(T.nb2[:], win.indirect(sl), wR + ["sel"], ["nb2"], 64, "nb2")
+        if OPT["p16"]:
+            ts(T.nb2[:], win.indirect(sl), -1024.0, A.add, wR + ["sel"], ["nb2"], 64, GA, "nb2")
+        else:
+            both(T.nb2[:], win.indirect(sl), wR + ["sel"], ["nb2"], 64, "nb2")
         both(T.ad2[:], T.ad[:].indirect(sl), ["gapD.0", "adpad", "sel"], ["ad2"], 64, "ad2")
         P(64, [(D2, T.nbo[:], T.ad2[:], True, False)], ["nbo", "ad2"], ["!DD"], "delta")
-        tt(T.EP2[:], T.PQ[:, PW * t:PW * t + 1024].indirect(T.mu[:, 32:36]), T.nb2[:], A.max, ["QP%d" % t, "mu2", "nb2"], ["EP2"], 64, GA, "E2")
-        act(T.E2[:], T.EP2[:], ["EP2"], ["E2"], 64, F.Abs, label="E2")
+        if OPT["p16"]:
+            tt(T.EP2[:], T.PQ[:].indirect(T.mu[:, 32:36]), T.nb2[:], A.max, ["PQ", "mu2", "nb2"], ["EP2"], 64, GA, "E2")
+            S(64, lambda e: e.activation(T.E2[:], T.EP2[:], F.Abs, bias=T.sc[:, 1:2]), ["EP2", "k1"], ["E2"], 1.0, "E2")
+        else:
+            tt(T.EP2[:], T.PQ[:, 1024 * t:1024 * t + 1024].indirect(T.mu[:, 32:36]), T.nb2[:], A.max, ["QP%d" % t, "mu2", "nb2"], ["EP2"], 64, GA, "E2")
+            act(T.E2[:], T.EP2[:], ["EP2"], ["E2"], 64, F.Abs, label="E2")
         tc(T.EU2[:], T.E2[:], ["E2"], ["EU2"], 64, label="E2")
-        far("2", T.EU2, "EU2", (32, 32), 0, T.mv2, "mv2", T.aE2, D2, "bo", True)
-        tc(T.EE[:].indirect(sl), T.E2[:], ["E2", "sel", "EEpad"], ["EE"], 64, SC, "EE")
+        after("U%d" % (t + 1))
+        far("2", T.EU2, "EU2", (32, 32), 2, mv2, "mv2", T.aE2, D2, "bo", True)
+        tc(T.EE[:].indirect(sl), T.E2[:], ["E2", "sel", "EEpad"], EE, 64, SC, "EE")
         if not last:
             if OPT["neq"] == "P":
-                P(1024, halves(U3, If, E, False, True), ["If", "EE"], ["!NN"], "P")
+                P(1024, halves(U3, If, E, False, True), ["If"] + EE, ["!NN"], "P")
                 act(T.ab[:], U3, ["!NN"], ["ab"], 256, F.Abs, label="P")
             else:
-                tt(T.ab[:], E, T.basI[:, tau::4], A.not_equal, ["EE", "basI"], ["ab"], 256, label="P")
+                tt(T.ab[:], E, T.basI[:, tau::4], A.not_equal, EE + ["basI"], ["ab"], 256, label="P")
             P(512, [(Lo, T.k15[0:1, :], row, True, False), (Lo, T.nH[0:1, :], row, False, False)], ["k15", "nH", "oneb"], ["!NN"], "P")
             P(256, [(Lo, T.tri[:], T.ab[:], False, False)], ["tri", "ab"], ["!NN"], "P")
+        tt(mor.indirect(off), T.d1[:], T.old[:], A.add, ["d1", "old", "of%d" % t], ["mor"], 256, SC, "mor1")
         ts(T.got2[:], D2, nm, A.is_lt, ["!DD", nmR], ["got2"], 64, label="got")
+        tt(T.d2[:], T.got2[:], U4, A.mult, ["!DD", "got2"], ["d2"], 64, 1.0, "got")
+        tt(T.morS[:].indirect(of2), T.d2[:], T.old2[:], A.add, ["d2", "old2", "of2", "morpad"], ["mor"], 64, SC, "got")
         tc(T.got[:].indirect(sl), T.got2[:], ["got2", "sel", "gotpad"], ["got"], 64, SC, "got")
-        tt(T.d1[:], U2, got, A.mult, ["!K2", "got"], ["d1"], 256, 1.0, "got")
-        tt(T.morS[:].indirect(off), T.d1[:], T.old[:], A.add, ["d1", "old", "of%d" % t], ["mor"], 256, SC, "got")
         P(256 * (1 + last), [(Lo, T.IH[:], got, False, i == last) for i in range(1 + last)], ["IH", "got"], ["!NN"], "P2")
         P(256, [(Hi, T.nIH[:], got, False, True)], ["nIH", "got"], ["!HI"], "P2")
-        tt(T.xm[:], E, Lo, A.min, ["EE", "!NN"], ["xm"], 256, 1.0, "P2")
+        tt(T.xm[:], E, Lo, A.min, EE + ["!NN"], ["xm"], 256, 1.0, "P2")
         tt(keep, T.xm[:], Hi, A.max, ["xm", "!HI"], keepR, 256, 1.0, "P2")
         if last:
-            store(T.ym[:], T.morS[:], ["mor"], 4.0)
+            store(T.ym[:], mor, ["mor"], 4.0)
             store(T.yd[:], T.ydS[:], ["yd%d" % x for x in range(4)], 3.5)
             return
         send_P(t + 1)
         decode(tau)
         if t == 0:
-            tc(T.D16[:, 0:256], T.ydS[:, 0::4], ["yd0"], ["D16_0"], 256, label="D16n")
-        S(84, lambda e: e.activation(T.aE2[:], T.got2[:], F.Copy, accum_out=T.cnt[:, 4:5]), ["got2"], ["n2", "gap2.0"], 1.0, "margin")
+            (gcopy if OPT["gconv"] else tc)(T.D16[:, 0:256], T.ydS[:, 0::4], ["yd0"], ["D16_0"], 256, label="D16n")
+        S(84, lambda e: e.activation(T.aE2[:], T.got2[:], F.Copy, accum_out=T.cnt[:, 4:5]), ["got2"], ["n2", "gap2.1"], 1.0, "margin")
         P(320, [(T.DD[:, 320:321], T.no16[:], T.cum[:, 255:256], True, False), (T.DD[:, 320:321], T.o16[:], T.cnt[:, 4:5], False, True)],
           ["o16", "no16", "cum", "n2"], ["!DD"], "margin")
         ts(T.qi[:, 224:225], T.DD[:, 320:321], 2048.0, A.add, ["!DD"], ["ai"], 1, label="margin")
@@ -574,6 +685,93 @@ def replay(order, where, cost, more, nxt):
     return span
 
 
+def timed(order, where, cost, more, prv, first, known, calm):
+    end, by = (list(known[0]), list(known[1])) if known else ([0.0] * len(cost), [None] * len(cost))
+    last, same = {where[k]: k for k in order[:first]}, -calm
+    for k in order[first:]:
+        s, b, q = 0.0, None, where[k]
+        for a, d in prv[k]:
+            x = end[a] + d
+            if x > s:
+                s, b = x, (a, False)
+        if q != "R":
+            a = last.get(q, -1)
+            if a >= 0 and end[a] >= s:
+                s, b = end[a], (a, True)
+            last[q] = k
+            if q == "S":
+                s += more[k]
+        s += cost[k]
+        same = same + 1 if s == end[k] else 0
+        end[k], by[k] = s, b
+        if same > 80:
+            break
+    return end, by
+
+
+def polish(order, where, costs, more, nxt, prv, prvs, qs, rng):
+    m = len(order)
+    order = [k for k in order if k != m - 1] + [m - 1]
+
+    def value(o, w, first, old, calm):
+        runs = [timed(o, w, c, more, p, first, x, calm) for c, p, x in zip(costs, prvs, old)]
+        return sum(r[0][m - 1] for r in runs), runs
+    val, runs = value(order, where, 0, [None] * len(costs), m)
+    best = (val, order, where)
+    steps = OPT["steps"]
+    for i in range(steps):
+        end, by = runs[int(rng.integers(0, len(runs)))]
+        k, pairs = m - 1, []
+        while by[k] is not None:
+            if by[k][1]:
+                pairs.append((by[k][0], k))
+            k = by[k][0]
+        if not pairs:
+            break
+        u, v = pairs[int(rng.integers(0, len(pairs)))]
+        r, o2, w2 = rng.random(), order, where
+        if r < 0.25:
+            x = u if r < 0.15 else v
+            if len(qs[x]) < 2:
+                continue
+            w2 = list(where)
+            w2[x] = "S" if where[x] == "V" else "V"
+            pu = pv = order.index(x)
+        elif r > 0.85:
+            pv = order.index(u)
+            pu = max([order.index(a) + 1 for a, _ in prv[u]] + [0])
+            if pu >= pv:
+                continue
+            pu += int(rng.integers(0, pv - pu)) * (r > 0.92)
+            o2 = order[:pu] + [u] + order[pu:pv] + order[pv + 1:]
+        else:
+            pu, pv = order.index(u), order.index(v)
+            if r < 0.6:
+                pu = max(0, pu - int(rng.integers(0, 12)) * (r < 0.35))
+                need, mid = {v}, order[pu:pv + 1]
+                for x in reversed(mid):
+                    if x in need:
+                        need.update(a for a, _ in prv[x])
+                if u in need:
+                    continue
+                o2 = order[:pu] + [x for x in mid if x in need] + [x for x in mid if x not in need] + order[pv + 1:]
+            else:
+                pv = min(m - 2, pv + int(rng.integers(0, 25)) * (r > 0.75))
+                late, mid = {u}, order[pu:pv + 1]
+                for x in mid:
+                    if x in late:
+                        late.update(b for b, _ in nxt[x])
+                if v in late:
+                    continue
+                o2 = order[:pu] + [x for x in mid if x not in late] + [x for x in mid if x in late] + order[pv + 1:]
+        v2, r2 = value(o2, w2, pu, runs, pv - pu if i % 50 else m)
+        if v2 <= val + rng.exponential(OPT["temp"]) * (1.0 - i / steps):
+            val, runs, order, where = v2, r2, o2, w2
+            if val < best[0]:
+                best = (val, order, where)
+    return best[1], best[2]
+
+
 def find_order(ops):
     m = len(ops) + 1
     nxt, prv = [[] for _ in range(m)], [[] for _ in range(m)]
@@ -585,7 +783,9 @@ def find_order(ops):
         if o["wake"]:
             nxt[k].append((m - 1, o["wake"]))
             prv[m - 1].append((k, o["wake"]))
-    costs = [[(o["cost"] + o["gat"] * (ga - GA)) * (f if o["q"] in "VSPG" else 1.0) for o in ops] + [0.0] for ga, f in ((GA, 1.0), (1.2, 0.92), (1.8, 1.2))]
+    costs = [[(o["cost"] + o["gat"] * (ga - GA) + fix * (o["q"] in "VS")) * (fp if o["q"] == "P" else f if o["q"] in "VSG" else OPT["far_links"] if o["q"] == "R" else 1.0)
+              for o in ops] + [0.0] for ga, f, fp, fix, _ in OPT["models"]]
+    prvs = [[[(a, d + dw * (d > 0.0)) for a, d in p] for p in prv] for _, _, _, _, dw in OPT["models"]]
     cost, more = costs[0], [o["more"] for o in ops] + [0.0]
     qs = [("V", "S") if o["q"] == "VS" else (o["q"],) for o in ops] + [("R",)]
     due = [0.0] * m
@@ -619,7 +819,8 @@ def find_order(ops):
             cur, due, lag = new, d2, l2
             if cur[0] < top[0]:
                 top = cur
-    top = (top[1], top[4], top[3])
+    order, where = polish(top[1], top[3], costs, more, nxt, prv, prvs, qs, rng)
+    top = (order, replay(order, where, cost, more, nxt), where)
     return [k for k in top[0] if k < m - 1], top[1], top[2]
 
 

@@ -6,10 +6,10 @@ BIG = float(2 ** 23)
 HUGE = float(2 ** 30)
 ROUND = 1.5 * 2 ** 34
 PAD = 256 + CAP
-OPT = {"far": (64, 64, 64, 32, 32), "farD": (64, 64, 64, 32, 32), "cand": (32,) * 8, "spath": (4, 5, 6, 7), "spath0": (4, 5, 6, 7), "vl": 128, "relu2": (), "p16": False, "far_links": 1.2,
-       "models": ((1.4, 0.93, 0.85, -0.01, 0.03), (1.7, 1.1, 1.4, 0.01, -0.04)), "dec": "P", "gconv": True,
-       "lists": [([0], [0]), ([0, 1, 2, 3], [1, 2, 3, 4])], "tail": 1, "ns": 3, "neq": "V", "kd": "P",
-       "vf": 0.04, "sf": 0.07, "pe": 0.6e-3, "wake": 0.16, "look": 0.2, "lag": 0.7, "tries": 100, "seed": 1, "noise": 0.4, "heat": 1.0, "steps": 140000, "temp": 0.35}
+OPT = {"far": (64, 64, 64, 32, 32), "farD": (64, 64, 64, 64), "cand": (32,) * 8, "spath": (4, 5, 6, 7), "spath0": (4, 5, 6, 7), "vl": 128, "relu2": (4,), "p16": False, "far_links": 1.2,
+       "models": ((1.4, 0.93, 0.9, -0.01, 0.05), (1.7, 1.1, 1.4, 0.01, -0.02)), "dec": "P", "relu1": True, "bits": True, "g2": False, "gconv": True,
+       "lists": [([0], [0]), ([0, 1, 2, 3], [1, 2, 3, 4])], "tail": 1, "ns": 3, "neq": "P", "kd": "P",
+       "vf": 0.04, "sf": 0.07, "pe": 0.6e-3, "wake": 0.16, "look": 0.2, "lag": 0.7, "tries": 100, "seed": 1, "noise": 0.4, "heat": 1.0, "steps": 250000, "temp": 0.35, "mean": 0.3, "starts": 3, "short": 5000}
 
 SCRATCH = {}
 
@@ -44,14 +44,13 @@ _b("cU2 EU2 mu", 64, "uint16")
 _b("sel", 8, "uint16")
 _b("EP1 xm mk8", 256)
 _b("cF1 val", 256, "float16")
-_b("SS", 384)
+_b("SS ZI", 384, "int32")
 _b("ZB LT", 408, "float16")
 _b("th", 128, "bfloat16")
 _b("Ih", 128 + 16, "float16")
 _b("cF2", 64, "float16")
-_b("hi", 32)
 _b("EE", PAD)
-_b("cA", PAD * RO)
+_b("cA", 256 * RO + CAP)
 _b("cS", 512)
 _b("clQ", 256, "uint16")
 if OPT["p16"]:
@@ -68,7 +67,7 @@ _b("le lc mseg", 2 * PAD, "bfloat16")
 _b("junk", 4 * PAD, "bfloat16")
 _b("ad2 aE2 got2 old2 d2", 64, "bfloat16")
 _b("n8k Ib nIb IB IH nIH nH no16 tmb bo bo2 nbo w128 tri k15", 128, "bfloat16")
-_b("W8 w8t", 8, "bfloat16")
+_b("W8 nW8 w8t", 8, "bfloat16")
 _b("RR", 16)
 _b("km", 260)
 _b("ikm", 260, "int32")
@@ -81,6 +80,7 @@ for _n in ["M%d" % d for d in (1, 2, 3)] + ["C%d" % d for d in range(4)] + ["U%d
 
 CY, WAKE = 0.9e-3, 0.08
 GA, SC = 1.4, 3.5
+FIRST = "If ik8 e15 RR c97 w8t lane0 b8h Ih pi"
 FOUND = {}
 
 
@@ -94,6 +94,8 @@ def rank_program(g, core, T, topo):
 
     def op(q, cost, calls, R=(), W=(), sem=None, inc=1, wake=0.0, label="", gat=0.0, more=0.0):
         k = len(ops)
+        if "sel" in R:
+            R = [r for r in R if r != "sel"] + ["selS", "selV"]
         deps = {}
 
         def dep(a, kind):
@@ -114,14 +116,14 @@ def rank_program(g, core, T, topo):
         for w in W:
             lastw[w] = k
             readers[w] = []
-        ops.append({"q": q, "cost": cost, "gat": gat, "more": more, "calls": calls, "deps": deps, "sem": sem, "inc": inc, "wake": wake, "label": label})
+        ops.append({"q": q, "cost": cost, "gat": gat, "more": more, "calls": calls, "deps": deps, "sem": sem, "inc": inc, "wake": wake, "label": label, "out": W[0] if W else ""})
         return k
 
     def V(c, call, R, W, f=1.0, label=""):
         op("V", OPT["vf"] + max(64.0, c * f) * CY, [call], R, W, label=label, gat=c * CY if f == GA else 0.0)
 
     def S(c, call, R, W, f=1.0, label=""):
-        op("S", OPT["sf"] + c * f * CY, [call], R, W, label=label, gat=c * CY if f == GA else 0.0)
+        op("S", OPT["sf"] + max(64.0, c * f) * CY, [call], R, W, label=label, gat=c * CY if f == GA else 0.0)
 
     def P(c, mms, R, W, label="pe"):
         def call(m):
@@ -170,9 +172,10 @@ def rank_program(g, core, T, topo):
     def act(out, in_, R, W, c, func=F.Copy, scale=1.0, f=1.0, label="act"):
         S(c, lambda e: e.activation(out, in_, func, scale=scale), R, W, f, label)
 
-    def both(out, in_, R, W, c, label, f=GA):
-        cv, cs = OPT["vf"] + max(64.0, c * f) * CY, OPT["sf"] + c * max(f, 1.0) * CY
-        op("VS", cv, [(lambda e: e.tensor_copy(out, in_), lambda e: e.activation(out, in_, F.Copy))], R, W, label=label, gat=c * CY if f == GA else 0.0, more=cs - cv)
+    def both(out, in_, R, W, c, label, f=GA, scale=1.0):
+        cv, cs = OPT["vf"] + max(64.0, c * f) * CY, OPT["sf"] + max(64.0, c * max(f, 1.0)) * CY
+        op("VS", cv, [(lambda e: e.tensor_copy(out, in_) if scale == 1.0 else e.tensor_scalar(out, in_, scale, None, A.mult), lambda e: e.activation(out, in_, F.Copy, scale=scale))],
+           R, W, label=label, gat=c * CY if f == GA else 0.0, more=cs - cv)
 
     def store(out, in_, R, us):
         op("Y", 0.1, [lambda e: e.dma_start(out, in_)], R, [], sem="st", inc=16, wake=us, label="out")
@@ -180,19 +183,19 @@ def rank_program(g, core, T, topo):
     def load(qn, i, out, in_, W, us):
         op(qn, 0.1, [lambda e: e.dma_start(out, in_)], (), W, sem="ld%d" % i, inc=16, wake=us, label="load")
     mor = T.morS[:, 0:3072]
-    load("S", 5, T.b15[0:8, :], T.bas[15::16, :], ["b15"], 2.3)
-    load("Y", 1, T.meaS[:], T.mea[:], ["meaS"], 3.2)
-    load("Y", 2, T.useI[:], T.use[:], ["useI"], 4.2)
-    load("Y", 3, T.derI[:], T.der[:], ["derI"], 6.2)
-    load("Y", 0, T.basI[:], T.bas[:], ["basI"], 8.2)
-    load("Y", 4, mor, T.mor[:], ["mor"], 11.0)
+    load("S", 5, T.b15[0:8, :], T.bas[15::16, :], ["b15"], 1.2)
+    load("Y", 1, T.meaS[:], T.mea[:], ["meaS"], 1.8)
+    load("Y", 2, T.useI[:], T.use[:], ["useI"], 2.5)
+    load("Y", 0, T.basI[:], T.bas[:], ["basI"], 4.0)
+    load("Y", 3, T.derI[:], T.der[:], ["derI"], 5.5)
+    load("Y", 4, mor, T.mor[:], ["mor"], 7.8)
     for k in range(1, 6):
         ops[k]["deps"][k - 1] = 0
 
     fill(T.one[:], 1.0, ["one"], 128)
     fill(T.oneb[:], 1.0, ["oneb"], 512)
     sel(T.e15[:], T.one[:, 0:64], [[-1, 8], [0, 8]], A.is_equal, 0, 1, ["one"], ["e15"], 64)
-    tc(T.ydS[0:8, :], T.b15[0:8, :], ["b15"], ["yd0", "yd1", "yd2", "yd3"], 1024, label="B")
+    both(T.ydS[0:8, 0::4], T.b15[0:8, 0::4], ["b15"], ["yd0"], 256, "B", 1.0)
     iota(T.ik8[:], [[0, 32], [-1, 8]], 128, 1, ["ik8"], 256)
     sel(T.RR[:], T.one[:, 0:16], [[-8, 16]], A.is_ge, 0, 1, ["one"], ["RR"], 16)
     sel(T.RR[:], T.RR[:], [[8, 16]], A.is_ge, 7, -1, ["RR"], ["RR"], 16)
@@ -203,6 +206,7 @@ def rank_program(g, core, T, topo):
     sel(T.w8t[:], T.w8t[:], [[16, 8]], A.is_ge, 15, -1, ["w8t"], ["w8t"], 8)
     act(T.W8[:], T.w8t[:], ["w8t"], ["W8"], 8, scale=2048.0)
     act(T.b8[:], T.w8t[:], ["w8t"], ["b8"], 8)
+    act(T.nW8[:], T.w8t[:], ["w8t"], ["nW8"], 8, scale=-2048.0)
     gcopy(T.Ih[:, 128:136], T.w8t[:], ["w8t"], ["b8h"], 8, "gsel")
     gcopy(T.Ih[:, 0:128], T.If[:], ["If"], ["Ih"], 128, "gsel")
     for nm_, sc_ in (("Ib", 1.0), ("IB", BIG), ("nIb", -1.0), ("nIf", -1.0), ("n2If", -2.0), ("IH", HUGE), ("nIH", -HUGE)):
@@ -218,12 +222,11 @@ def rank_program(g, core, T, topo):
         fill(T[nm_][:], x, [nm_], c)
         fill(first, y, [nm_], 64)
     ts(T.ZB[:], T.oneb[:, 0:408], 0.0, A.mult, ["oneb"], ["ZB0", "ZB1", "ZB2"], 408, 0.5)
+    iota(T.ZI[:], [[0, 384]], 0, 0, ["ZI0", "ZI1", "ZI2"], 384)
     ts(T.LT[:, 128::136], T.oneb[:, 0:3], 0.0, A.mult, ["oneb"], ["LTpad"], 3)
     act(T.Ih[:, 136:144], T.w8t[:], ["w8t"], ["nb8h"], 8, scale=-1.0)
-    for t in range(RO):
-        fill(T.cA[:, PAD * t + 256:PAD * t + PAD], 0.0, ["cApad%d" % t], CAP)
-    fill(T.sc[:, 1:2], 1024.0, ["k1"], 1)
-    for nm_, a in (("EE", 256), ("ad", 256), ("got", 256), ("meaT", 1024), ("nbT", 1024)):
+    fill(T.sc[:, 1:2], PAD / 2.0, ["k1"], 1)
+    for nm_, a in (("cA", 256 * RO), ("EE", 256), ("ad", 256), ("got", 256), ("meaT", 1024), ("nbT", 1024)):
         fill(T[nm_][:, a:a + CAP], 0.0, [nm_ + "pad"], CAP)
     qi = [T.qi[:, 16 * i:16 * i + 16] for i in range(16)]
     pw = T.sc[:, 0:1]
@@ -243,7 +246,6 @@ def rank_program(g, core, T, topo):
     act(T.nbo[:], T.bo[:], ["bo"], ["nbo"], 128, scale=-1.0)
     act(T.bo2[:], T.bo[:], ["bo"], ["bo2"], 128, scale=2.0)
     ts(T.w128[:], T.bo[:], pw, A.mult, ["bo", "pw"], ["w128"], 128, 0.5)
-    fill(T.morS[:, 3072:3840], 0.0, ["morpad"], 384)
     sel(T.tmb[:], T.bo[:], [[1, 128]], A.is_ge, 0, -1, ["bo"], ["tmb"], 128)
     act(T.tri[:], T.tmb[:], ["tmb"], ["tri"], 128, scale=8192.0)
     sel(T.tmb[:], T.oneb[:, 0:128], [[0, 8], [1, 16]], A.is_equal, -15, 0, ["oneb"], ["tmb"], 128)
@@ -256,12 +258,16 @@ def rank_program(g, core, T, topo):
     for tau in range(4):
         iota(T.lane[:, 256 * tau:256 * tau + 256], [[4, 256]], tau, 0, ["lane%d" % tau], 256)
     iota(T.nbr[:], [[2, 512], [-1, 2]], 1, 0, ["nbr"], 1024)
+    iota(T.morS[:, 3072:3840], [[0, 768]], 0, 0, ["morpad"], 768)
 
     for tau in range(4):
-        ts(T.nbT[:, 256 * tau:256 * tau + 256], T.basI[:, tau::4], -1.0, A.mult, ["basI"], ["nbT%d" % tau], 256, label="nbT")
+        both(T.nbT[:, 256 * tau:256 * tau + 256], T.basI[:, tau::4], ["basI"], ["nbT%d" % tau], 256, "nbT", 1.0, -1.0)
     (gcopy if OPT["gconv"] else tc)(T.useF[:], T.useI[:], ["useI"], ["useF"], 512, label="useF")
     for tau in range(4):
-        (gcopy if OPT["gconv"] and tau else tc)(T.D16[:, 256 * tau:256 * tau + 256], T.derI[:, tau::4], ["derI"], ["D16_%d" % tau], 256, label="D16")
+        if tau:
+            gcopy(T.D16[:, 256 * tau:256 * tau + 256], T.derI[:, tau::4], ["derI"], ["D16_%d" % tau], 256, "D16")
+        else:
+            both(T.D16[:, 0:256], T.derI[:, 0::4], ["derI"], ["D16_0"], 256, "D16", 1.0)
         gcopy(T.meaT[:, 256 * tau:256 * tau + 256], T.meaS[:, tau::4], ["meaS"], ["meaT%d" % tau], 256, "meaT")
 
     def wide(nm_, tau):
@@ -285,7 +291,7 @@ def rank_program(g, core, T, topo):
     Ph = ["Ph0", "Ph1"]
     for hf in range(2):
         c0 = slice(512 * hf, 512 * hf + 512)
-        bank = ("NN", "DF")[hf]
+        bank = ("NN", "DD")[hf]
         P(2048, [(T[bank][:, tau::4], T.nIf[:], T.nbT[:, 256 * tau + 128 * hf:256 * tau + 128 * hf + 128], tau == 0, tau == 3) for tau in range(4)],
           ["nIf"] + ["nbT%d" % tau for tau in range(4)], ["!" + bank])
         tt(T.neq[:, c0], T.derI[:, c0], T[bank][:], A.not_equal, ["!" + bank, "derI"], ["neq%d" % hf], 512, 1.0, "neq")
@@ -316,7 +322,7 @@ def rank_program(g, core, T, topo):
         tt(T.qc[:, c], T.qd[:, c], T.t12[:, c], A.add, ["qd", "t12"], ["qc"], w, label="Z")
         tc(T.of[:, c], T.qc[:, c], ["qc"], ["of%d" % t for t in rounds], w, label="Z")
 
-    sent, issued = {}, {}
+    sent, issued, line = {}, {}, [0, 0]
 
     def send(d, buf, in_, name, R, us):
         to, frm = T.cores[(rank - d) % n], T.cores[(rank + d) % n]
@@ -324,12 +330,12 @@ def rank_program(g, core, T, topo):
         mask = topo.mask(core, to)
         sent["s" + name] = len(topo.engines(core, to))
         k = op("G", 0.7 if len(sent) > 1 else 3.5, [lambda e: e.remote_dma(buf, in_, sm["a" + name], sm["s" + name], pid, rid, mask)], R, (), sem="s" + name, inc=0, wake=us, label="send")
-        j = op("R", us, [], (), ["Q" + name], sem="a" + name, inc=len(topo.engines(frm, core)), label="arrive")
+        j = op("R", us - 2.5, [], (), ["Q" + name], sem="a" + name, inc=len(topo.engines(frm, core)), wake=2.5, label="arrive")
         ops[j]["deps"][k] = 0
-        issued[name] = k
-        for a in early:
-            if ops[a]["q"] == "G":
-                ops[k]["deps"].setdefault(a, 0)
+        if issued:
+            ops[k]["deps"].setdefault(line[0], 0)
+            ops[j]["deps"].setdefault(line[1], 0)
+        issued[name], line[0], line[1] = k, k, j
 
     def after(*names):
         for x in names:
@@ -338,13 +344,13 @@ def rank_program(g, core, T, topo):
 
     def send_classes(j):
         c = slice(16, 80) if j else slice(0, 16)
-        send(-max(j, 1), T.clQ[:, 64 * j:64 * j + c.stop - c.start], T.cl[:, c], "C%d" % j, ["cl%d" % t for t in range(RO) if (t > 0) == (j > 0)], 3.0)
+        send(-max(j, 1), T.clQ[:, 64 * j:64 * j + c.stop - c.start], T.cl[:, c], "C%d" % j, ["cl%d" % t for t in range(RO) if (t > 0) == (j > 0)], 3.2)
 
     def send_use(t):
         d, s = 1 + t % 3, T.cS[:, 256 * (t % 2):256 * (t % 2) + 256]
         lst = T.clQ[:, 64 * d + 16 * t - 16:64 * d + 16 * t] if t else T.clQ[:, 0:16]
         both(s, T.useF[:].indirect(lst), ["useF", "QC%d" % (d if t else 0)], ["cS%d" % (t % 2)], 256, "cA")
-        send(d, T.cA[:, PAD * t:PAD * t + 256], s, "U%d" % t, ["cS%d" % (t % 2)], 4.5)
+        send(d, T.cA[:, 1024 - 256 * t:1280 - 256 * t], s, "U%d" % t, ["cS%d" % (t % 2)], 4.5)
 
     def send_P(t):
         if OPT["p16"]:
@@ -358,7 +364,7 @@ def rank_program(g, core, T, topo):
     def send_mea(d):
         send(d, T.meaQ[:, 1024 * d - 1024:1024 * d], T.meaS[:], "M%d" % d, ["meaS"], 6.0)
 
-    flip = [0]
+    flip, last_v, first_v = [0], [0], [0]
 
     def cands(c, cuts, spath, mea, meaR, rep, repR, own):
         cU, dd, aa = T["cU" + c], T["dd" + c], T["aa" + c]
@@ -380,20 +386,27 @@ def rank_program(g, core, T, topo):
                 act(aa[:, a:b], o, ["!" + bank], aR, b - a, F.Abs, label="scand" + c)
             else:
                 tt(dd[:, a:b], src, rep[:, a:b], A.subtract, [meaR, "cU" + c] + repR, [dR], b - a, GA, "cand" + c)
-                act(aa[:, a:b], dd[:, a:b], [dR], aR, b - a, F.Abs, label="abs" + c)
+                if OPT["relu1"]:
+                    cv, cs = OPT["vf"] + 0.5 * (b - a) * CY, OPT["sf"] + (b - a) * CY
+                    op("VS", cv, [(lambda e, a=a, b=b: e.tensor_scalar(aa[:, a:b], dd[:, a:b], 0.0, 2.0, A.max, A.mult),
+                                   lambda e, a=a, b=b: e.activation(aa[:, a:b], dd[:, a:b], F.Relu, scale=2.0))], [dR], aR, label="abs" + c, more=cs - cv)
+                else:
+                    act(aa[:, a:b], dd[:, a:b], [dR], aR, b - a, F.Abs, label="abs" + c)
+                last_v[0] = len(ops) - 2
+                first_v[0] = first_v[0] or len(ops) - 2
 
     def least(j, bank, p, out, outW):
         K, c, lb = T[bank], slice(128 * j, 128 * j + 128), "min%d" % (j // 2 + 1)
         c0, c1 = slice(136 * j, 136 * j + 128), slice(136 * j + 1, 136 * j + 129)
-        SS, ZB, LT, hi = T.SS[0:p, c], T.ZB[0:p, c0], T.LT[0:p, c0], T.hi[0:p, 8 * j:8 * j + 8]
+        SS, ZB, LT, ZI = T.SS[0:p, c], T.ZB[0:p, c0], T.LT[0:p, c0], T.ZI[0:p, c]
         scan(SS, T.mbig[0:p, :], K[0:p, 0:128], A.max, A.min, ["!" + bank, "mbig"], ["SS%d" % j], 128, 1.0, lb)
-        ts(hi, SS[:, 15::16], ROUND, A.add, ["SS%d" % j], ["hi%d" % j], 8, label=lb, s2=ROUND, op1=A.subtract)
-        tt(ZB[:, 0::16], SS[:, 15::16], hi, A.subtract, ["SS%d" % j, "hi%d" % j], ["ZB%d" % j], 8, label=lb)
-        scan(LT, T.th[0:p, :], ZB, A.mult, A.add, ["ZB%d" % j, "th"], ["LT%d" % j], 128, 0.5, lb)
+        ts(ZI[:, 0::16], SS[:, 15::16], 1023, A.bitwise_and, ["SS%d" % j], ["ZI%d" % j], 8, label=lb)
+        both(ZB[:, 0::16], ZI[:, 0::16], ["ZI%d" % j], ["ZB%d" % j], 8, lb, 1.0)
+        scan(LT, T.th[0:p, :], ZI, A.mult, A.add, ["ZI%d" % j, "th"], ["LT%d" % j], 128, 1.0, lb)
         o, pos, neg = K[:, 0:p // 16], T.Ih[0:p, 128:128 + p // 16], T.Ih[0:p, 136:136 + p // 16]
         P(64, [(o, T.ZB[0:p, c1], pos, True, False)], ["ZB%d" % j, "b8h"], ["!" + bank], lb)
         P(128, [(o, LT, pos, False, False), (o, T.LT[0:p, c1], neg, False, True)], ["LT%d" % j, "b8h", "nb8h", "LTpad"], ["!" + bank], lb)
-        tc(out, K[:, 0:p // 16], ["!" + bank], [outW], 8, label=lb)
+        both(out, K[:, 0:p // 16], ["!" + bank], [outW], 8, lb, 1.0)
 
     def mu(t):
         return T.mu[:, 16 * (t % 2):16 * (t % 2) + 16], ["mu%d.%d" % (t % 2, h) for h in range(2)]
@@ -401,10 +414,11 @@ def rank_program(g, core, T, topo):
     def own_lists(t):
         tau = t % 4
         use, cl, clR = T.useF[:] if t else T.useI[:], T.cl[:, 16 * t:16 * t + 16], ["useF" if t else "useI", "cl%d" % t]
-        tc(T.cU1[:], use.indirect(cl), clR, ["cU1"], 256, GA, "cU1")
-        both(T.cF1[:], use.indirect(cl), clR, ["cF1"], 256, "cF1")
-        for a in early if t == 0 else ():
-            ops[-1]["deps"].setdefault(a, 0)
+        both(T.cU1[:], use.indirect(cl), clR, ["cU1"], 256, "cU1")
+        if t:
+            gcopy(T.cF1[:], T.cU1[:], ["cU1"], ["cF1"], 256, "cF1")
+        else:
+            both(T.cF1[:], T.cU1[:], ["cU1"], ["cF1"], 256, "cF1", 0.5)
         tt(T.eq[:], use.indirect(cl), T.lane[:, 256 * tau:256 * tau + 256], A.is_equal, clR + ["lane%d" % tau], ["eq"], 256, GA, "eq")
 
     def own(t):
@@ -413,6 +427,8 @@ def rank_program(g, core, T, topo):
         for h, bank in enumerate(("K1", "DF")):
             K, c = T[bank], slice(128 * h, 128 * h + 128)
             P(256, [(K[:, 0:128], T.cF1[:, c], T.Ih[:, 0:128], True, False), (K[:, 0:128], T.eq[:, c], T.IB[:], False, False)], ["cF1", "Ih", "eq", "IB"], ["!" + bank], "keys1")
+            if OPT["relu1"] and h == 0:
+                P(1024, [(K[:, k:128:16], T.dd1[:, k:2048:16], T.nW8[:], False, False) for k in range(16)], ["nW8"] + ["dd1.%d" % x for x in range(4)], ["!" + bank], "keys1")
             P(1024, [(K[:, k:128:16], T.aa1[:, 2048 * h + k:2048 * h + 2048:16], T.W8[:], False, k == 15) for k in range(16)],
               ["W8"] + ["aa1.%d" % x for x in range(8 * h, 8 * h + 8)], ["!" + bank], "keys1")
             least(h, bank, 128, mu(t)[0][:, 8 * h:8 * h + 8], mu(t)[1][h])
@@ -420,12 +436,15 @@ def rank_program(g, core, T, topo):
     def ask(t):
         tau, d, K = t % 4, 1 + t % 3, T.K2
         sl, mea, mv2 = T.sel[:, 0:4], T.meaQ[:, 1024 * d - 1024:1024 * d], T.mvx[:, 0::2]
-        cA, cR = T.cA[:, PAD * t:PAD * t + PAD], ["QU%d" % t, "cApad%d" % t, "sel"]
-        tc(T.cU2[:], cA.indirect(sl), cR, ["cU2"], 64, GA, "cU2")
+        cA, cR = T.cA[:, 1024 - 256 * t:1024 - 256 * t + PAD], ["QU%d" % t, "QU%d" % (t - 1) if t else "cApad", "sel"]
+        both(T.cU2[:], cA.indirect(sl), cR, ["cU2"], 64, "cU2")
         win, wR = wide("meaT", tau)
         both(mv2, win.indirect(sl), wR + ["sel"], ["mv2"], 64, "mv2")
-        both(T.mvx[:, 1::2], win.indirect(sl), wR + ["sel"], ["mv3"], 64, "mv2")
-        both(T.cF2[:], cA.indirect(sl), cR, ["cF2"], 64, "cF2")
+        if OPT["g2"]:
+            gcopy(T.mvx[:, 1::2], mv2, ["mv2"], ["mv3"], 64, "mv2")
+        else:
+            both(T.mvx[:, 1::2], win.indirect(sl), wR + ["sel"], ["mv3"], 64, "mv2")
+        both(T.cF2[:], T.cU2[:], ["cU2"], ["cF2"], 64, "cF2", 0.5)
         P(128, [(K[0:64, 0:128], T.cF2[:], T.Ih[:, 0:128], True, False)], ["cF2", "Ih"], ["!K2"], "keys2")
         for h, bank in enumerate(("CC", "WW")):
             B, c = T[bank], slice(512 * h, 512 * h + 512)
@@ -433,7 +452,7 @@ def rank_program(g, core, T, topo):
             P(512, [(B[:, k::8], T.nIb[:], T.mvx[:, 64 * h:64 * h + 64], k == 0, False) for k in range(8)], ["nIb", "mv2", "mv3"], ["!" + bank], "cand2")
             P(512, [(B[:], T.Ib[:], T.dd2[:, c], False, True)], ["Ib", "dd2.%d" % h], ["!" + bank], "cand2")
             o = [K[32 * h:32 * h + 32, k:128:16] for k in range(16)]
-            if h in OPT["relu2"]:
+            if h == 0 and t in OPT["relu2"]:
                 P(512, [(o[k], T.dd2[:, 512 * h + k:512 * h + 512:16], T.nW8[:], False, False) for k in range(16)], ["nW8", "dd2.%d" % h], ["!K2"], "keys2")
                 ts(T.aa2[:, c], B[:], 0.0, A.max, ["!" + bank], ["aa2.%d" % h], 512, label="abs2", s2=2.0, op1=A.mult)
             else:
@@ -470,22 +489,31 @@ def rank_program(g, core, T, topo):
             tt(T.xm[:], x, T.nbT[:, 256 * tau:256 * tau + 256], A.max, Ph + ["nbT%d" % tau], ["xm"], 256, label="dec")
             act(T.ydS[:, tau::4], T.xm[:], ["xm"], ["yd%d" % tau], 256, F.Abs, label="dec")
             return
-        P(2304, halves(o, T.nIf[:], T.nbT[:, 256 * tau:256 * tau + 256], True, False) + [(o, T.n8k[0:1, :], T.oneb[0:1, 0:256], False, False)], ["nIf", "n8k", "oneb", "nbT%d" % tau], ["!DF"], "dec")
+        P(1280, halves(o, T.nIf[:], T.nbT[:, 256 * tau:256 * tau + 256], True, False) + [(o, T.n8k[0:1, :], T.oneb[0:1, 0:256], False, False)], ["nIf", "n8k", "oneb", "nbT%d" % tau], ["!DF"], "dec")
         P(1024, halves(o, T.n2If[:], x, False, True), ["n2If"] + Ph, ["!DF"], "dec")
         tt(T.ydS[:, tau::4], x, o, A.max, Ph + ["!DF"], ["yd%d" % tau], 256, 1.0, "dec")
 
-    for taus, rounds in OPT["lists"]:
-        lists(taus, rounds, "WW")
+    lists([0], [0], "WW")
+    send_classes(0)
     send_mea(1)
-    for j in range(4):
-        send_classes(j)
-        after("M1")
-        ops[-2]["deps"][issued["M1"]] = 0
-    send_use(0)
     send_P(0)
     own_lists(0)
+    k = len(ops)
     own(0)
+    ops[last_v[0]]["deps"].update({k - 1: 0, k - 2: 0})
+    k = len(ops)
+    send_use(0)
+    ops[k]["deps"][k - 1] = 0
+    for tau in range(1, 4):
+        gcopy(T.ydS[0:8, tau::4], T.b15[0:8, tau::4], ["b15"], ["yd%d" % tau], 256, "B")
+    k = len(ops)
+    lists([0, 1, 2, 3], [1, 2, 3, 4], "HI")
     places([0, 1, 2, 3], [0, 1, 2, 3, 4], "K2")
+    for x in ops[k:]:
+        if x["q"] == "V":
+            x["deps"].setdefault(last_v[0], 0)
+    for j in range(1, 4):
+        send_classes(j)
     send_mea(2)
     mvrep(1)
     send_mea(3)
@@ -513,9 +541,11 @@ def rank_program(g, core, T, topo):
         for h in range(2):
             c = slice(128 * h, 128 * h + 128)
             tt(T.EP1[:, c], T.Pt[:, 0:1024].indirect(m[0][:, 8 * h:8 * h + 8]), nb[:, c], A.max, Ph + [m[1][h], nbR], ["EP1.%d" % h], 128, GA, "E1")
-            act(E[:, c], T.EP1[:, c], ["EP1.%d" % h], [EE[h]], 128, F.Abs, label="E1")
-            tc(T.EU1[:, c], E[:, c], [EE[h]], ["EU1.%d" % h], 128, label="E1")
-        after(*(["P%d" % t, "M3"] if t else ["U0", "M1", "C1", "C2", "C3"]))
+            act(T.EU1[:, c], T.EP1[:, c], ["EP1.%d" % h], ["EU1.%d" % h], 128, F.Abs, label="E1")
+        gcopy(E, T.EU1[:], ["EU1.0", "EU1.1"], EE, 256, "EG")
+        ops.append(ops.pop())
+        for x in ["P%d" % t, "M3"] if t else []:
+            ops[-2]["deps"].setdefault(issued[x], 0)
         useT = T.useF[:, 37 * t:37 * t + 256]
         if OPT["kd"] == "P":
             both(T.val[:], T.nbr[:].indirect(m[0]), ["nbr"] + m[1], ["val"], 256, "val")
@@ -529,7 +559,7 @@ def rank_program(g, core, T, topo):
         both(T.old[:], mor.indirect(off), ["mor", "of%d" % t], ["old"], 256, "old")
         P(512, [(U2, Ib, mv, True, False), (U2, nIb, T.old[:], False, True)], ["Ib", "nIb", "meaS", "old"], ["!K2"], "dmo")
         ts(got, D1, nm, A.is_lt, ["!DD", nmR], ["got"], 256, label="ad1")
-        after("P0", "M2")
+        after("P0")
         scan(T.cum[:], T.oneb[:, 0:PAD], T.got[:], A.add, A.subtract, ["oneb", "got", "gotpad"], ["cum"], PAD, 0.5, "cum")
         for c in range(NS):
             S(PAD + 20, lambda e, c=c: e.activation(T.junk[:, PAD * c:PAD * c + PAD], T.cum[:], F.Sign, bias=T.sc[:, 4 + c:5 + c], scale=-1.0, accum_out=T.cnt[:, c:c + 1]),
@@ -538,8 +568,10 @@ def rank_program(g, core, T, topo):
             for c in range(NV):
                 ts(T.le[:, PAD * c:PAD * c + PAD], T.cum[:], T.sc[:, 4 + NS + c:5 + NS + c], A.is_lt, ["cum", "sc"], ["le%d" % c], PAD, 0.5, "count", -0.5, A.add)
             scan(T.lc[:, 0:NV * PAD], T.mseg[:, 0:NV * PAD], T.le[:, 0:NV * PAD], A.mult, A.add, ["mseg"] + ["le%d" % c for c in range(NV)], ["lc"], NV * PAD, 0.5, "count")
-            ts(T.sel[:, NS:4], T.lc[:, PAD - 1:NV * PAD:PAD], PAD / 2.0, A.add, ["lc"], ["selV", "sel"], NV, label="count")
-        ts(T.sel[:, 0:NS], T.cnt[:, 0:NS], float(PAD), A.add, ["cnt%d" % c for c in range(NS)] + (["selV"] if NV else []), ["sel"], NS, label="count", s2=0.5, op1=A.mult)
+            ts(T.sel[:, NS:4], T.lc[:, PAD - 1:NV * PAD:PAD], PAD / 2.0, A.add, ["lc"], ["selV"], NV, label="count")
+        op("VS", OPT["vf"] + 64 * CY, [(lambda e: e.tensor_scalar(T.sel[:, 0:NS], T.cnt[:, 0:NS], float(PAD), 0.5, A.add, A.mult),
+                                        lambda e: e.activation(T.sel[:, 0:NS], T.cnt[:, 0:NS], F.Identity, bias=T.sc[:, 1:2], scale=0.5))],
+           ["cnt%d" % c for c in range(NS)] + ["k1"], ["selS"], label="count", more=0.04)
         tt(U1, got, U1, A.mult, ["!K1", "got"], ["!K1"], 256, 1.0, "up")
         tt(useT, useT, U1, A.add, ["useF", "!K1"], ["useF"], 256, 1.0, "up")
         if last:
@@ -549,6 +581,10 @@ def rank_program(g, core, T, topo):
             own_lists(t + 1)
         ask(t)
         tt(T.d1[:], U2, got, A.mult, ["!K2", "got"], ["d1"], 256, 1.0, "d1")
+        if t:
+            decode(t - 1)
+        if t == 1:
+            gcopy(T.D16[:, 0:256], T.ydS[:, 0::4], ["yd0"], ["D16_0"], 256, "D16n")
         of2, z, s12, U4 = T.sel[:, 4:8], T.qi[:, 32:36], T.qi[:, 48:52], T.DD[:, 384:448]
         mv2 = T.mvx[:, 0::2]
         P(128, [(T.DF[0:64, 0:128], mv2, T.w128[:], True, True)], ["mv2", "w128"], ["!DF"], "of2")
@@ -556,9 +592,9 @@ def rank_program(g, core, T, topo):
         P(256, [(T.DF[:, 0:4], T.LT3[0:64, :], T.b8[0:64, 0:4], True, True)], ["LT3", "b8"], ["!DF"], "of2")
         ts(z, T.DF[:, 0:4], float(t), A.add, ["!DF"], ["z"], 4, label="of2")
         ts(z, z, 7, A.bitwise_and, ["z"], ["z"], 4, label="of2")
-        ts(s12, sl, 12.0, A.mult, ["sel"], ["s12"], 4, label="of2")
+        both(s12, sl, ["sel"], ["s12"], 4, "of2", 1.0, 12.0)
         tt(z, z, s12, A.add, ["z", "s12"], ["z"], 4, label="of2")
-        tc(of2, z, ["z"], ["of2"], 4, label="of2")
+        both(of2, z, ["z"], ["of2"], 4, "of2", 1.0)
         both(T.old2[:], T.morS[:].indirect(of2), ["mor", "morpad", "of2"], ["old2"], 64, "of2")
         P(128, [(U4, Ib, mv2, True, False), (U4, nIb, T.old2[:], False, True)], ["Ib", "nIb", "mv2", "old2"], ["!DD"], "of2")
         if not last:
@@ -575,8 +611,8 @@ def rank_program(g, core, T, topo):
             S(64, lambda e: e.activation(T.E2[:], T.EP2[:], F.Abs, bias=T.sc[:, 1:2]), ["EP2", "k1"], ["E2"], 1.0, "E2")
         else:
             tt(T.EP2[:], T.PQ[:, 1024 * t:1024 * t + 1024].indirect(T.mu[:, 32:36]), T.nb2[:], A.max, ["QP%d" % t, "mu2", "nb2"], ["EP2"], 64, GA, "E2")
-            act(T.E2[:], T.EP2[:], ["EP2"], ["E2"], 64, F.Abs, label="E2")
-        tc(T.EU2[:], T.E2[:], ["E2"], ["EU2"], 64, label="E2")
+            act(T.EU2[:], T.EP2[:], ["EP2"], ["EU2"], 64, F.Abs, label="E2")
+            both(T.E2[:], T.EU2[:], ["EU2"], ["E2"], 64, "EG", 1.0)
         after("U%d" % (t + 1))
         far("2", T.EU2, "EU2", (32, 32), 2, mv2, "mv2", T.aE2, D2, "bo", True)
         tc(T.EE[:].indirect(sl), T.E2[:], ["E2", "sel", "EEpad"], EE, 64, SC, "EE")
@@ -598,22 +634,31 @@ def rank_program(g, core, T, topo):
         tt(T.xm[:], E, Lo, A.min, EE + ["!NN"], ["xm"], 256, 1.0, "P2")
         tt(keep, T.xm[:], Hi, A.max, ["xm", "!HI"], keepR, 256, 1.0, "P2")
         if last:
-            store(T.ym[:], mor, ["mor"], 4.0)
-            store(T.yd[:], T.ydS[:], ["yd%d" % x for x in range(4)], 3.5)
+            store(T.yd[:], T.ydS[:], ["yd%d" % x for x in range(4)], 4.0)
+            store(T.ym[:], mor, ["mor"], 5.0)
             return
         send_P(t + 1)
-        decode(tau)
-        if t == 0:
-            (gcopy if OPT["gconv"] else tc)(T.D16[:, 0:256], T.ydS[:, 0::4], ["yd0"], ["D16_0"], 256, label="D16n")
         S(84, lambda e: e.activation(T.aE2[:], T.got2[:], F.Copy, accum_out=T.cnt[:, 4:5]), ["got2"], ["n2", "gap2.1"], 1.0, "margin")
         P(320, [(T.DD[:, 320:321], T.no16[:], T.cum[:, 255:256], True, False), (T.DD[:, 320:321], T.o16[:], T.cnt[:, 4:5], False, True)],
           ["o16", "no16", "cum", "n2"], ["!DD"], "margin")
         ts(T.qi[:, 224:225], T.DD[:, 320:321], 2048.0, A.add, ["!DD"], ["ai"], 1, label="margin")
         ts(T.qi[:, 240:241], T.qi[:, 224:225], 127, A.bitwise_and, ["ai"], ["aj"], 1, label="margin")
-        ts(T.nm[:, t + 1:t + 2], T.qi[:, 240:241], -1.0, A.mult, ["aj"], ["nm%d" % (t + 1)], 1, label="margin")
+        both(T.nm[:, t + 1:t + 2], T.qi[:, 240:241], ["aj"], ["nm%d" % (t + 1)], 1, "margin", 1.0, -1.0)
 
     for t in range(RO):
         rnd(t)
+    chain = [k for x in FIRST.split() for k in early if ops[k]["q"] == "G" and ops[k]["out"] == x]
+    for a, b in zip(chain, chain[1:]):
+        ops[b]["deps"].setdefault(a, 0)
+    for o in ops:
+        if o["label"] == "nbT":
+            o["deps"].setdefault(first_v[0], 0)
+    for k, o in enumerate(ops):
+        if o["q"] == "G" and k != issued["C0"]:
+            if k in early:
+                ops[issued["C0"]]["deps"].setdefault(k, 0)
+            else:
+                o["deps"].setdefault(issued["C0"], 0)
     emit(g, sm, ops, sent)
 
 
@@ -709,16 +754,15 @@ def timed(order, where, cost, more, prv, first, known, calm):
     return end, by
 
 
-def polish(order, where, costs, more, nxt, prv, prvs, qs, rng):
+def polish(order, where, costs, more, nxt, prv, prvs, qs, rng, steps, temp, floor):
     m = len(order)
     order = [k for k in order if k != m - 1] + [m - 1]
 
     def value(o, w, first, old, calm):
         runs = [timed(o, w, c, more, p, first, x, calm) for c, p, x in zip(costs, prvs, old)]
-        return sum(r[0][m - 1] for r in runs), runs
+        return sum(r[0][m - 1] + OPT["mean"] * sum(r[0]) / m for r in runs), runs
     val, runs = value(order, where, 0, [None] * len(costs), m)
     best = (val, order, where)
-    steps = OPT["steps"]
     for i in range(steps):
         end, by = runs[int(rng.integers(0, len(runs)))]
         k, pairs = m - 1, []
@@ -765,11 +809,11 @@ def polish(order, where, costs, more, nxt, prv, prvs, qs, rng):
                     continue
                 o2 = order[:pu] + [x for x in mid if x not in late] + [x for x in mid if x in late] + order[pv + 1:]
         v2, r2 = value(o2, w2, pu, runs, pv - pu if i % 50 else m)
-        if v2 <= val + rng.exponential(OPT["temp"]) * (1.0 - i / steps):
+        if v2 <= val + rng.exponential(temp) * (1.0 - (1.0 - floor) * i / steps):
             val, runs, order, where = v2, r2, o2, w2
             if val < best[0]:
                 best = (val, order, where)
-    return best[1], best[2]
+    return best
 
 
 def find_order(ops):
@@ -783,13 +827,29 @@ def find_order(ops):
         if o["wake"]:
             nxt[k].append((m - 1, o["wake"]))
             prv[m - 1].append((k, o["wake"]))
+    below = [0] * m
+    left = [len(p) for p in prv]
+    sort = [k for k in range(m) if not left[k]]
+    for k in sort:
+        for b, _ in nxt[k]:
+            left[b] -= 1
+            if not left[b]:
+                sort.append(b)
+    for k in reversed(sort):
+        for b, _ in nxt[k]:
+            below[k] |= below[b] | 1 << b
+    nxt = [[(c, d) for c, d in x if not any(e >= d and below[b] >> c & 1 for b, e in x)] for x in nxt]
+    prv = [[] for _ in range(m)]
+    for k in range(m):
+        for b, d in nxt[k]:
+            prv[b].append((k, d))
     costs = [[(o["cost"] + o["gat"] * (ga - GA) + fix * (o["q"] in "VS")) * (fp if o["q"] == "P" else f if o["q"] in "VSG" else OPT["far_links"] if o["q"] == "R" else 1.0)
               for o in ops] + [0.0] for ga, f, fp, fix, _ in OPT["models"]]
-    prvs = [[[(a, d + dw * (d > 0.0)) for a, d in p] for p in prv] for _, _, _, _, dw in OPT["models"]]
+    prvs = [[[(a, d + dw * (d > 0.0) if d < 1.0 or dw > 0.0 else 1.25 * d) for a, d in p] for p in prv] for _, _, _, _, dw in OPT["models"]]
     cost, more = costs[0], [o["more"] for o in ops] + [0.0]
     qs = [("V", "S") if o["q"] == "VS" else (o["q"],) for o in ops] + [("R",)]
     due = [0.0] * m
-    for k in range(m - 1, -1, -1):
+    for k in reversed(sort):
         due[k] = min([due[b] - d for b, d in nxt[k]] + [0.0]) - cost[k]
     FOUND["dbg"] = (due, cost, nxt, ops)
     rng = np.random.default_rng(OPT["seed"])
@@ -803,23 +863,14 @@ def find_order(ops):
         ends = [s + c + (x if q == "S" else 0.0) for s, c, x, q in zip(start, cost, more, where)]
         _, back, _, bspan = one_pass(cost, more, prv, [(q,) for q in where], [-x for x in ends], look, one)
         return [bspan - b - (e - s) for b, e, s in zip(back, ends, start)]
-    lag = [OPT["lag"]] * m
-    cur = forward(due, lag)
-    top = cur
-    for i in range(OPT["tries"]):
-        if i % 8 == 0:
-            d2, l2 = backward(cur[2], cur[3]), lag
-        else:
-            a, x = float(rng.uniform(-5.0, cur[4])), rng.normal(0.0, 1.0, (2, m)).tolist()
-            w, s = float(rng.uniform(3.0, 12.0)), OPT["noise"] * float(rng.uniform(0.3, 2.0))
-            d2 = [d + s * y if a <= t < a + w else d for d, t, y in zip(due, cur[2], x[0])]
-            l2 = [OPT["lag"] + 0.6 * y if a <= t < a + w and y * y > 1.0 else z for z, t, y in zip(lag, cur[2], x[1])]
-        new = forward(d2, l2)
-        if new[0] <= cur[0] + OPT["heat"] * (1.0 - i / OPT["tries"]) or i == 0:
-            cur, due, lag = new, d2, l2
-            if cur[0] < top[0]:
-                top = cur
-    order, where = polish(top[1], top[3], costs, more, nxt, prv, prvs, qs, rng)
+    lag, found = [OPT["lag"]] * m, []
+    for i in range(OPT["starts"]):
+        cur = forward([d + y for d, y in zip(due, rng.normal(0.0, OPT["noise"], m).tolist())], lag)
+        for _ in range(2):
+            cur = min(cur, forward(backward(cur[2], cur[3]), lag))
+        found.append(polish(cur[1], cur[3], costs, more, nxt, prv, prvs, qs, rng, OPT["short"], OPT["temp"], 0.5))
+    _, order, where = min(found)
+    _, order, where = polish(order, where, costs, more, nxt, prv, prvs, qs, rng, OPT["steps"], 0.7 * OPT["temp"], 0.0)
     top = (order, replay(order, where, cost, more, nxt), where)
     return [k for k in top[0] if k < m - 1], top[1], top[2]
 

import numpy as np
from concourse.mybir import AluOpType as A, ActivationFunctionType as F

RO, CAP = 5, 64
BIG = float(2 ** 23)
HUGE = float(2 ** 30)
ROUND = 1.5 * 2 ** 34
PAD = 256 + CAP
OPT = {"far": (64, 64, 64, 32, 32), "farD": (64, 64, 64, 64), "cand": (32,) * 8, "spath": (4, 5, 6, 7), "spath0": (4, 5, 6, 7), "vl": 128, "relu2": (4,), "p16": False, "far_links": 1.2,
       "models": ((1.4, 0.93, 0.9, -0.01, 0.05), (1.7, 1.1, 1.4, 0.01, -0.02)), "dec": "P", "relu1": True, "bits": True, "g2": False, "gconv": True,
       "lists": [([0], [0]), ([0, 1, 2, 3], [1, 2, 3, 4])], "tail": 1, "ns": 3, "neq": "P", "kd": "P",
       "vf": 0.04, "sf": 0.07, "pe": 0.6e-3, "wake": 0.16, "look": 0.2, "lag": 0.7, "tries": 100, "seed": 1, "noise": 0.4, "heat": 1.0, "steps": 250000, "temp": 0.35, "mean": 0.3, "starts": 3, "short": 5000}

SCRATCH = {}


def _b(names, cols, dtype="float32", where="sbuf"):
    for nm in names.split():
        SCRATCH[nm] = (where, [128, cols], dtype)


_b("K1 K2 CC WW DD DF NN HI", 512, "float32", "psum")
_b("morS", 12 * PAD, "bfloat16")
_b("meaQ", 3072, "bfloat16")
_b("meaS neq m16 dd2 aa2 X2 Y2", 1024, "bfloat16")
_b("oneb", 512, "bfloat16")
_b("meaT", 1024 + CAP, "bfloat16")
_b("basI derI b15", 1024, "int32")
_b("useI", 512, "int32")
PW = 1024
_b("Pt", PW)
_b("lane nbr ydS", 1024)
_b("nbT", 1024 + CAP)
_b("useF", 512)
_b("PQ", 1024 if OPT["p16"] else 1024 * RO)
_b("mvr", 16384, "bfloat16")
_b("mvt", 2048, "bfloat16")
_b("mvx", 128, "bfloat16")
_b("D16", 1024, "uint16")
_b("cl of", 80, "uint16")
_b("XD YD XL YL dd1 aa1", 4096, "bfloat16")
_b("cU1 EU1", 256, "uint16")
_b("cU2 EU2 mu", 64, "uint16")
_b("sel", 8, "uint16")
_b("EP1 xm mk8", 256)
_b("cF1 val", 256, "float16")
_b("SS ZI", 384, "int32")
_b("ZB LT", 408, "float16")
_b("th", 128, "bfloat16")
_b("Ih", 128 + 16, "float16")
_b("cF2", 64, "float16")
_b("EE", PAD)
_b("cA", 256 * RO + CAP)
_b("cS", 512)
_b("clQ", 256, "uint16")
if OPT["p16"]:
    _b("P16", 1024, "float16")
    _b("PL", 1024 * RO, "float16")
_b("nb2 EP2 E2 e15", 64)
_b("LZ LB", 512)
_b("LT3 one If nIf n2If o16 mbig", 128)
_b("qi ik8", 256, "int32")
_b("qa qc qd s16 t12 c97 c1", 80, "int32")
_b("eq aE1 d1 old ab", 256, "bfloat16")
_b("ad got cum", PAD, "bfloat16")
_b("le lc mseg", 2 * PAD, "bfloat16")
_b("junk", 4 * PAD, "bfloat16")
_b("ad2 aE2 got2 old2 d2", 64, "bfloat16")
_b("n8k Ib nIb IB IH nIH nH no16 tmb bo bo2 nbo w128 tri k15", 128, "bfloat16")
_b("W8 nW8 w8t", 8, "bfloat16")
_b("RR", 16)
_b("km", 260)
_b("ikm", 260, "int32")
_b("nm b8 sc cnt", 8)

QS = ("V", "S", "P", "G")
SEMAPHORES = list(QS) + ["ld%d" % i for i in range(6)] + ["st"]
for _n in ["M%d" % d for d in (1, 2, 3)] + ["C%d" % d for d in range(4)] + ["U%d" % t for t in range(RO)] + ["P%d" % t for t in range(RO)]:
    SEMAPHORES += ["a" + _n, "s" + _n]

CY, WAKE = 0.9e-3, 0.08
GA, SC = 1.4, 3.5
FIRST = "If ik8 e15 RR c97 w8t lane0 b8h Ih pi"
FOUND = {}


def rank_program(g, core, T, topo):
    rank = T.rank_of(core)
    if rank is None:
        return
    n = len(T.cores)
    sm = T.sem
    ops, lastw, readers = [], {}, {}

    def op(q, cost, calls, R=(), W=(), sem=None, inc=1, wake=0.0, label="", gat=0.0, more=0.0):
        k = len(ops)
        if "sel" in R:
            R = [r for r in R if r != "sel"] + ["selS", "selV"]
        deps = {}

        def dep(a, kind):
            deps[a] = max(deps.get(a, 0), kind)
        for r in R:
            if r in lastw:
                a = lastw[r]
                dep(a, 1 if r[0] == "!" and q == "P" and ops[a]["q"] == "P" else 2)
            if r[0] == "!":
                for a in readers.get(r, ()):
                    if ops[a]["q"] != q or q == "VS":
                        dep(a, 1)
        for w in W:
            for a in ([lastw[w]] if w in lastw else []) + readers.get(w, []):
                dep(a, 1)
        for r in R:
            readers.setdefault(r, []).append(k)
        for w in W:
            lastw[w] = k
            readers[w] = []
        ops.append({"q": q, "cost": cost, "gat": gat, "more": more, "calls": calls, "deps": deps, "sem": sem, "inc": inc, "wake": wake, "label": label, "out": W[0] if W else ""})
        return k

    def V(c, call, R, W, f=1.0, label=""):
        op("V", OPT["vf"] + max(64.0, c * f) * CY, [call], R, W, label=label, gat=c * CY if f == GA else 0.0)

    def S(c, call, R, W, f=1.0, label=""):
        op("S", OPT["sf"] + max(64.0, c * f) * CY, [call], R, W, label=label, gat=c * CY if f == GA else 0.0)

    def P(c, mms, R, W, label="pe"):
        def call(m):
            return lambda e: e.matmul(m[0], m[1], m[2], m[3], m[4])
        per = max(1, len(mms) * 512 // max(c, 512))
        for i in range(0, len(mms), per):
            part = mms[i:i + per]
            op("P", len(part) * (0.005 + c * OPT["pe"] / len(mms)), [call(m) for m in part], R, W, label=label)

    def halves(out, w, x, start, stop):
        return [(out[:, 0:128], w, x[:, 0:128], start, False), (out[:, 128:256], w, x[:, 128:256], False, stop)]

    def G(c, call, R, W, label="g"):
        op("G", 0.2 + 2 * c * CY, [call], R, W, label=label)

    def sel(out, in_, pattern, opc, base, cm, R, W, c, label="gsel"):
        G(c, lambda e: e.affine_select(out, in_, pattern, opc, 0.0, base, cm), R, W, label)

    def gcopy(out, in_, R, W, c, label):
        sel(out, in_, [[0, c]], A.is_ge, 0, 0, R, W, c, label)

    def iota(out, pattern, base, cm, W, c):
        if out.dtype == T.qi.dtype:
            G(c, lambda e: e.iota(out, pattern, base, cm), [], W)
        else:
            G(c, lambda e: e.iota(out, pattern, base, cm, allow_small_or_imprecise_dtypes=True), [], W)

    def ts(out, in0, s1, op0, R, W, c, f=1.0, label="ts", s2=None, op1=None):
        if op1 is None:
            V(c, lambda e: e.tensor_scalar(out, in0, s1, None, op0), R, W, f, label)
        else:
            V(c, lambda e: e.tensor_scalar(out, in0, s1, s2, op0, op1), R, W, f, label)

    def tt(out, a, b, o, R, W, c, f=2.0, label="tt"):
        V(c, lambda e: e.tensor_tensor(out, a, b, o), R, W, f, label)

    def tc(out, a, R, W, c, f=1.0, label="tc"):
        V(c, lambda e: e.tensor_copy(out, a), R, W, f, label)

    def fill(out, x, W, c):
        V(c, lambda e: e.memset(out, x), [], W, label="fill")

    def scan(out, d0, d1, o0, o1, R, W, c, f, label):
        V(c, lambda e: e.tensor_tensor_scan(out, d0, d1, 0.0, o0, o1), R, W, f, label)

    def act(out, in_, R, W, c, func=F.Copy, scale=1.0, f=1.0, label="act"):
        S(c, lambda e: e.activation(out, in_, func, scale=scale), R, W, f, label)

    def both(out, in_, R, W, c, label, f=GA, scale=1.0):
        cv, cs = OPT["vf"] + max(64.0, c * f) * CY, OPT["sf"] + max(64.0, c * max(f, 1.0)) * CY
        op("VS", cv, [(lambda e: e.tensor_copy(out, in_) if scale == 1.0 else e.tensor_scalar(out, in_, scale, None, A.mult), lambda e: e.activation(out, in_, F.Copy, scale=scale))],
           R, W, label=label, gat=c * CY if f == GA else 0.0, more=cs - cv)

    def store(out, in_, R, us):
        op("Y", 0.1, [lambda e: e.dma_start(out, in_)], R, [], sem="st", inc=16, wake=us, label="out")

    def load(qn, i, out, in_, W, us):
        op(qn, 0.1, [lambda e: e.dma_start(out, in_)], (), W, sem="ld%d" % i, inc=16, wake=us, label="load")
    mor = T.morS[:, 0:3072]
    load("S", 5, T.b15[0:8, :], T.bas[15::16, :], ["b15"], 1.2)
    load("Y", 1, T.meaS[:], T.mea[:], ["meaS"], 1.8)
    load("Y", 2, T.useI[:], T.use[:], ["useI"], 2.5)
    load("Y", 0, T.basI[:], T.bas[:], ["basI"], 4.0)
    load("Y", 3, T.derI[:], T.der[:], ["derI"], 5.5)
    load("Y", 4, mor, T.mor[:], ["mor"], 7.8)
    for k in range(1, 6):
        ops[k]["deps"][k - 1] = 0

    fill(T.one[:], 1.0, ["one"], 128)
    fill(T.oneb[:], 1.0, ["oneb"], 512)
    sel(T.e15[:], T.one[:, 0:64], [[-1, 8], [0, 8]], A.is_equal, 0, 1, ["one"], ["e15"], 64)
    both(T.ydS[0:8, 0::4], T.b15[0:8, 0::4], ["b15"], ["yd0"], 256, "B", 1.0)
    iota(T.ik8[:], [[0, 32], [-1, 8]], 128, 1, ["ik8"], 256)
    sel(T.RR[:], T.one[:, 0:16], [[-8, 16]], A.is_ge, 0, 1, ["one"], ["RR"], 16)
    sel(T.RR[:], T.RR[:], [[8, 16]], A.is_ge, 7, -1, ["RR"], ["RR"], 16)
    ts(T.ik8[:], T.ik8[:], 7, A.bitwise_and, ["ik8"], ["ik8"], 256)
    ts(T.mk8[:], T.ik8[:], 0.0, A.is_equal, ["ik8"], ["mk8"], 256)
    sel(T.If[:], T.one[:], [[-1, 128]], A.is_equal, 0, 1, ["one"], ["If"], 128)
    sel(T.w8t[:], T.oneb[:, 0:8], [[-16, 8]], A.is_ge, 0, 1, ["oneb"], ["w8t"], 8)
    sel(T.w8t[:], T.w8t[:], [[16, 8]], A.is_ge, 15, -1, ["w8t"], ["w8t"], 8)
    act(T.W8[:], T.w8t[:], ["w8t"], ["W8"], 8, scale=2048.0)
    act(T.b8[:], T.w8t[:], ["w8t"], ["b8"], 8)
    act(T.nW8[:], T.w8t[:], ["w8t"], ["nW8"], 8, scale=-2048.0)
    gcopy(T.Ih[:, 128:136], T.w8t[:], ["w8t"], ["b8h"], 8, "gsel")
    gcopy(T.Ih[:, 0:128], T.If[:], ["If"], ["Ih"], 128, "gsel")
    for nm_, sc_ in (("Ib", 1.0), ("IB", BIG), ("nIb", -1.0), ("nIf", -1.0), ("n2If", -2.0), ("IH", HUGE), ("nIH", -HUGE)):
        act(T[nm_][:], T.If[:], ["If"], [nm_], 128, scale=sc_)
    act(T.o16[:], T.one[:], ["one"], ["o16"], 128, scale=1.0 / 16)
    act(T.no16[:], T.one[:], ["one"], ["no16"], 128, scale=-1.0 / 16)
    act(T.nH[:], T.one[:], ["one"], ["nH"], 128, scale=-HUGE)
    act(T.n8k[:], T.one[:], ["one"], ["n8k"], 128, scale=-8192.0)
    NS = OPT["ns"]
    NV = 4 - NS
    for nm_, x, y, first, c in (("mbig", -2.0 * BIG, 2.0 * BIG, T.mbig[:, 0::16], 128), ("m16", 1.0, 0.0, T.m16[:, 0::16], 512),
                                ("mseg", 1.0, 0.0, T.mseg[:, 0::PAD], PAD)):
        fill(T[nm_][:], x, [nm_], c)
        fill(first, y, [nm_], 64)
    ts(T.ZB[:], T.oneb[:, 0:408], 0.0, A.mult, ["oneb"], ["ZB0", "ZB1", "ZB2"], 408, 0.5)
    iota(T.ZI[:], [[0, 384]], 0, 0, ["ZI0", "ZI1", "ZI2"], 384)
    ts(T.LT[:, 128::136], T.oneb[:, 0:3], 0.0, A.mult, ["oneb"], ["LTpad"], 3)
    act(T.Ih[:, 136:144], T.w8t[:], ["w8t"], ["nb8h"], 8, scale=-1.0)
    fill(T.sc[:, 1:2], PAD / 2.0, ["k1"], 1)
    for nm_, a in (("cA", 256 * RO), ("EE", 256), ("ad", 256), ("got", 256), ("meaT", 1024), ("nbT", 1024)):
        fill(T[nm_][:, a:a + CAP], 0.0, [nm_ + "pad"], CAP)
    qi = [T.qi[:, 16 * i:16 * i + 16] for i in range(16)]
    pw = T.sc[:, 0:1]
    iota(qi[0], [[0, 16]], 0, 1, ["pi"], 16)
    ts(qi[1], qi[0], 15, A.bitwise_and, ["pi"], ["pj"], 16)
    ts(pw, T.qi[:, 16:17], 1.0, A.add, ["pj"], ["pw"], 1)
    iota(T.th[:], [[0, 8], [1, 16]], 0, 0, ["th"], 128)
    ts(T.th[:], T.th[:], pw, A.is_lt, ["th", "pw"], ["th"], 128, 0.5)
    fill(T.th[:, 0::16], 0.0, ["th"], 8)
    iota(T.s16[:], [[0, 5], [16, 16]], -1, 0, ["s16"], 80)
    ts(T.t12[:], T.s16[:], pw, A.add, ["pw", "s16"], ["t12"], 80, s2=12.0, op1=A.mult)
    ts(T.sc[:, 4:8], T.s16[:, 0:4], pw, A.add, ["pw", "s16"], ["sc"], 4, s2=0.5, op1=A.add)
    iota(T.c97[:], [[97, 5], [0, 16]], 0, 0, ["c97"], 80)
    iota(T.c1[:], [[1, 5], [0, 16]], 0, 0, ["c1"], 80)
    sel(T.tmb[:], T.oneb[:, 0:128], [[-16, 8], [0, 16]], A.is_ge, 0, 1, ["oneb"], ["tmb"], 128)
    sel(T.bo[:], T.tmb[:], [[16, 8], [0, 16]], A.is_ge, 15, -1, ["tmb"], ["bo"], 128)
    act(T.nbo[:], T.bo[:], ["bo"], ["nbo"], 128, scale=-1.0)
    act(T.bo2[:], T.bo[:], ["bo"], ["bo2"], 128, scale=2.0)
    ts(T.w128[:], T.bo[:], pw, A.mult, ["bo", "pw"], ["w128"], 128, 0.5)
    sel(T.tmb[:], T.bo[:], [[1, 128]], A.is_ge, 0, -1, ["bo"], ["tmb"], 128)
    act(T.tri[:], T.tmb[:], ["tmb"], ["tri"], 128, scale=8192.0)
    sel(T.tmb[:], T.oneb[:, 0:128], [[0, 8], [1, 16]], A.is_equal, -15, 0, ["oneb"], ["tmb"], 128)
    ts(T.k15[:], T.tmb[:], 8192.0, A.mult, ["tmb"], ["k15"], 128, 0.5, s2=-4096.0, op1=A.add)
    iota(T.ikm[:], [[1, 260]], 128, -1, ["ikm"], 260)
    ts(T.ikm[:], T.ikm[:], 15, A.bitwise_and, ["ikm"], ["ikm"], 260)
    ts(T.km[:], T.ikm[:], 0.0, A.is_equal, ["ikm"], ["km"], 260)
    fill(T.nm[:, 0:1], 0.0, ["nm0"], 1)
    early = range(6, len(ops) + 1)
    for tau in range(4):
        iota(T.lane[:, 256 * tau:256 * tau + 256], [[4, 256]], tau, 0, ["lane%d" % tau], 256)
    iota(T.nbr[:], [[2, 512], [-1, 2]], 1, 0, ["nbr"], 1024)
    iota(T.morS[:, 3072:3840], [[0, 768]], 0, 0, ["morpad"], 768)

    for tau in range(4):
        both(T.nbT[:, 256 * tau:256 * tau + 256], T.basI[:, tau::4], ["basI"], ["nbT%d" % tau], 256, "nbT", 1.0, -1.0)
    (gcopy if OPT["gconv"] else tc)(T.useF[:], T.useI[:], ["useI"], ["useF"], 512, label="useF")
    for tau in range(4):
        if tau:
            gcopy(T.D16[:, 256 * tau:256 * tau + 256], T.derI[:, tau::4], ["derI"], ["D16_%d" % tau], 256, "D16")
        else:
            both(T.D16[:, 0:256], T.derI[:, 0::4], ["derI"], ["D16_0"], 256, "D16", 1.0)
        gcopy(T.meaT[:, 256 * tau:256 * tau + 256], T.meaS[:, tau::4], ["meaS"], ["meaT%d" % tau], 256, "meaT")

    def wide(nm_, tau):
        return T[nm_][:, 256 * tau:256 * tau + PAD], [nm_ + str(tau), nm_ + (str(tau + 1) if tau < 3 else "pad")]

    def mvrep(tau):
        for k in range(16):
            o, i_ = T.mvr[:, 4096 * tau + k:4096 * tau + 16 * VL:16], T.meaS[:, tau:4 * VL:4]
            if tau:
                gcopy(o, i_, ["meaS"], ["mvr%d.%d" % (tau, k)], VL, "mvrg")
            else:
                both(o, i_, ["meaS"], ["mvr%d.%d" % (tau, k)], VL, "mvr", 0.5)
        for k in range(2 * (VL < 256)):
            o, i_ = T.mvt[:, 512 * tau + 2 * VL + k:512 * tau + 512:2], T.meaS[:, 4 * VL + tau::4]
            if tau:
                gcopy(o, i_, ["meaS"], ["mvt%d.%d" % (tau, k)], 256 - VL, "mvrg")
            else:
                both(o, i_, ["meaS"], ["mvt%d.%d" % (tau, k)], 256 - VL, "mvr", 0.5)
    VL = OPT["vl"]
    mvrep(0)
    Ph = ["Ph0", "Ph1"]
    for hf in range(2):
        c0 = slice(512 * hf, 512 * hf + 512)
        bank = ("NN", "DD")[hf]
        P(2048, [(T[bank][:, tau::4], T.nIf[:], T.nbT[:, 256 * tau + 128 * hf:256 * tau + 128 * hf + 128], tau == 0, tau == 3) for tau in range(4)],
          ["nIf"] + ["nbT%d" % tau for tau in range(4)], ["!" + bank])
        tt(T.neq[:, c0], T.derI[:, c0], T[bank][:], A.not_equal, ["!" + bank, "derI"], ["neq%d" % hf], 512, 1.0, "neq")
        P(1024, [(T[bank][:], T.k15[0:1, :], T.oneb[0:1, 0:512], True, False), (T[bank][:], T.tri[:], T.neq[:, c0], False, True)],
          ["tri", "k15", "neq%d" % hf, "oneb"], ["!" + bank])
        tt(T.Pt[:, c0], T.derI[:, c0], T[bank][:], A.min, ["derI", "!" + bank], ["Ph%d" % hf], 512, 1.0, "P0")

    def bylane(name, taus, rounds, src, srcR, pick, pickR, cy, bank):
        w, B, L = len(taus), T[bank], T["L" + name]
        P(2 * w * cy, [(B[:, 64 * (w * h + j):64 * (w * h + j) + 64], src(tau, h), pick, True, True) for h in range(2) for j, tau in enumerate(taus)],
          srcR + [pickR], ["!" + bank], name)
        for h in range(2):
            tt(L[:, h:128 * w:2], B[:, 64 * w * h:64 * w * (h + 1)], T.mk8[:, 0:64 * w], A.mult, ["!" + bank, "mk8"], ["L%s%d" % (name, h)], 64 * w, 1.0, name)
        P(256 * len(rounds), [(B[:, 16 * j:16 * j + 16], L[:, 128 * taus.index(t % 4):128 * taus.index(t % 4) + 128], T.RR[:], True, True) for j, t in enumerate(rounds)],
          ["L%s0" % name, "L%s1" % name, "RR"], ["!" + bank], name)
        return B[:, 0:16 * len(rounds)], slice(16 * rounds[0], 16 * rounds[-1] + 16), 16 * len(rounds)

    def lists(taus, rounds, bank):
        x, c, w = bylane("B", taus, rounds, lambda tau, h: T.ydS[0:8, 4 * h + tau::8], ["yd%d" % tau for tau in taus], T.e15[0:8, :], "e15", 256, bank)
        tt(T.qa[:, c], T.c97[:, c], x, A.add, ["!" + bank, "c97"], ["qa"], w, 1.0, "B")
        ts(T.qa[:, c], T.qa[:, c], 511, A.bitwise_and, ["qa"], ["qa"], w, label="B")
        tc(T.cl[:, c], T.qa[:, c], ["qa"], ["cl%d" % t for t in rounds], w, label="B")

    def places(taus, rounds, bank):
        x, c, w = bylane("Z", taus, rounds, lambda tau, h: T.meaS[:, 4 * h + tau::8], ["meaS"], T.w128[:, 0::2], "w128", 64, bank)
        tt(T.qc[:, c], T.c1[:, c], x, A.add, ["!" + bank, "c1"], ["qc"], w, 1.0, "Z")
        ts(T.qd[:, c], T.qc[:, c], 7, A.bitwise_and, ["qc"], ["qd"], w, label="Z")
        tt(T.qc[:, c], T.qd[:, c], T.t12[:, c], A.add, ["qd", "t12"], ["qc"], w, label="Z")
        tc(T.of[:, c], T.qc[:, c], ["qc"], ["of%d" % t for t in rounds], w, label="Z")

    sent, issued, line = {}, {}, [0, 0]

    def send(d, buf, in_, name, R, us):
        to, frm = T.cores[(rank - d) % n], T.cores[(rank + d) % n]
        rid, pid = topo.addr(to)[:2]
        mask = topo.mask(core, to)
        sent["s" + name] = len(topo.engines(core, to))
        k = op("G", 0.7 if len(sent) > 1 else 3.5, [lambda e: e.remote_dma(buf, in_, sm["a" + name], sm["s" + name], pid, rid, mask)], R, (), sem="s" + name, inc=0, wake=us, label="send")
        j = op("R", us - 2.5, [], (), ["Q" + name], sem="a" + name, inc=len(topo.engines(frm, core)), wake=2.5, label="arrive")
        ops[j]["deps"][k] = 0
        if issued:
            ops[k]["deps"].setdefault(line[0], 0)
            ops[j]["deps"].setdefault(line[1], 0)
        issued[name], line[0], line[1] = k, k, j

    def after(*names):
        for x in names:
            if x in issued:
                ops[-1]["deps"].setdefault(issued[x], 0)

    def send_classes(j):
        c = slice(16, 80) if j else slice(0, 16)
        send(-max(j, 1), T.clQ[:, 64 * j:64 * j + c.stop - c.start], T.cl[:, c], "C%d" % j, ["cl%d" % t for t in range(RO) if (t > 0) == (j > 0)], 3.2)

    def send_use(t):
        d, s = 1 + t % 3, T.cS[:, 256 * (t % 2):256 * (t % 2) + 256]
        lst = T.clQ[:, 64 * d + 16 * t - 16:64 * d + 16 * t] if t else T.clQ[:, 0:16]
        both(s, T.useF[:].indirect(lst), ["useF", "QC%d" % (d if t else 0)], ["cS%d" % (t % 2)], 256, "cA")
        send(d, T.cA[:, 1024 - 256 * t:1280 - 256 * t], s, "U%d" % t, ["cS%d" % (t % 2)], 4.5)

    def send_P(t):
        if OPT["p16"]:
            c = slice((t - 1) % 4, 1024, 4) if t else slice(0, 1024)
            ts(T.P16[:, c], T.Pt[:, c], -1024.0, A.add, Ph, ["P16"], 256 if t else 1024, label="P16")
            send(1 + t % 3, T.PL[:, 1024 * t:1024 * t + 1024], T.P16[:], "P%d" % t, ["P16"], 6.0)
            gcopy(T.PQ[:, 0:1024], T.PL[:, 1024 * t:1024 * t + 1024], ["QP%d" % t], ["PQ"], 1024, "PQ")
        else:
            send(1 + t % 3, T.PQ[:, 1024 * t:1024 * t + 1024], T.Pt[:], "P%d" % t, Ph, 9.0)

    def send_mea(d):
        send(d, T.meaQ[:, 1024 * d - 1024:1024 * d], T.meaS[:], "M%d" % d, ["meaS"], 6.0)

    flip, last_v, first_v = [0], [0], [0]

    def cands(c, cuts, spath, mea, meaR, rep, repR, own):
        cU, dd, aa = T["cU" + c], T["dd" + c], T["aa" + c]
        l0 = 0
        for j, w in enumerate(cuts):
            a, b, dR, aR = 16 * l0, 16 * (l0 + w), "dd%s.%d" % (c, j), ["aa%s.%d" % (c, x) for x in range(l0 // 16, (l0 + w) // 16)]
            src = mea.indirect(cU[:, l0:l0 + w])
            l0 += w
            if j in spath:
                flip[0] = 1 - flip[0]
                bank = ("CC", "WW")[flip[0]]
                o = T[bank][:, 0:b - a]
                act(dd[:, a:b], src, [meaR, "cU" + c], [dR], b - a, f=GA, label="scand" + c)
                if l0 <= VL:
                    P(b - a, [(o, T.nIb[:], rep[:, a:b], True, False)], ["nIb"] + repR, ["!" + bank], "scand" + c)
                else:
                    P(512, [(o[:, k::8], T.nIb[:], own[0][:, 2 * (l0 - w):2 * l0], k == 0, False) for k in range(8)], ["nIb"] + own[1], ["!" + bank], "scand" + c)
                P(b - a, [(o, T.Ib[:], dd[:, a:b], False, True)], ["Ib", dR], ["!" + bank], "scand" + c)
                act(aa[:, a:b], o, ["!" + bank], aR, b - a, F.Abs, label="scand" + c)
            else:
                tt(dd[:, a:b], src, rep[:, a:b], A.subtract, [meaR, "cU" + c] + repR, [dR], b - a, GA, "cand" + c)
                if OPT["relu1"]:
                    cv, cs = OPT["vf"] + 0.5 * (b - a) * CY, OPT["sf"] + (b - a) * CY
                    op("VS", cv, [(lambda e, a=a, b=b: e.tensor_scalar(aa[:, a:b], dd[:, a:b], 0.0, 2.0, A.max, A.mult),
                                   lambda e, a=a, b=b: e.activation(aa[:, a:b], dd[:, a:b], F.Relu, scale=2.0))], [dR], aR, label="abs" + c, more=cs - cv)
                else:
                    act(aa[:, a:b], dd[:, a:b], [dR], aR, b - a, F.Abs, label="abs" + c)
                last_v[0] = len(ops) - 2
                first_v[0] = first_v[0] or len(ops) - 2

    def least(j, bank, p, out, outW):
        K, c, lb = T[bank], slice(128 * j, 128 * j + 128), "min%d" % (j // 2 + 1)
        c0, c1 = slice(136 * j, 136 * j + 128), slice(136 * j + 1, 136 * j + 129)
        SS, ZB, LT, ZI = T.SS[0:p, c], T.ZB[0:p, c0], T.LT[0:p, c0], T.ZI[0:p, c]
        scan(SS, T.mbig[0:p, :], K[0:p, 0:128], A.max, A.min, ["!" + bank, "mbig"], ["SS%d" % j], 128, 1.0, lb)
        ts(ZI[:, 0::16], SS[:, 15::16], 1023, A.bitwise_and, ["SS%d" % j], ["ZI%d" % j], 8, label=lb)
        both(ZB[:, 0::16], ZI[:, 0::16], ["ZI%d" % j], ["ZB%d" % j], 8, lb, 1.0)
        scan(LT, T.th[0:p, :], ZI, A.mult, A.add, ["ZI%d" % j, "th"], ["LT%d" % j], 128, 1.0, lb)
        o, pos, neg = K[:, 0:p // 16], T.Ih[0:p, 128:128 + p // 16], T.Ih[0:p, 136:136 + p // 16]
        P(64, [(o, T.ZB[0:p, c1], pos, True, False)], ["ZB%d" % j, "b8h"], ["!" + bank], lb)
        P(128, [(o, LT, pos, False, False), (o, T.LT[0:p, c1], neg, False, True)], ["LT%d" % j, "b8h", "nb8h", "LTpad"], ["!" + bank], lb)
        both(out, K[:, 0:p // 16], ["!" + bank], [outW], 8, lb, 1.0)

    def mu(t):
        return T.mu[:, 16 * (t % 2):16 * (t % 2) + 16], ["mu%d.%d" % (t % 2, h) for h in range(2)]

    def own_lists(t):
        tau = t % 4
        use, cl, clR = T.useF[:] if t else T.useI[:], T.cl[:, 16 * t:16 * t + 16], ["useF" if t else "useI", "cl%d" % t]
        both(T.cU1[:], use.indirect(cl), clR, ["cU1"], 256, "cU1")
        if t:
            gcopy(T.cF1[:], T.cU1[:], ["cU1"], ["cF1"], 256, "cF1")
        else:
            both(T.cF1[:], T.cU1[:], ["cU1"], ["cF1"], 256, "cF1", 0.5)
        tt(T.eq[:], use.indirect(cl), T.lane[:, 256 * tau:256 * tau + 256], A.is_equal, clR + ["lane%d" % tau], ["eq"], 256, GA, "eq")

    def own(t):
        tau = t % 4
        cands("1", OPT["cand"], OPT["spath0" if t == 0 else "spath"], T.meaS[:], "meaS", T.mvr[:, 4096 * tau:4096 * tau + 4096], ["mvr%d.%d" % (tau, k) for k in range(16)], (T.mvt[:, 512 * tau:512 * tau + 512], ["mvt%d.%d" % (tau, k) for k in range(2)]))
        for h, bank in enumerate(("K1", "DF")):
            K, c = T[bank], slice(128 * h, 128 * h + 128)
            P(256, [(K[:, 0:128], T.cF1[:, c], T.Ih[:, 0:128], True, False), (K[:, 0:128], T.eq[:, c], T.IB[:], False, False)], ["cF1", "Ih", "eq", "IB"], ["!" + bank], "keys1")
            if OPT["relu1"] and h == 0:
                P(1024, [(K[:, k:128:16], T.dd1[:, k:2048:16], T.nW8[:], False, False) for k in range(16)], ["nW8"] + ["dd1.%d" % x for x in range(4)], ["!" + bank], "keys1")
            P(1024, [(K[:, k:128:16], T.aa1[:, 2048 * h + k:2048 * h + 2048:16], T.W8[:], False, k == 15) for k in range(16)],
              ["W8"] + ["aa1.%d" % x for x in range(8 * h, 8 * h + 8)], ["!" + bank], "keys1")
            least(h, bank, 128, mu(t)[0][:, 8 * h:8 * h + 8], mu(t)[1][h])

    def ask(t):
        tau, d, K = t % 4, 1 + t % 3, T.K2
        sl, mea, mv2 = T.sel[:, 0:4], T.meaQ[:, 1024 * d - 1024:1024 * d], T.mvx[:, 0::2]
        cA, cR = T.cA[:, 1024 - 256 * t:1024 - 256 * t + PAD], ["QU%d" % t, "QU%d" % (t - 1) if t else "cApad", "sel"]
        both(T.cU2[:], cA.indirect(sl), cR, ["cU2"], 64, "cU2")
        win, wR = wide("meaT", tau)
        both(mv2, win.indirect(sl), wR + ["sel"], ["mv2"], 64, "mv2")
        if OPT["g2"]:
            gcopy(T.mvx[:, 1::2], mv2, ["mv2"], ["mv3"], 64, "mv2")
        else:
            both(T.mvx[:, 1::2], win.indirect(sl), wR + ["sel"], ["mv3"], 64, "mv2")
        both(T.cF2[:], T.cU2[:], ["cU2"], ["cF2"], 64, "cF2", 0.5)
        P(128, [(K[0:64, 0:128], T.cF2[:], T.Ih[:, 0:128], True, False)], ["cF2", "Ih"], ["!K2"], "keys2")
        for h, bank in enumerate(("CC", "WW")):
            B, c = T[bank], slice(512 * h, 512 * h + 512)
            both(T.dd2[:, c], mea.indirect(T.cU2[:, 32 * h:32 * h + 32]), ["QM%d" % d, "cU2"], ["dd2.%d" % h], 512, "cand2")
            P(512, [(B[:, k::8], T.nIb[:], T.mvx[:, 64 * h:64 * h + 64], k == 0, False) for k in range(8)], ["nIb", "mv2", "mv3"], ["!" + bank], "cand2")
            P(512, [(B[:], T.Ib[:], T.dd2[:, c], False, True)], ["Ib", "dd2.%d" % h], ["!" + bank], "cand2")
            o = [K[32 * h:32 * h + 32, k:128:16] for k in range(16)]
            if h == 0 and t in OPT["relu2"]:
                P(512, [(o[k], T.dd2[:, 512 * h + k:512 * h + 512:16], T.nW8[:], False, False) for k in range(16)], ["nW8", "dd2.%d" % h], ["!K2"], "keys2")
                ts(T.aa2[:, c], B[:], 0.0, A.max, ["!" + bank], ["aa2.%d" % h], 512, label="abs2", s2=2.0, op1=A.mult)
            else:
                act(T.aa2[:, c], B[:], ["!" + bank], ["aa2.%d" % h], 512, F.Abs, label="abs2")
            P(512, [(o[k], T.aa2[:, 512 * h + k:512 * h + 512:16], T.W8[:], False, k == 15) for k in range(16)], ["W8", "aa2.%d" % h], ["!K2"], "keys2")
        least(2, "K2", 64, T.mu[:, 32:36], "mu2")

    def far(nm_, lst, lstR, cuts, tail, mv, mvR, gap, out, sign, stop):
        X, Y, at = T["X" + nm_], T["Y" + nm_], [sum(cuts[:j]) for j in range(len(cuts) + 1)]
        for j in range(len(cuts)):
            a, b = 16 * at[j], 16 * at[j + 1]
            both(X[:, a:b], mor.indirect(lst[:, at[j]:at[j + 1]]), [lstR % (at[j] // 128) if "%" in lstR else lstR, "mor"], ["X%s.%d" % (nm_, j)], b - a, nm_)
            scan(Y[:, a:b], T.m16[:, 0:b - a], X[:, a:b], A.mult, A.max, ["X%s.%d" % (nm_, j), "m16"], ["Y%s.%d" % (nm_, j)], b - a, 0.5, "scan" + nm_)
        parts = [(0, len(cuts) - tail), (len(cuts) - tail, len(cuts))] if tail else [(0, len(cuts))]
        for i, (j0, j1) in enumerate(parts):
            a, b, gR = at[j0], at[j1], "gap%s.%d" % (nm_, i)
            if a == b:
                continue
            if i:
                yR = ["Y%s.%d" % (nm_, j) for j in range(j0, j1)]
                P(64, [(out[:, a:b], T.nbo[:], mv[:, a:b], False, False)], ["nbo", mvR], ["!DD"], "delta")
                tt(gap[:, a:b], Y[:, 16 * a + 15:16 * b:16], mv[:, a:b], A.max, yR + [mvR], [gR], b - a, label="gap" + nm_)
                P(64, [(out[:, a:b], T.nbo[:], Y[:, 16 * a + 15:16 * b:16], False, False)], ["nbo"] + yR, ["!DD"], "delta")
                P(64, [(out[:, a:b], T.bo2[:], gap[:, a:b], False, True)], ["bo2", gR], ["!DD"], "delta")
                continue
            P(b - a, [(T.DF[:, a:b], T.nIb[:], mv[:, a:b], True, False)], ["nIb", mvR] + (["YD.0"] if nm_ == "D" else []), ["!DF"], "diff")
            P(b - a, [(T.DF[:, a:b], T.Ib[:], Y[:, 16 * a + 15:16 * b:16], False, True)], ["Ib"] + ["Y%s.%d" % (nm_, j) for j in range(j0, j1)], ["!DF"], "diff")
            act(gap[:, a:b], T.DF[:, a:b], ["!DF"], [gR], b - a, F.Abs, label="gap" + nm_)
            P(b - a, [(out[:, a:b], T[sign][:], gap[:, a:b], not stop, stop and j1 == len(cuts))], [sign, gR], ["!DD"], "delta")

    def decode(tau):
        x, o = T.Pt[:, tau:1024:4], T.DF[:, 256:512]
        if OPT["dec"] == "V":
            tt(T.xm[:], x, T.nbT[:, 256 * tau:256 * tau + 256], A.max, Ph + ["nbT%d" % tau], ["xm"], 256, label="dec")
            act(T.ydS[:, tau::4], T.xm[:], ["xm"], ["yd%d" % tau], 256, F.Abs, label="dec")
            return
        P(1280, halves(o, T.nIf[:], T.nbT[:, 256 * tau:256 * tau + 256], True, False) + [(o, T.n8k[0:1, :], T.oneb[0:1, 0:256], False, False)], ["nIf", "n8k", "oneb", "nbT%d" % tau], ["!DF"], "dec")
        P(1024, halves(o, T.n2If[:], x, False, True), ["n2If"] + Ph, ["!DF"], "dec")
        tt(T.ydS[:, tau::4], x, o, A.max, Ph + ["!DF"], ["yd%d" % tau], 256, 1.0, "dec")

    lists([0], [0], "WW")
    send_classes(0)
    send_mea(1)
    send_P(0)
    own_lists(0)
    k = len(ops)
    own(0)
    ops[last_v[0]]["deps"].update({k - 1: 0, k - 2: 0})
    k = len(ops)
    send_use(0)
    ops[k]["deps"][k - 1] = 0
    for tau in range(1, 4):
        gcopy(T.ydS[0:8, tau::4], T.b15[0:8, tau::4], ["b15"], ["yd%d" % tau], 256, "B")
    k = len(ops)
    lists([0, 1, 2, 3], [1, 2, 3, 4], "HI")
    places([0, 1, 2, 3], [0, 1, 2, 3, 4], "K2")
    for x in ops[k:]:
        if x["q"] == "V":
            x["deps"].setdefault(last_v[0], 0)
    for j in range(1, 4):
        send_classes(j)
    send_mea(2)
    mvrep(1)
    send_mea(3)
    mvrep(2)
    mvrep(3)

    If, nIf, Ib, nIb = T.If[:], T.nIf[:], T.Ib[:], T.nIb[:]
    D1, D2, Lo, Hi = T.DD[:, 0:256], T.DD[:, 256:320], T.NN[:, 0:256], T.HI[:, 0:256]
    U1, U2, U3 = T.K1[:, 256:512], T.K2[:, 256:512], T.NN[:, 256:512]
    row, EE = T.oneb[0:1, 0:256], ["EE.0", "EE.1"]

    def rnd(t):
        tau, last = t % 4, t + 1 == RO
        nm, nmR = T.nm[:, t:t + 1], "nm%d" % t
        nb, nbR, mv = T.nbT[:, 256 * tau:256 * tau + 256], "nbT%d" % tau, T.meaS[:, tau::4]
        off, sl, got, E = T.of[:, 16 * t:16 * t + 16], T.sel[:, 0:4], T.got[:, 0:256], T.EE[:, 0:256]
        keep, keepR = (T.ydS[:, tau::4], ["yd%d" % tau]) if last else (T.Pt[:, tau:1024:4], Ph)
        P(1024, halves(Hi, If, keep, True, False), ["If"] + keepR, ["!HI"], "Hi")
        if last:
            P(256, [(Lo, T.nH[0:1, :], row, True, False)], ["nH", "oneb"], ["!NN"], "Hi")
        elif OPT["neq"] == "P":
            P(1024, halves(U3, If, nb, True, False), ["If", nbR], ["!NN"], "Hi")
        far("D", T.D16[:, 256 * tau:256 * tau + 256], "D16_%d" % tau, OPT["farD"], 0, mv, "meaS", T.ad, D1, "nbo", False)
        m = mu(t)
        for h in range(2):
            c = slice(128 * h, 128 * h + 128)
            tt(T.EP1[:, c], T.Pt[:, 0:1024].indirect(m[0][:, 8 * h:8 * h + 8]), nb[:, c], A.max, Ph + [m[1][h], nbR], ["EP1.%d" % h], 128, GA, "E1")
            act(T.EU1[:, c], T.EP1[:, c], ["EP1.%d" % h], ["EU1.%d" % h], 128, F.Abs, label="E1")
        gcopy(E, T.EU1[:], ["EU1.0", "EU1.1"], EE, 256, "EG")
        ops.append(ops.pop())
        for x in ["P%d" % t, "M3"] if t else []:
            ops[-2]["deps"].setdefault(issued[x], 0)
        useT = T.useF[:, 37 * t:37 * t + 256]
        if OPT["kd"] == "P":
            both(T.val[:], T.nbr[:].indirect(m[0]), ["nbr"] + m[1], ["val"], 256, "val")
            P(1024, halves(U1, nIf, useT, True, False), ["nIf", "useF"] + m[1], ["!K1"], "kd")
            P(256, [(U1, T.Ih[:, 0:128], T.val[:], False, True)], ["Ih", "val"], ["!K1"], "kd")
            tt(U1, U1, T.km[:, t:t + 256], A.mult, ["!K1", "km"], ["!K1"], 256, 1.0, "kd")
        else:
            tt(T.val[:], T.nbr[:].indirect(m[0]), useT, A.subtract, ["nbr", "useF"] + m[1], ["val"], 256, GA, "val")
            tt(U1, T.val[:], T.km[:, t:t + 256], A.mult, ["val", "km"], ["!K1"], 256, 2.0, "kd")
        far("L", T.EU1, "EU1.%d", OPT["far"], OPT["tail"], mv, "meaS", T.aE1, D1, "bo", True)
        both(T.old[:], mor.indirect(off), ["mor", "of%d" % t], ["old"], 256, "old")
        P(512, [(U2, Ib, mv, True, False), (U2, nIb, T.old[:], False, True)], ["Ib", "nIb", "meaS", "old"], ["!K2"], "dmo")
        ts(got, D1, nm, A.is_lt, ["!DD", nmR], ["got"], 256, label="ad1")
        after("P0")
        scan(T.cum[:], T.oneb[:, 0:PAD], T.got[:], A.add, A.subtract, ["oneb", "got", "gotpad"], ["cum"], PAD, 0.5, "cum")
        for c in range(NS):
            S(PAD + 20, lambda e, c=c: e.activation(T.junk[:, PAD * c:PAD * c + PAD], T.cum[:], F.Sign, bias=T.sc[:, 4 + c:5 + c], scale=-1.0, accum_out=T.cnt[:, c:c + 1]),
              ["cum", "sc"], ["cnt%d" % c], 1.0, "count")
        if NV:
            for c in range(NV):
                ts(T.le[:, PAD * c:PAD * c + PAD], T.cum[:], T.sc[:, 4 + NS + c:5 + NS + c], A.is_lt, ["cum", "sc"], ["le%d" % c], PAD, 0.5, "count", -0.5, A.add)
            scan(T.lc[:, 0:NV * PAD], T.mseg[:, 0:NV * PAD], T.le[:, 0:NV * PAD], A.mult, A.add, ["mseg"] + ["le%d" % c for c in range(NV)], ["lc"], NV * PAD, 0.5, "count")
            ts(T.sel[:, NS:4], T.lc[:, PAD - 1:NV * PAD:PAD], PAD / 2.0, A.add, ["lc"], ["selV"], NV, label="count")
        op("VS", OPT["vf"] + 64 * CY, [(lambda e: e.tensor_scalar(T.sel[:, 0:NS], T.cnt[:, 0:NS], float(PAD), 0.5, A.add, A.mult),
                                        lambda e: e.activation(T.sel[:, 0:NS], T.cnt[:, 0:NS], F.Identity, bias=T.sc[:, 1:2], scale=0.5))],
           ["cnt%d" % c for c in range(NS)] + ["k1"], ["selS"], label="count", more=0.04)
        tt(U1, got, U1, A.mult, ["!K1", "got"], ["!K1"], 256, 1.0, "up")
        tt(useT, useT, U1, A.add, ["useF", "!K1"], ["useF"], 256, 1.0, "up")
        if last:
            store(T.yu[:], T.useF[:], ["useF"], 3.0)
        else:
            send_use(t + 1)
            own_lists(t + 1)
        ask(t)
        tt(T.d1[:], U2, got, A.mult, ["!K2", "got"], ["d1"], 256, 1.0, "d1")
        if t:
            decode(t - 1)
        if t == 1:
            gcopy(T.D16[:, 0:256], T.ydS[:, 0::4], ["yd0"], ["D16_0"], 256, "D16n")
        of2, z, s12, U4 = T.sel[:, 4:8], T.qi[:, 32:36], T.qi[:, 48:52], T.DD[:, 384:448]
        mv2 = T.mvx[:, 0::2]
        P(128, [(T.DF[0:64, 0:128], mv2, T.w128[:], True, True)], ["mv2", "w128"], ["!DF"], "of2")
        tt(T.LT3[0:64, :], T.DF[0:64, 0:128], T.km[0:64, 0:128], A.mult, ["!DF", "km"], ["LT3"], 128, 1.0, "of2")
        P(256, [(T.DF[:, 0:4], T.LT3[0:64, :], T.b8[0:64, 0:4], True, True)], ["LT3", "b8"], ["!DF"], "of2")
        ts(z, T.DF[:, 0:4], float(t), A.add, ["!DF"], ["z"], 4, label="of2")
        ts(z, z, 7, A.bitwise_and, ["z"], ["z"], 4, label="of2")
        both(s12, sl, ["sel"], ["s12"], 4, "of2", 1.0, 12.0)
        tt(z, z, s12, A.add, ["z", "s12"], ["z"], 4, label="of2")
        both(of2, z, ["z"], ["of2"], 4, "of2", 1.0)
        both(T.old2[:], T.morS[:].indirect(of2), ["mor", "morpad", "of2"], ["old2"], 64, "of2")
        P(128, [(U4, Ib, mv2, True, False), (U4, nIb, T.old2[:], False, True)], ["Ib", "nIb", "mv2", "old2"], ["!DD"], "of2")
        if not last:
            own(t + 1)
        win, wR = wide("nbT", tau)
        if OPT["p16"]:
            ts(T.nb2[:], win.indirect(sl), -1024.0, A.add, wR + ["sel"], ["nb2"], 64, GA, "nb2")
        else:
            both(T.nb2[:], win.indirect(sl), wR + ["sel"], ["nb2"], 64, "nb2")
        both(T.ad2[:], T.ad[:].indirect(sl), ["gapD.0", "adpad", "sel"], ["ad2"], 64, "ad2")
        P(64, [(D2, T.nbo[:], T.ad2[:], True, False)], ["nbo", "ad2"], ["!DD"], "delta")
        if OPT["p16"]:
            tt(T.EP2[:], T.PQ[:].indirect(T.mu[:, 32:36]), T.nb2[:], A.max, ["PQ", "mu2", "nb2"], ["EP2"], 64, GA, "E2")
            S(64, lambda e: e.activation(T.E2[:], T.EP2[:], F.Abs, bias=T.sc[:, 1:2]), ["EP2", "k1"], ["E2"], 1.0, "E2")
        else:
            tt(T.EP2[:], T.PQ[:, 1024 * t:1024 * t + 1024].indirect(T.mu[:, 32:36]), T.nb2[:], A.max, ["QP%d" % t, "mu2", "nb2"], ["EP2"], 64, GA, "E2")
            act(T.EU2[:], T.EP2[:], ["EP2"], ["EU2"], 64, F.Abs, label="E2")
            both(T.E2[:], T.EU2[:], ["EU2"], ["E2"], 64, "EG", 1.0)
        after("U%d" % (t + 1))
        far("2", T.EU2, "EU2", (32, 32), 2, mv2, "mv2", T.aE2, D2, "bo", True)
        tc(T.EE[:].indirect(sl), T.E2[:], ["E2", "sel", "EEpad"], EE, 64, SC, "EE")
        if not last:
            if OPT["neq"] == "P":
                P(1024, halves(U3, If, E, False, True), ["If"] + EE, ["!NN"], "P")
                act(T.ab[:], U3, ["!NN"], ["ab"], 256, F.Abs, label="P")
            else:
                tt(T.ab[:], E, T.basI[:, tau::4], A.not_equal, EE + ["basI"], ["ab"], 256, label="P")
            P(512, [(Lo, T.k15[0:1, :], row, True, False), (Lo, T.nH[0:1, :], row, False, False)], ["k15", "nH", "oneb"], ["!NN"], "P")
            P(256, [(Lo, T.tri[:], T.ab[:], False, False)], ["tri", "ab"], ["!NN"], "P")
        tt(mor.indirect(off), T.d1[:], T.old[:], A.add, ["d1", "old", "of%d" % t], ["mor"], 256, SC, "mor1")
        ts(T.got2[:], D2, nm, A.is_lt, ["!DD", nmR], ["got2"], 64, label="got")
        tt(T.d2[:], T.got2[:], U4, A.mult, ["!DD", "got2"], ["d2"], 64, 1.0, "got")
        tt(T.morS[:].indirect(of2), T.d2[:], T.old2[:], A.add, ["d2", "old2", "of2", "morpad"], ["mor"], 64, SC, "got")
        tc(T.got[:].indirect(sl), T.got2[:], ["got2", "sel", "gotpad"], ["got"], 64, SC, "got")
        P(256 * (1 + last), [(Lo, T.IH[:], got, False, i == last) for i in range(1 + last)], ["IH", "got"], ["!NN"], "P2")
        P(256, [(Hi, T.nIH[:], got, False, True)], ["nIH", "got"], ["!HI"], "P2")
        tt(T.xm[:], E, Lo, A.min, EE + ["!NN"], ["xm"], 256, 1.0, "P2")
        tt(keep, T.xm[:], Hi, A.max, ["xm", "!HI"], keepR, 256, 1.0, "P2")
        if last:
            store(T.yd[:], T.ydS[:], ["yd%d" % x for x in range(4)], 4.0)
            store(T.ym[:], mor, ["mor"], 5.0)
            return
        send_P(t + 1)
        S(84, lambda e: e.activation(T.aE2[:], T.got2[:], F.Copy, accum_out=T.cnt[:, 4:5]), ["got2"], ["n2", "gap2.1"], 1.0, "margin")
        P(320, [(T.DD[:, 320:321], T.no16[:], T.cum[:, 255:256], True, False), (T.DD[:, 320:321], T.o16[:], T.cnt[:, 4:5], False, True)],
          ["o16", "no16", "cum", "n2"], ["!DD"], "margin")
        ts(T.qi[:, 224:225], T.DD[:, 320:321], 2048.0, A.add, ["!DD"], ["ai"], 1, label="margin")
        ts(T.qi[:, 240:241], T.qi[:, 224:225], 127, A.bitwise_and, ["ai"], ["aj"], 1, label="margin")
        both(T.nm[:, t + 1:t + 2], T.qi[:, 240:241], ["aj"], ["nm%d" % (t + 1)], 1, "margin", 1.0, -1.0)

    for t in range(RO):
        rnd(t)
    chain = [k for x in FIRST.split() for k in early if ops[k]["q"] == "G" and ops[k]["out"] == x]
    for a, b in zip(chain, chain[1:]):
        ops[b]["deps"].setdefault(a, 0)
    for o in ops:
        if o["label"] == "nbT":
            o["deps"].setdefault(first_v[0], 0)
    for k, o in enumerate(ops):
        if o["q"] == "G" and k != issued["C0"]:
            if k in early:
                ops[issued["C0"]]["deps"].setdefault(k, 0)
            else:
                o["deps"].setdefault(issued["C0"], 0)
    emit(g, sm, ops, sent)


def one_pass(cost, more, nxt, qs, due, look, lag):
    m = len(cost)
    left = [0] * m
    for a in range(m):
        for b, _ in nxt[a]:
            left[b] += 1
    at, start, where, order = [0.0] * m, [0.0] * m, [""] * m, []
    ready = {q: [] for q in "VSPGYR"}
    free = {q: 0.0 for q in ready}
    for k in range(m):
        if not left[k]:
            for q in qs[k]:
                ready[q].append(k)
    span = 0.0
    while len(order) < m:
        bs, bk, bq = 1e9, -1, ""
        for q, rs in ready.items():
            if not rs:
                continue
            f = free[q]
            s0 = min([at[k] for k in rs])
            s0 = (f if f > s0 else s0) + look
            k, dk = -1, 1e9
            for j in rs:
                if at[j] <= s0 and due[j] < dk:
                    if q == "V" and len(qs[j]) == 2 and free["S"] < max(f, at[j]) + lag[j] * cost[j] - more[j]:
                        continue
                    k, dk = j, due[j]
            if k >= 0:
                s = f if f > at[k] else at[k]
                if s < bs:
                    bs, bk, bq = s, k, q
        if bk < 0:
            lag = [-1e9] * m
            continue
        start[bk], where[bk] = bs, bq
        order.append(bk)
        for q in qs[bk]:
            ready[q].remove(bk)
        e = bs + cost[bk] + (more[bk] if bq == "S" else 0.0)
        if bq != "R":
            free[bq] = e
        if e > span:
            span = e
        for b, d in nxt[bk]:
            if e + d > at[b]:
                at[b] = e + d
            left[b] -= 1
            if not left[b]:
                for q in qs[b]:
                    ready[q].append(b)
    return order, start, where, span


def replay(order, where, cost, more, nxt):
    at, free, span = [0.0] * len(cost), {q: 0.0 for q in "VSPGYR"}, 0.0
    for k in order:
        q = where[k]
        e = max(at[k], free[q]) + cost[k] + (more[k] if q == "S" else 0.0)
        if q != "R":
            free[q] = e
        span = max(span, e)
        for b, d in nxt[k]:
            if e + d > at[b]:
                at[b] = e + d
    return span


def timed(order, where, cost, more, prv, first, known, calm):
    end, by = (list(known[0]), list(known[1])) if known else ([0.0] * len(cost), [None] * len(cost))
    last, same = {where[k]: k for k in order[:first]}, -calm
    for k in order[first:]:
        s, b, q = 0.0, None, where[k]
        for a, d in prv[k]:
            x = end[a] + d
            if x > s:
                s, b = x, (a, False)
        if q != "R":
            a = last.get(q, -1)
            if a >= 0 and end[a] >= s:
                s, b = end[a], (a, True)
            last[q] = k
            if q == "S":
                s += more[k]
        s += cost[k]
        same = same + 1 if s == end[k] else 0
        end[k], by[k] = s, b
        if same > 80:
            break
    return end, by


def polish(order, where, costs, more, nxt, prv, prvs, qs, rng, steps, temp, floor):
    m = len(order)
    order = [k for k in order if k != m - 1] + [m - 1]

    def value(o, w, first, old, calm):
        runs = [timed(o, w, c, more, p, first, x, calm) for c, p, x in zip(costs, prvs, old)]
        return sum(r[0][m - 1] + OPT["mean"] * sum(r[0]) / m for r in runs), runs
    val, runs = value(order, where, 0, [None] * len(costs), m)
    best = (val, order, where)
    for i in range(steps):
        end, by = runs[int(rng.integers(0, len(runs)))]
        k, pairs = m - 1, []
        while by[k] is not None:
            if by[k][1]:
                pairs.append((by[k][0], k))
            k = by[k][0]
        if not pairs:
            break
        u, v = pairs[int(rng.integers(0, len(pairs)))]
        r, o2, w2 = rng.random(), order, where
        if r < 0.25:
            x = u if r < 0.15 else v
            if len(qs[x]) < 2:
                continue
            w2 = list(where)
            w2[x] = "S" if where[x] == "V" else "V"
            pu = pv = order.index(x)
        elif r > 0.85:
            pv = order.index(u)
            pu = max([order.index(a) + 1 for a, _ in prv[u]] + [0])
            if pu >= pv:
                continue
            pu += int(rng.integers(0, pv - pu)) * (r > 0.92)
            o2 = order[:pu] + [u] + order[pu:pv] + order[pv + 1:]
        else:
            pu, pv = order.index(u), order.index(v)
            if r < 0.6:
                pu = max(0, pu - int(rng.integers(0, 12)) * (r < 0.35))
                need, mid = {v}, order[pu:pv + 1]
                for x in reversed(mid):
                    if x in need:
                        need.update(a for a, _ in prv[x])
                if u in need:
                    continue
                o2 = order[:pu] + [x for x in mid if x in need] + [x for x in mid if x not in need] + order[pv + 1:]
            else:
                pv = min(m - 2, pv + int(rng.integers(0, 25)) * (r > 0.75))
                late, mid = {u}, order[pu:pv + 1]
                for x in mid:
                    if x in late:
                        late.update(b for b, _ in nxt[x])
                if v in late:
                    continue
                o2 = order[:pu] + [x for x in mid if x not in late] + [x for x in mid if x in late] + order[pv + 1:]
        v2, r2 = value(o2, w2, pu, runs, pv - pu if i % 50 else m)
        if v2 <= val + rng.exponential(temp) * (1.0 - (1.0 - floor) * i / steps):
            val, runs, order, where = v2, r2, o2, w2
            if val < best[0]:
                best = (val, order, where)
    return best


def find_order(ops):
    m = len(ops) + 1
    nxt, prv = [[] for _ in range(m)], [[] for _ in range(m)]
    for k, o in enumerate(ops):
        for a, w in o["deps"].items():
            d = ops[a]["wake"] + OPT["wake"] if w == 2 or (w == 1 and (o["q"] != "P" or ops[a]["q"] != "P")) else 0.0
            nxt[a].append((k, d))
            prv[k].append((a, d))
        if o["wake"]:
            nxt[k].append((m - 1, o["wake"]))
            prv[m - 1].append((k, o["wake"]))
    below = [0] * m
    left = [len(p) for p in prv]
    sort = [k for k in range(m) if not left[k]]
    for k in sort:
        for b, _ in nxt[k]:
            left[b] -= 1
            if not left[b]:
                sort.append(b)
    for k in reversed(sort):
        for b, _ in nxt[k]:
            below[k] |= below[b] | 1 << b
    nxt = [[(c, d) for c, d in x if not any(e >= d and below[b] >> c & 1 for b, e in x)] for x in nxt]
    prv = [[] for _ in range(m)]
    for k in range(m):
        for b, d in nxt[k]:
            prv[b].append((k, d))
    costs = [[(o["cost"] + o["gat"] * (ga - GA) + fix * (o["q"] in "VS")) * (fp if o["q"] == "P" else f if o["q"] in "VSG" else OPT["far_links"] if o["q"] == "R" else 1.0)
              for o in ops] + [0.0] for ga, f, fp, fix, _ in OPT["models"]]
    prvs = [[[(a, d + dw * (d > 0.0) if d < 1.0 or dw > 0.0 else 1.25 * d) for a, d in p] for p in prv] for _, _, _, _, dw in OPT["models"]]
    cost, more = costs[0], [o["more"] for o in ops] + [0.0]
    qs = [("V", "S") if o["q"] == "VS" else (o["q"],) for o in ops] + [("R",)]
    due = [0.0] * m
    for k in reversed(sort):
        due[k] = min([due[b] - d for b, d in nxt[k]] + [0.0]) - cost[k]
    FOUND["dbg"] = (due, cost, nxt, ops)
    rng = np.random.default_rng(OPT["seed"])
    look, one = OPT["look"], [0.0] * m

    def forward(due, lag):
        order, start, where, span = one_pass(cost, more, nxt, qs, due, look, lag)
        return span + sum(replay(order, where, c, more, nxt) for c in costs[1:]), order, start, where, span

    def backward(start, where):
        ends = [s + c + (x if q == "S" else 0.0) for s, c, x, q in zip(start, cost, more, where)]
        _, back, _, bspan = one_pass(cost, more, prv, [(q,) for q in where], [-x for x in ends], look, one)
        return [bspan - b - (e - s) for b, e, s in zip(back, ends, start)]
    lag, found = [OPT["lag"]] * m, []
    for i in range(OPT["starts"]):
        cur = forward([d + y for d, y in zip(due, rng.normal(0.0, OPT["noise"], m).tolist())], lag)
        for _ in range(2):
            cur = min(cur, forward(backward(cur[2], cur[3]), lag))
        found.append(polish(cur[1], cur[3], costs, more, nxt, prv, prvs, qs, rng, OPT["short"], OPT["temp"], 0.5))
    _, order, where = min(found)
    _, order, where = polish(order, where, costs, more, nxt, prv, prvs, qs, rng, OPT["steps"], 0.7 * OPT["temp"], 0.0)
    top = (order, replay(order, where, cost, more, nxt), where)
    return [k for k in top[0] if k < m - 1], top[1], top[2]


def emit(g, sem, ops, sent):
    if "order" not in FOUND:
        FOUND["order"], FOUND["span"], FOUND["where"] = find_order(ops)
    where = FOUND["where"]
    eng = {"V": g.vector, "S": g.scalar, "P": g.tensor, "G": g, "Y": g.sync}
    count = {}
    at = {}
    known = {q: {} for q in eng}
    snap = {}
    for k in FOUND["order"]:
        o = ops[k]
        q = where[k]
        if q == "R":
            at[k] = (o["sem"], o["inc"])
            continue
        need = {}
        for a in o["deps"]:
            w = o["deps"][a]
            if w == 2 or (w == 1 and (q != "P" or where[a] != "P")):
                s, v = at[a]
                need[s] = max(need.get(s, 0), v)
        e, kn = eng[q], known[q]
        for s in need:
            v = need[s]
            if kn.get(s, 0) >= v:
                continue
            if any(s2 != s and kn.get(s2, 0) < need[s2] and snap.get((s2, need[s2]), {}).get(s, 0) >= v for s2 in need):
                continue
            e.wait_ge(sem[s], v)
            kn[s] = v
            for s3, v3 in snap.get((s, v), {}).items():
                if kn.get(s3, 0) < v3:
                    kn[s3] = v3
        for s in need:
            if kn.get(s, 0) < need[s]:
                e.wait_ge(sem[s], need[s])
                kn[s] = need[s]
        for c in o["calls"]:
            ins = (c["VS".index(q)] if o["q"] == "VS" else c)(e)
            s = q if o["sem"] is None else o["sem"]
            if o["inc"]:
                count[s] = count.get(s, 0) + o["inc"]
                ins.then_inc(sem[s], o["inc"])
        if o["inc"]:
            at[k] = (s, count[s])
            snap[at[k]] = dict(kn)
        else:
            at[k] = (o["sem"], sent[o["sem"]])
    for s in list(count) + list(sent):
        v = sent[s] if s in sent else count[s]
        if known["Y"].get(s, 0) < v:
            eng["Y"].wait_ge(sem[s], v)
            known["Y"][s] = v
